import numpy as np
import ml_dtypes


def mxq(x, axis, fmt="e4m3"):
    dtype, down = {"e4m3": (ml_dtypes.float8_e4m3fn, 7), "e5m2": (ml_dtypes.float8_e5m2, 14)}[fmt]
    v = np.moveaxis(np.asarray(x, np.float32).astype(ml_dtypes.bfloat16).astype(np.float64), axis, -1)
    blocks = v.reshape(v.shape[:-1] + (-1, 32))
    amax = np.abs(blocks).max(-1, keepdims=True)
    byte = np.maximum(np.where(amax > 0, np.frexp(amax)[1] - 1 + 127, 0) - down, 1)
    scale = np.exp2(byte - 127.0)
    codes = (blocks / scale).astype(np.float32).astype(dtype).astype(np.float64)
    return np.moveaxis((codes * scale).reshape(v.shape), -1, axis)


WIDE = False


def mx_kscale(k):
    if not WIDE:
        return np.ones(k)
    levels = np.array([30, -30])
    if k % 512:
        return np.exp2(np.random.permutation(np.resize(levels, k // 32))).repeat(32)
    a = np.empty((k // 512, 16))
    for p in range(k // 512):
        a[p, :8] = np.random.permutation(np.resize(levels, 8))
        for g in range(8):
            far = levels[np.abs(levels - a[p, g]) >= 10]
            a[p, g + 8] = far[np.random.randint(len(far))]
    return np.exp2(a.ravel()).repeat(32)


def f64(x):
    return np.asarray(x).astype(np.float64)


def striped(idx):
    return np.tile(idx.reshape(-1, 16).T, (8, 1)).astype(np.uint16)


def unstriped(offs):
    return offs[:16].T.reshape(-1).astype(np.int64)


E2M1 = np.array([0.0, 0.5, 1.0, 1.5, 2.0, 3.0, 4.0, 6.0, -0.0, -0.5, -1.0, -1.5, -2.0, -3.0, -4.0, -6.0])


def pack_weight(w, fmt):
    k, n = w.shape
    w = f64(np.asarray(w, np.float32).astype(ml_dtypes.bfloat16)).reshape(k // 32, 32, n)
    amax = np.abs(w).max(1)
    if fmt == "e4m3":
        byte = np.frexp(amax)[1] - 1 + 127 - 7
    elif fmt == "e5m2":
        byte = np.frexp(amax)[1] - 1 + 127 - 14
    else:
        mant, ex = np.frexp(amax / 6.0)
        byte = np.where(mant > 0.5, ex, ex - 1) + 127
    byte = np.clip(np.where(amax > 0, byte, 1), 1, 254)
    scaled = (w * np.exp2(127.0 - byte)[:, None, :]).reshape(k, n).astype(np.float32)
    by_word = np.ascontiguousarray(scaled.reshape(k // 512, 128, 4, n).transpose(0, 1, 3, 2))
    if fmt == "e4m3":
        words = by_word.astype(ml_dtypes.float8_e4m3fn).view(np.uint8)
    elif fmt == "e5m2":
        words = by_word.astype(ml_dtypes.float8_e5m2).view(np.uint8)
    else:
        c = by_word.astype(ml_dtypes.float4_e2m1fn).view(np.uint8) & 0xF
        words = (c[..., 0::2] | (c[..., 1::2] << 4)).reshape(k // 512, 128, 2 * n)
    return np.ascontiguousarray(words), np.ascontiguousarray(byte.astype(np.uint8).reshape(k // 512, 16, n))


def unpack_weight(words, scales, fmt):
    g, _, n = scales.shape
    words = np.ascontiguousarray(words).reshape(g, 128, n, -1)
    if fmt == "e4m3":
        vals = words.view(ml_dtypes.float8_e4m3fn).astype(np.float64)
    elif fmt == "e5m2":
        vals = words.view(ml_dtypes.float8_e5m2).astype(np.float64)
    else:
        nib = np.empty((g, 128, n, 4), np.uint8)
        nib[..., 0::2] = words & 0xF
        nib[..., 1::2] = words >> 4
        vals = E2M1[nib]
    vals = vals * np.repeat(np.exp2(scales.astype(np.float64) - 127.0), 8, axis=1)[..., None]
    return vals.transpose(0, 1, 3, 2).reshape(g * 512, n)


def d_silu(v):
    s = 1.0 / (1.0 + np.exp(-np.maximum(v, -700.0)))
    return s * (1.0 + v * (1.0 - s))


K, T, E, C, H, N = 256, 1024, 4, 512, 512, 1024


def by_expert(wq, xq):
    return np.concatenate([wq[e].T @ xq[:, e * C:(e + 1) * C] for e in range(E)], axis=1)


def setup_inputs():
    n = np.random.standard_normal
    v = mx_kscale(N)
    u = mx_kscale(H)
    first = np.random.permutation(np.repeat(np.arange(E), T // E))
    second = (first + 1 + np.random.permutation(np.repeat(np.arange(E - 1), -(-T // (E - 1)))[:T])) % E
    while np.bincount(second, minlength=E).max() != T // E:
        load = np.bincount(second, minlength=E); hi, lo = int(load.argmax()), int(load.argmin())
        t = np.flatnonzero((second == hi) & (first != lo))[0]; second[t] = lo
    slot_token = np.empty(E * C, np.int64); pos = np.empty((2, T), np.int64); fill = np.zeros(E, np.int64)
    place = np.stack([np.random.permutation(C) for _ in range(E)])
    for r, deal in enumerate((first, second)):
        for t in np.random.permutation(T):
            e = deal[t]; j = e * C + place[e, fill[e]]; fill[e] += 1; slot_token[j] = t; pos[r, t] = j
    g = np.random.uniform(0.2, 0.8, T)
    dy = pack_weight(n((N, T)) * v[:, None], "e5m2")
    w2t = [pack_weight(m, "e4m3") for m in n((E, N, H)) / np.sqrt(N) / v[None, :, None] * u]
    return {
        "dy_words": dy[0],
        "dy_scales": dy[1],
        "w2t_words": np.stack([m[0] for m in w2t]),
        "w2t_scales": np.stack([m[1] for m in w2t]),
        "w1t": (n((H, K)) / np.sqrt(H) / u[:, None]).astype(np.float32),
        "a": (n((H, T))).astype(np.float32),
        "gate": np.stack([np.tile(g, (128, 1)), np.tile(1.0 - g, (128, 1))]).astype(np.float32),
        "offs": striped(slot_token),
        "pos1": striped(pos[0]),
        "pos2": striped(pos[1]),
    }


def reference(dy_words, dy_scales, w2t_words, w2t_scales, w1t, a, gate, offs, pos1, pos2):
    w2t = np.stack([unpack_weight(w2t_words[e], w2t_scales[e], "e4m3") for e in range(E)])
    w1tq = mxq(f64(w1t), 0, "e4m3")
    idx = unstriped(offs)
    gq = unpack_weight(dy_words, dy_scales, "e5m2")[:, idx]
    y = by_expert(w2t, gq)
    dh = sum(f64(gate[r, :1]) * y[:, unstriped(p)] for r, p in enumerate((pos1, pos2)))
    return w1tq.T @ mxq(dh * d_silu(f64(a)), 0, "e5m2")

@@ -1,0 +1,259 @@
+from contextlib import ExitStack
+
+import concourse.mybir as mybir
+from concourse.masks import make_identity
+
+K, T, E, C, H, N = 256, 1024, 4, 512, 512, 1024
+FLOPS = 2 * E * C * N * H + 2 * T * H * K
+
+F32 = mybir.dt.float32
+BF16 = mybir.dt.bfloat16
+I32 = mybir.dt.int32
+U32 = mybir.dt.uint32
+U16 = mybir.dt.uint16
+U8 = mybir.dt.uint8
+E4M3 = mybir.dt.float8_e4m3fn_x4
+E5M2 = mybir.dt.float8_e5m2_x4
+ACT = mybir.ActivationFunctionType
+ALU = mybir.AluOpType
+
+P = 128
+PACK = 4
+PASSES = N // (P * PACK)
+TILES = H // P
+SLOTS = E * C
+BLOCKS = [256, 256, 256, 128, 128]
+SHIFTED = 112
+
+
+def tile_moe_sub_silu_kernel(
+    tc, dy_words, dy_scales, w2t_words, w2t_scales, w1t, a, gate, offs, pos1, pos2, out
+):
+    nc = tc.nc
+    with ExitStack() as ctx:
+        keep = ctx.enter_context(tc.tile_pool(name="keep", bufs=1))
+        ring = ctx.enter_context(tc.tile_pool(name="ring", bufs=10))
+        ring4 = ctx.enter_context(tc.tile_pool(name="ring4", bufs=4))
+        psum = ctx.enter_context(tc.psum_pool(name="psum", bufs=1))
+
+        def bank(b):
+            return psum.tile([P, 512], F32, name="bank%d" % b)
+
+        offs_sb = keep.tile([P, SLOTS // 16], U16, name="offs_sb")
+        pos_sb = [keep.tile([P, T // 16], U16, name="pos_sb%d" % r) for r in range(2)]
+        dy_sc = keep.tile([P, T], U8, name="dy_sc", align_bytes=64)
+        dy_w = [keep.tile([P, T], I32, name="dy_w%d" % s, align_bytes=64) for s in range(PASSES)]
+        w2_sc = keep.tile([P, E * PASSES, H], U8, name="w2_sc", align_bytes=64)
+        w2_w = [keep.tile([P, PASSES, H], I32, name="w2_w%d" % e, align_bytes=64) for e in range(E)]
+        slot_sc = keep.tile([P, SLOTS], U8, name="slot_sc", align_bytes=64)
+        slot_sc1 = keep.tile([P, SLOTS], U8, name="slot_sc1", align_bytes=64)
+        slot_w = [[keep.tile([P, C], U32, name="slot_w%d_%d" % (e, s), align_bytes=64) for s in range(PASSES)] for e in range(E)]
+        y = [keep.tile([P, SLOTS], F32, name="y%d" % j) for j in range(TILES)]
+        a_nat = [keep.tile([P, TILES, 512], F32, name="a_nat%d" % h) for h in range(2)]
+        a_quad = [keep.tile([P, PACK, 512], F32, name="a_quad%d" % h) for h in range(2)]
+        sg = [keep.tile([P, TILES, 512], F32, name="sg%d" % h) for h in range(2)]
+        gate_rows = keep.tile([P, P], F32, name="gate_rows")
+        gate_neg = keep.tile([P, 16], F32, name="gate_neg")
+        ident = keep.tile([P, P], F32, name="ident")
+        warm = keep.tile([P, 1], F32, name="warm")
+        w1_raw = keep.tile([P, PACK, K], F32, name="w1_raw")
+        w1_bf = keep.tile([P, K, PACK], BF16, name="w1_bf", align_bytes=64)
+        w1_w = keep.tile([P, K], U32, name="w1_w", align_bytes=64)
+        w1_sc = keep.tile([P, K], U8, name="w1_sc", align_bytes=64)
+        da_w = keep.tile([P, T], U32, name="da_w", align_bytes=64)
+        da_sc = keep.tile([P, T], U8, name="da_sc", align_bytes=64)
+
+        nc.vector.memset(dy_sc[:].bitcast(I32), 0)
+        nc.vector.memset(w2_sc[:].rearrange("p g i -> p (g i)").bitcast(I32), 0)
+        nc.vector.memset(slot_sc1[:].bitcast(I32), 0)
+        nc.vector.memset(gate_rows[:], 0.0)
+        make_identity(nc, ident[:])
+        nc.scalar.activation(out=warm[:], in_=gate_rows[:, 0:1], func=ACT.Sigmoid)
+
+        nc.sync.dma_start(offs_sb[:], offs)
+        for q in range(4):
+            nc.sync.dma_start(
+                out=dy_sc[32 * q : 32 * q + 8, :].bitcast(I32),
+                in_=dy_scales[:, 4 * q : 4 * q + 4, :].bitcast(I32),
+            )
+        w2_rows = w2t_scales.rearrange("e s b i -> b (e s) i")
+        for q in range(4):
+            nc.sync.dma_start(
+                out=w2_sc[32 * q : 32 * q + 4, :, :].bitcast(I32),
+                in_=w2_rows[4 * q : 4 * q + 4, :, :].bitcast(I32),
+            )
+        for s in range(PASSES):
+            nc.sync.dma_start(out=dy_w[s][:], in_=dy_words[s].rearrange("p t d -> p (t d)").bitcast(I32))
+
+        def load_w2(e):
+            nc.sync.dma_start(out=w2_w[e][:], in_=w2t_words[e].rearrange("s p i d -> p s (i d)").bitcast(I32))
+
+        a_by_tile = a.rearrange("(j p) t -> p j t", p=P)
+        a_by_quad = a.rearrange("(p j) t -> p j t", j=PACK)
+        nc.sync.dma_start(out=a_nat[0][:], in_=a_by_tile[:, :, 0:512])
+        load_w2(0)
+        load_w2(1)
+        nc.sync.dma_start(out=a_nat[1][:], in_=a_by_tile[:, :, 512:1024])
+        load_w2(2)
+        load_w2(3)
+        nc.sync.dma_start(out=w1_raw[:], in_=w1t.rearrange("(p j) k -> p j k", j=PACK))
+        nc.sync.dma_start(pos_sb[0][:], pos1)
+        nc.sync.dma_start(pos_sb[1][:], pos2)
+        for r in range(2):
+            nc.sync.dma_start(out=gate_rows[8 * r : 8 * r + 8, :], in_=gate[r, 0, :].rearrange("(c t) -> c t", t=P))
+        for h in range(2):
+            nc.sync.dma_start(out=a_quad[h][:], in_=a_by_quad[:, :, 512 * h : 512 * h + 512])
+
+        def expert_offs(e):
+            return offs_sb[:, e * C // 16 : (e + 1) * C // 16]
+
+        for e in range(E):
+            nc.vector.tensor_copy(slot_sc[:, e * C : (e + 1) * C], dy_sc[:].indirect(expert_offs(e)))
+            if e % 2 == 1:
+                cols = slice((e - 1) * C, (e + 1) * C)
+                nc.scalar.dma_start(
+                    out=slot_sc1[0:SHIFTED, cols].bitcast(I32), in_=slot_sc[4 : 4 + SHIFTED, cols].bitcast(I32)
+                )
+
+        planes = [slot_sc, slot_sc1]
+        for e in range(E):
+            for s in range(PASSES):
+                nc.vector.tensor_copy(slot_w[e][s][:], dy_w[s][:].bitcast(U32).indirect(expert_offs(e)))
+            accs = [bank((e * TILES + j) % 8) for j in range(TILES)]
+            for s in range(PASSES):
+                for j in range(TILES):
+                    nc.tensor.matmul_mx(
+                        out=accs[j][:],
+                        lhsT=w2_w[e][:, s, j * P : (j + 1) * P].bitcast(E4M3),
+                        lhsT_scale=w2_sc[:, e * PASSES + s, j * P : (j + 1) * P],
+                        rhs=slot_w[e][s][:].bitcast(E5M2),
+                        rhs_scale=planes[s][:, e * C : (e + 1) * C],
+                        start=(s == 0),
+                        stop=(s == PASSES - 1),
+                    )
+            for j in range(TILES):
+                nc.scalar.copy(out=y[j][:, e * C : (e + 1) * C], in_=accs[j][:])
+
+        for h in range(2):
+            for jj in range(2):
+                nc.scalar.activation(out=sg[h][:, 2 * jj : 2 * jj + 2, :], in_=a_nat[h][:, 2 * jj : 2 * jj + 2, :], func=ACT.Sigmoid)
+
+        nc.vector.tensor_copy(out=w1_bf[:], in_=w1_raw[:].rearrange("p j k -> p k j"))
+        gate_t = bank(6)
+        nc.tensor.transpose(gate_t[:, 0:P], gate_rows[:], ident[:])
+        nc.scalar.activation(out=gate_neg[:], in_=gate_t[:, 0:16], func=ACT.Copy, scale=-1.0)
+        nc.vector.quantize_mx(out=w1_w[:].bitcast(E4M3), scales=w1_sc[:], in_=w1_bf[:].rearrange("p k j -> p (k j)"))
+
+        starts = [sum(BLOCKS[:b]) for b in range(len(BLOCKS))]
+        last = len(BLOCKS) - 1
+        turn_banks = [[[0, 1], [2, 3]]] * 3 + [[[0], [1]], [[2], [3]]]
+        sum_banks = [[4, 5], [6, 7], [4, 5], [6], [7]]
+        sums = {}
+        grouped = {}
+
+        def fetch(b, after):
+            t0, width = starts[b], BLOCKS[b]
+            subs = width // P
+            for c in range(subs):
+                sums[b, c] = bank(sum_banks[b][c])
+            for r in range(2):
+                split = b == last and r == 1
+                turned = [bank(turn_banks[b][r][c]) for c in range(subs)]
+                gated = [ring.tile([P, PACK, P], F32, name="gated") for c in range(subs)]
+
+                def weigh(c, source, j0, j1):
+                    col = 8 * r + t0 // P + c
+                    nc.scalar.activation(
+                        out=gated[c][:, :, 32 * j0 : 32 * j1],
+                        in_=source[:, j0 * P : j1 * P].rearrange("t (p j) -> t j p", j=PACK),
+                        func=ACT.Copy,
+                        scale=gate_neg[:, col : col + 1],
+                    )
+
+                for j in range(TILES):
+                    picked = ring.tile([P, width], F32, name="picked")
+                    nc.vector.tensor_tensor(
+                        picked[:],
+                        y[j][:].indirect(pos_sb[r][:, t0 // 16 : (t0 + width) // 16]),
+                        sg[t0 // 512][:, j, t0 % 512 : t0 % 512 + width],
+                        ALU.mult,
+                    )
+                    if split and j == TILES - 1:
+                        weigh(0, turned[0], 0, j)
+                        turned = [bank(0)]
+                    for c in range(subs):
+                        nc.tensor.transpose(turned[c][:, j * P : (j + 1) * P], picked[:, c * P : (c + 1) * P], ident[:])
+                    if j == TILES - 1:
+                        for c in range(subs):
+                            weigh(c, turned[c], j if split else 0, TILES)
+                            for d in range(PACK):
+                                nc.tensor.matmul(
+                                    sums[b, c][:, d * P : (d + 1) * P], gated[c][:, d, :], ident[:],
+                                    start=(r == 0 and d == 0), stop=(r == 1 and d == PACK - 1), is_transpose=True,
+                                )
+                    for step in after.get(8 * b + 4 * r + j, []):
+                        step()
+
+        def finish(b, c):
+            t0 = starts[b] + c * P
+            silu_neg = ring.tile([P, P, PACK], F32, name="silu_neg")
+            nc.scalar.activation(
+                out=silu_neg[:],
+                in_=a_quad[t0 // 512][:, :, t0 % 512 : t0 % 512 + P].rearrange("p j t -> p t j"),
+                func=ACT.Silu,
+                scale=-1.0,
+            )
+            if c == 0:
+                grouped[b] = ring4.tile([P, BLOCKS[b], PACK], BF16, name="da_bf", align_bytes=64)
+            nc.vector.scalar_tensor_tensor(
+                out=grouped[b][:, c * P : (c + 1) * P, :],
+                in0=silu_neg[:],
+                scalar=1.0,
+                in1=sums[b, c][:].rearrange("p (j t) -> p t j", j=PACK),
+                op0=ALU.subtract,
+                op1=ALU.mult,
+            )
+
+        def quantise(b):
+            t0, width = starts[b], BLOCKS[b]
+            nc.vector.quantize_mx(
+                out=da_w[:, t0 : t0 + width].bitcast(E5M2),
+                scales=da_sc[:, t0 : t0 + width],
+                in_=grouped[b][:].rearrange("p t j -> p (t j)"),
+            )
+
+        def project(t0, new, banks, both_engines):
+            for m in range(K // P):
+                acc = bank(banks[m])
+                nc.tensor.matmul_mx(
+                    out=acc[:],
+                    lhsT=w1_w[:, m * P : (m + 1) * P].bitcast(E4M3),
+                    lhsT_scale=w1_sc[:, m * P : (m + 1) * P],
+                    rhs=da_w[:, t0 : t0 + 512].bitcast(E5M2),
+                    rhs_scale=da_sc[:, t0 : t0 + 512],
+                    start=True,
+                    stop=True,
+                )
+                res = ring4.tile([P, new], F32, name="res")
+                if m == 1 and both_engines:
+                    nc.vector.tensor_copy(out=res[:], in_=acc[:, 512 - new : 512])
+                else:
+                    nc.scalar.copy(out=res[:], in_=acc[:, 512 - new : 512])
+                nc.sync.dma_start(out=out[m * P : (m + 1) * P, t0 + 512 - new : t0 + 512], in_=res[:])
+
+        after = {
+            13: [lambda: finish(0, 0), lambda: finish(0, 1)],
+            15: [lambda: quantise(0)],
+            21: [lambda: finish(1, 0), lambda: finish(1, 1)],
+            23: [lambda: quantise(1), lambda: project(0, 512, [6, 7], False)],
+            31: [lambda: finish(2, 0)],
+            33: [lambda: finish(2, 1)],
+            35: [lambda: quantise(2)],
+            38: [lambda: finish(3, 0)],
+            39: [lambda: quantise(3), lambda: project(384, 384, [4, 5], False)],
+        }
+        for b in range(len(BLOCKS)):
+            fetch(b, after)
+        finish(last, 0)
+        quantise(last)
+        project(512, 128, [1, 6], True)

@@ -23,7 +23,7 @@ PASSES = N // (P * PACK)
 TILES = H // P
 SLOTS = E * C
 BLOCKS = [256, 256, 256, 128, 128]
-SHIFTED = 112
+AHEAD = 3
 
 
 def tile_moe_sub_silu_kernel(
@@ -33,6 +33,7 @@ def tile_moe_sub_silu_kernel(
     with ExitStack() as ctx:
         keep = ctx.enter_context(tc.tile_pool(name="keep", bufs=1))
         ring = ctx.enter_context(tc.tile_pool(name="ring", bufs=10))
+        slots = ctx.enter_context(tc.tile_pool(name="slots", bufs=AHEAD))
         ring4 = ctx.enter_context(tc.tile_pool(name="ring4", bufs=4))
         psum = ctx.enter_context(tc.psum_pool(name="psum", bufs=1))
 
@@ -41,13 +42,10 @@ def tile_moe_sub_silu_kernel(
 
         offs_sb = keep.tile([P, SLOTS // 16], U16, name="offs_sb")
         pos_sb = [keep.tile([P, T // 16], U16, name="pos_sb%d" % r) for r in range(2)]
-        dy_sc = keep.tile([P, T], U8, name="dy_sc", align_bytes=64)
+        dy_sc = keep.tile([P, PASSES, T], U8, name="dy_sc", align_bytes=64)
         dy_w = [keep.tile([P, T], I32, name="dy_w%d" % s, align_bytes=64) for s in range(PASSES)]
         w2_sc = keep.tile([P, E * PASSES, H], U8, name="w2_sc", align_bytes=64)
         w2_w = [keep.tile([P, PASSES, H], I32, name="w2_w%d" % e, align_bytes=64) for e in range(E)]
-        slot_sc = keep.tile([P, SLOTS], U8, name="slot_sc", align_bytes=64)
-        slot_sc1 = keep.tile([P, SLOTS], U8, name="slot_sc1", align_bytes=64)
-        slot_w = [[keep.tile([P, C], U32, name="slot_w%d_%d" % (e, s), align_bytes=64) for s in range(PASSES)] for e in range(E)]
         y = [keep.tile([P, SLOTS], F32, name="y%d" % j) for j in range(TILES)]
         a_nat = [keep.tile([P, TILES, 512], F32, name="a_nat%d" % h) for h in range(2)]
         a_quad = [keep.tile([P, PACK, 512], F32, name="a_quad%d" % h) for h in range(2)]
@@ -63,26 +61,12 @@ def tile_moe_sub_silu_kernel(
         da_w = keep.tile([P, T], U32, name="da_w", align_bytes=64)
         da_sc = keep.tile([P, T], U8, name="da_sc", align_bytes=64)
 
-        nc.vector.memset(dy_sc[:].bitcast(I32), 0)
-        nc.vector.memset(w2_sc[:].rearrange("p g i -> p (g i)").bitcast(I32), 0)
-        nc.vector.memset(slot_sc1[:].bitcast(I32), 0)
-        nc.vector.memset(gate_rows[:], 0.0)
+        nc.gpsimd.memset(dy_sc[:].rearrange("p s t -> p (s t)").bitcast(I32), 0)
+        nc.gpsimd.memset(gate_rows[:], 0.0)
         make_identity(nc, ident[:])
         nc.scalar.activation(out=warm[:], in_=gate_rows[:, 0:1], func=ACT.Sigmoid)
 
-        nc.sync.dma_start(offs_sb[:], offs)
-        for q in range(4):
-            nc.sync.dma_start(
-                out=dy_sc[32 * q : 32 * q + 8, :].bitcast(I32),
-                in_=dy_scales[:, 4 * q : 4 * q + 4, :].bitcast(I32),
-            )
-        w2_rows = w2t_scales.rearrange("e s b i -> b (e s) i")
-        for q in range(4):
-            nc.sync.dma_start(
-                out=w2_sc[32 * q : 32 * q + 4, :, :].bitcast(I32),
-                in_=w2_rows[4 * q : 4 * q + 4, :, :].bitcast(I32),
-            )
-        for s in range(PASSES):
+        def load_dy(s):
             nc.sync.dma_start(out=dy_w[s][:], in_=dy_words[s].rearrange("p t d -> p (t d)").bitcast(I32))
 
         def load_w2(e):
@@ -90,17 +74,30 @@ def tile_moe_sub_silu_kernel(
 
         a_by_tile = a.rearrange("(j p) t -> p j t", p=P)
         a_by_quad = a.rearrange("(p j) t -> p j t", j=PACK)
-        nc.sync.dma_start(out=a_nat[0][:], in_=a_by_tile[:, :, 0:512])
+        dy_rows = dy_scales.rearrange("s b t -> b s t")
+        w2_rows = w2t_scales.rearrange("e s b i -> b (e s) i")
+
+        nc.sync.dma_start(offs_sb[:], offs)
+        for q in range(4):
+            nc.sync.dma_start(
+                out=dy_sc[32 * q : 32 * q + 4, :, :].bitcast(I32), in_=dy_rows[4 * q : 4 * q + 4, :, :].bitcast(I32)
+            )
+        load_dy(0)
         load_w2(0)
+        load_dy(1)
+        for q in range(4):
+            nc.sync.dma_start(
+                out=w2_sc[32 * q : 32 * q + 4, :, :].bitcast(I32), in_=w2_rows[4 * q : 4 * q + 4, :, :].bitcast(I32)
+            )
+        nc.sync.dma_start(out=a_nat[0][:], in_=a_by_tile[:, :, 0:512])
         load_w2(1)
         nc.sync.dma_start(out=a_nat[1][:], in_=a_by_tile[:, :, 512:1024])
         load_w2(2)
-        load_w2(3)
         nc.sync.dma_start(out=w1_raw[:], in_=w1t.rearrange("(p j) k -> p j k", j=PACK))
+        load_w2(3)
         nc.sync.dma_start(pos_sb[0][:], pos1)
         nc.sync.dma_start(pos_sb[1][:], pos2)
-        for r in range(2):
-            nc.sync.dma_start(out=gate_rows[8 * r : 8 * r + 8, :], in_=gate[r, 0, :].rearrange("(c t) -> c t", t=P))
+        nc.sync.dma_start(out=gate_rows[0:16, :], in_=gate[:, 0, :].rearrange("r (c t) -> r c t", t=P))
         for h in range(2):
             nc.sync.dma_start(out=a_quad[h][:], in_=a_by_quad[:, :, 512 * h : 512 * h + 512])
 
@@ -108,26 +105,19 @@ def tile_moe_sub_silu_kernel(
             return offs_sb[:, e * C // 16 : (e + 1) * C // 16]
 
         for e in range(E):
-            nc.vector.tensor_copy(slot_sc[:, e * C : (e + 1) * C], dy_sc[:].indirect(expert_offs(e)))
-            if e % 2 == 1:
-                cols = slice((e - 1) * C, (e + 1) * C)
-                nc.scalar.dma_start(
-                    out=slot_sc1[0:SHIFTED, cols].bitcast(I32), in_=slot_sc[4 : 4 + SHIFTED, cols].bitcast(I32)
-                )
-
-        planes = [slot_sc, slot_sc1]
-        for e in range(E):
-            for s in range(PASSES):
-                nc.vector.tensor_copy(slot_w[e][s][:], dy_w[s][:].bitcast(U32).indirect(expert_offs(e)))
             accs = [bank((e * TILES + j) % 8) for j in range(TILES)]
             for s in range(PASSES):
+                slot_sc = slots.tile([P, C], U8, name="slot_sc", align_bytes=64)
+                slot_w = slots.tile([P, C], U32, name="slot_w", align_bytes=64)
+                nc.vector.tensor_copy(slot_sc[:], dy_sc[:, s, :].indirect(expert_offs(e)))
+                nc.vector.tensor_copy(slot_w[:], dy_w[s][:].bitcast(U32).indirect(expert_offs(e)))
                 for j in range(TILES):
                     nc.tensor.matmul_mx(
                         out=accs[j][:],
                         lhsT=w2_w[e][:, s, j * P : (j + 1) * P].bitcast(E4M3),
                         lhsT_scale=w2_sc[:, e * PASSES + s, j * P : (j + 1) * P],
-                        rhs=slot_w[e][s][:].bitcast(E5M2),
-                        rhs_scale=planes[s][:, e * C : (e + 1) * C],
+                        rhs=slot_w[:].bitcast(E5M2),
+                        rhs_scale=slot_sc[:],
                         start=(s == 0),
                         stop=(s == PASSES - 1),
                     )
@@ -222,7 +212,10 @@ def tile_moe_sub_silu_kernel(
                 in_=grouped[b][:].rearrange("p t j -> p (t j)"),
             )
 
+        out_by_tile = out.rearrange("(m p) t -> p m t", p=P)
+
         def project(t0, new, banks, both_engines):
+            res = ring4.tile([P, K // P, new], F32, name="res")
             for m in range(K // P):
                 acc = bank(banks[m])
                 nc.tensor.matmul_mx(
@@ -234,12 +227,11 @@ def tile_moe_sub_silu_kernel(
                     start=True,
                     stop=True,
                 )
-                res = ring4.tile([P, new], F32, name="res")
                 if m == 1 and both_engines:
-                    nc.vector.tensor_copy(out=res[:], in_=acc[:, 512 - new : 512])
+                    nc.vector.tensor_copy(out=res[:, m, :], in_=acc[:, 512 - new : 512])
                 else:
-                    nc.scalar.copy(out=res[:], in_=acc[:, 512 - new : 512])
-                nc.sync.dma_start(out=out[m * P : (m + 1) * P, t0 + 512 - new : t0 + 512], in_=res[:])
+                    nc.scalar.copy(out=res[:, m, :], in_=acc[:, 512 - new : 512])
+            nc.sync.dma_start(out=out_by_tile[:, :, t0 + 512 - new : t0 + 512], in_=res[:])
 
         after = {
             13: [lambda: finish(0, 0), lambda: finish(0, 1)],

@@ -23,7 +23,8 @@ PASSES = N // (P * PACK)
 TILES = H // P
 SLOTS = E * C
 BLOCKS = [256, 256, 256, 128, 128]
-AHEAD = 3
+AHEAD = 2
+SHIFTED = 112
 
 
 def tile_moe_sub_silu_kernel(
@@ -34,6 +35,7 @@ def tile_moe_sub_silu_kernel(
         keep = ctx.enter_context(tc.tile_pool(name="keep", bufs=1))
         ring = ctx.enter_context(tc.tile_pool(name="ring", bufs=10))
         slots = ctx.enter_context(tc.tile_pool(name="slots", bufs=AHEAD))
+        ring3 = ctx.enter_context(tc.tile_pool(name="ring3", bufs=3))
         ring4 = ctx.enter_context(tc.tile_pool(name="ring4", bufs=4))
         psum = ctx.enter_context(tc.psum_pool(name="psum", bufs=1))
 
@@ -42,14 +44,16 @@ def tile_moe_sub_silu_kernel(
 
         offs_sb = keep.tile([P, SLOTS // 16], U16, name="offs_sb")
         pos_sb = [keep.tile([P, T // 16], U16, name="pos_sb%d" % r) for r in range(2)]
-        dy_sc = keep.tile([P, PASSES, T], U8, name="dy_sc", align_bytes=64)
+        dy_sc = [keep.tile([P, T], U8, name="dy_sc%d" % s, align_bytes=64) for s in range(PASSES)]
+        late_sc = [keep.tile([P, 2 * C], U8, name="late_sc%d" % s, align_bytes=64) for s in range(PASSES)]
         dy_w = [keep.tile([P, T], I32, name="dy_w%d" % s, align_bytes=64) for s in range(PASSES)]
         w2_sc = keep.tile([P, E * PASSES, H], U8, name="w2_sc", align_bytes=64)
         w2_w = [keep.tile([P, PASSES, H], I32, name="w2_w%d" % e, align_bytes=64) for e in range(E)]
         y = [keep.tile([P, SLOTS], F32, name="y%d" % j) for j in range(TILES)]
-        a_nat = [keep.tile([P, TILES, 512], F32, name="a_nat%d" % h) for h in range(2)]
+        a_early = [keep.tile([P, TILES, 256], F32, name="a_early%d" % u) for u in range(2)]
+        a_late = keep.tile([P, TILES, 512], F32, name="a_late")
         a_quad = [keep.tile([P, PACK, 512], F32, name="a_quad%d" % h) for h in range(2)]
-        sg = [keep.tile([P, TILES, 512], F32, name="sg%d" % h) for h in range(2)]
+        sg = [keep.tile([P, TILES, 512], F32, name="sg0")]
         gate_rows = keep.tile([P, P], F32, name="gate_rows")
         gate_neg = keep.tile([P, 16], F32, name="gate_neg")
         ident = keep.tile([P, P], F32, name="ident")
@@ -61,7 +65,8 @@ def tile_moe_sub_silu_kernel(
         da_w = keep.tile([P, T], U32, name="da_w", align_bytes=64)
         da_sc = keep.tile([P, T], U8, name="da_sc", align_bytes=64)
 
-        nc.gpsimd.memset(dy_sc[:].rearrange("p s t -> p (s t)").bitcast(I32), 0)
+        for s in range(PASSES):
+            nc.gpsimd.memset(dy_sc[s][:].bitcast(I32), 0)
         nc.gpsimd.memset(gate_rows[:], 0.0)
         make_identity(nc, ident[:])
         nc.scalar.activation(out=warm[:], in_=gate_rows[:, 0:1], func=ACT.Sigmoid)
@@ -74,42 +79,56 @@ def tile_moe_sub_silu_kernel(
 
         a_by_tile = a.rearrange("(j p) t -> p j t", p=P)
         a_by_quad = a.rearrange("(p j) t -> p j t", j=PACK)
-        dy_rows = dy_scales.rearrange("s b t -> b s t")
         w2_rows = w2t_scales.rearrange("e s b i -> b (e s) i")
 
         nc.sync.dma_start(offs_sb[:], offs)
         for q in range(4):
             nc.sync.dma_start(
-                out=dy_sc[32 * q : 32 * q + 4, :, :].bitcast(I32), in_=dy_rows[4 * q : 4 * q + 4, :, :].bitcast(I32)
+                out=dy_sc[0][32 * q : 32 * q + 8, :].bitcast(I32), in_=dy_scales[:, 4 * q : 4 * q + 4, :].bitcast(I32)
             )
-        load_dy(0)
-        load_w2(0)
-        load_dy(1)
+        for q in range(4):
+            nc.sync.dma_start(
+                out=dy_sc[1][32 * q : 32 * q + 4, :].bitcast(I32), in_=dy_scales[1, 4 * q : 4 * q + 4, :].bitcast(I32)
+            )
         for q in range(4):
             nc.sync.dma_start(
                 out=w2_sc[32 * q : 32 * q + 4, :, :].bitcast(I32), in_=w2_rows[4 * q : 4 * q + 4, :, :].bitcast(I32)
             )
-        nc.sync.dma_start(out=a_nat[0][:], in_=a_by_tile[:, :, 0:512])
+        load_dy(0)
+        load_dy(1)
+        load_w2(0)
+        for u in range(2):
+            nc.sync.dma_start(out=a_early[u][:], in_=a_by_tile[:, :, 256 * u : 256 * u + 256])
         load_w2(1)
-        nc.sync.dma_start(out=a_nat[1][:], in_=a_by_tile[:, :, 512:1024])
-        load_w2(2)
-        nc.sync.dma_start(out=w1_raw[:], in_=w1t.rearrange("(p j) k -> p j k", j=PACK))
-        load_w2(3)
         nc.sync.dma_start(pos_sb[0][:], pos1)
         nc.sync.dma_start(pos_sb[1][:], pos2)
         nc.sync.dma_start(out=gate_rows[0:16, :], in_=gate[:, 0, :].rearrange("r (c t) -> r c t", t=P))
+        load_w2(2)
+        nc.sync.dma_start(out=a_late[:], in_=a_by_tile[:, :, 512:1024])
+        load_w2(3)
+        nc.sync.dma_start(out=w1_raw[:], in_=w1t.rearrange("(p j) k -> p j k", j=PACK))
         for h in range(2):
             nc.sync.dma_start(out=a_quad[h][:], in_=a_by_quad[:, :, 512 * h : 512 * h + 512])
 
         def expert_offs(e):
             return offs_sb[:, e * C // 16 : (e + 1) * C // 16]
 
+        for u in range(2):
+            nc.vector.tensor_copy(late_sc[0][:, u * C : (u + 1) * C], dy_sc[0][:].indirect(expert_offs(2 + u)))
+        nc.scalar.dma_start(out=late_sc[1][0:SHIFTED, :].bitcast(I32), in_=late_sc[0][4 : 4 + SHIFTED, :].bitcast(I32))
+
+        for u in range(2):
+            nc.scalar.activation(out=sg[0][:, :, 256 * u : 256 * u + 256], in_=a_early[u][:], func=ACT.Sigmoid)
+
         for e in range(E):
             accs = [bank((e * TILES + j) % 8) for j in range(TILES)]
             for s in range(PASSES):
-                slot_sc = slots.tile([P, C], U8, name="slot_sc", align_bytes=64)
-                slot_w = slots.tile([P, C], U32, name="slot_w", align_bytes=64)
-                nc.vector.tensor_copy(slot_sc[:], dy_sc[:, s, :].indirect(expert_offs(e)))
+                if e < 2:
+                    slot_sc = slots.tile([P, C], U8, name="slot_sc", align_bytes=64)[:]
+                    nc.vector.tensor_copy(slot_sc, dy_sc[s][:].indirect(expert_offs(e)))
+                else:
+                    slot_sc = late_sc[s][:, (e - 2) * C : (e - 1) * C]
+                slot_w = ring3.tile([P, C], U32, name="slot_w", align_bytes=64)
                 nc.vector.tensor_copy(slot_w[:], dy_w[s][:].bitcast(U32).indirect(expert_offs(e)))
                 for j in range(TILES):
                     nc.tensor.matmul_mx(
@@ -117,16 +136,16 @@ def tile_moe_sub_silu_kernel(
                         lhsT=w2_w[e][:, s, j * P : (j + 1) * P].bitcast(E4M3),
                         lhsT_scale=w2_sc[:, e * PASSES + s, j * P : (j + 1) * P],
                         rhs=slot_w[:].bitcast(E5M2),
-                        rhs_scale=slot_sc[:],
+                        rhs_scale=slot_sc,
                         start=(s == 0),
                         stop=(s == PASSES - 1),
                     )
             for j in range(TILES):
                 nc.scalar.copy(out=y[j][:, e * C : (e + 1) * C], in_=accs[j][:])
 
-        for h in range(2):
-            for jj in range(2):
-                nc.scalar.activation(out=sg[h][:, 2 * jj : 2 * jj + 2, :], in_=a_nat[h][:, 2 * jj : 2 * jj + 2, :], func=ACT.Sigmoid)
+        sg.append(keep.tile([P, TILES, 512], F32, name="w2_w3", align_bytes=64))
+        for jj in range(2):
+            nc.scalar.activation(out=sg[1][:, 2 * jj : 2 * jj + 2, :], in_=a_late[:, 2 * jj : 2 * jj + 2, :], func=ACT.Sigmoid)
 
         nc.vector.tensor_copy(out=w1_bf[:], in_=w1_raw[:].rearrange("p j k -> p k j"))
         gate_t = bank(6)

@@ -19,12 +19,27 @@ ALU = mybir.AluOpType
 
 P = 128
 PACK = 4
+QUADRANTS = 4
+SCALE_ROWS = 4
+BANK = 512
+BANKS = 8
+LISTS = 2
+PER_COLUMN = 16
 PASSES = N // (P * PACK)
 TILES = H // P
 SLOTS = E * C
+HALF = T // 2
+QUARTER = T // 4
+GATE_ROWS = T // P
+
 BLOCKS = [256, 256, 256, 128, 128]
-AHEAD = 2
-SHIFTED = 112
+GATHERS = LISTS * TILES
+DIRECT = 2
+MOVED_PARTITIONS = 112
+SCALE_BUFS = 2
+WORD_BUFS = 3
+COMBINE_BUFS = 10
+RESULT_BUFS = 4
 
 
 def tile_moe_sub_silu_kernel(
@@ -33,31 +48,30 @@ def tile_moe_sub_silu_kernel(
     nc = tc.nc
     with ExitStack() as ctx:
         keep = ctx.enter_context(tc.tile_pool(name="keep", bufs=1))
-        ring = ctx.enter_context(tc.tile_pool(name="ring", bufs=10))
-        slots = ctx.enter_context(tc.tile_pool(name="slots", bufs=AHEAD))
-        ring3 = ctx.enter_context(tc.tile_pool(name="ring3", bufs=3))
-        ring4 = ctx.enter_context(tc.tile_pool(name="ring4", bufs=4))
+        combine = ctx.enter_context(tc.tile_pool(name="combine", bufs=COMBINE_BUFS))
+        scale_ring = ctx.enter_context(tc.tile_pool(name="scale_ring", bufs=SCALE_BUFS))
+        word_ring = ctx.enter_context(tc.tile_pool(name="word_ring", bufs=WORD_BUFS))
+        results = ctx.enter_context(tc.tile_pool(name="results", bufs=RESULT_BUFS))
         psum = ctx.enter_context(tc.psum_pool(name="psum", bufs=1))
 
         def bank(b):
-            return psum.tile([P, 512], F32, name="bank%d" % b)
+            return psum.tile([P, BANK], F32, name="bank%d" % b)
 
-        offs_sb = keep.tile([P, SLOTS // 16], U16, name="offs_sb")
-        pos_sb = [keep.tile([P, T // 16], U16, name="pos_sb%d" % r) for r in range(2)]
+        offs_sb = keep.tile([P, SLOTS // PER_COLUMN], U16, name="offs_sb")
+        pos_sb = [keep.tile([P, T // PER_COLUMN], U16, name="pos_sb%d" % r) for r in range(LISTS)]
         dy_sc = [keep.tile([P, T], U8, name="dy_sc%d" % s, align_bytes=64) for s in range(PASSES)]
-        late_sc = [keep.tile([P, 2 * C], U8, name="late_sc%d" % s, align_bytes=64) for s in range(PASSES)]
+        late_sc = [keep.tile([P, (E - DIRECT) * C], U8, name="late_sc%d" % s, align_bytes=64) for s in range(PASSES)]
         dy_w = [keep.tile([P, T], I32, name="dy_w%d" % s, align_bytes=64) for s in range(PASSES)]
         w2_sc = keep.tile([P, E * PASSES, H], U8, name="w2_sc", align_bytes=64)
         w2_w = [keep.tile([P, PASSES, H], I32, name="w2_w%d" % e, align_bytes=64) for e in range(E)]
         y = [keep.tile([P, SLOTS], F32, name="y%d" % j) for j in range(TILES)]
-        a_early = [keep.tile([P, TILES, 256], F32, name="a_early%d" % u) for u in range(2)]
-        a_late = keep.tile([P, TILES, 512], F32, name="a_late")
-        a_quad = [keep.tile([P, PACK, 512], F32, name="a_quad%d" % h) for h in range(2)]
-        sg = [keep.tile([P, TILES, 512], F32, name="sg0")]
+        a_early = [keep.tile([P, TILES, QUARTER], F32, name="a_early%d" % u) for u in range(2)]
+        a_late = keep.tile([P, TILES, HALF], F32, name="a_late")
+        a_quad = [keep.tile([P, PACK, HALF], F32, name="a_quad%d" % h) for h in range(2)]
+        sigmoid = [keep.tile([P, TILES, HALF], F32, name="sigmoid_early")]
         gate_rows = keep.tile([P, P], F32, name="gate_rows")
-        gate_neg = keep.tile([P, 16], F32, name="gate_neg")
+        gate_neg = keep.tile([P, LISTS * GATE_ROWS], F32, name="gate_neg")
         ident = keep.tile([P, P], F32, name="ident")
-        warm = keep.tile([P, 1], F32, name="warm")
         w1_raw = keep.tile([P, PACK, K], F32, name="w1_raw")
         w1_bf = keep.tile([P, K, PACK], BF16, name="w1_bf", align_bytes=64)
         w1_w = keep.tile([P, K], U32, name="w1_w", align_bytes=64)
@@ -69,7 +83,6 @@ def tile_moe_sub_silu_kernel(
             nc.gpsimd.memset(dy_sc[s][:].bitcast(I32), 0)
         nc.gpsimd.memset(gate_rows[:], 0.0)
         make_identity(nc, ident[:])
-        nc.scalar.activation(out=warm[:], in_=gate_rows[:, 0:1], func=ACT.Sigmoid)
 
         def load_dy(s):
             nc.sync.dma_start(out=dy_w[s][:], in_=dy_words[s].rearrange("p t d -> p (t d)").bitcast(I32))
@@ -77,58 +90,59 @@ def tile_moe_sub_silu_kernel(
         def load_w2(e):
             nc.sync.dma_start(out=w2_w[e][:], in_=w2t_words[e].rearrange("s p i d -> p s (i d)").bitcast(I32))
 
+        def load_scale_rows(tile, rows_a_quadrant, source):
+            for q in range(QUADRANTS):
+                nc.sync.dma_start(
+                    out=tile[32 * q : 32 * q + rows_a_quadrant].bitcast(I32),
+                    in_=source(SCALE_ROWS * q, SCALE_ROWS * (q + 1)).bitcast(I32),
+                )
+
         a_by_tile = a.rearrange("(j p) t -> p j t", p=P)
-        a_by_quad = a.rearrange("(p j) t -> p j t", j=PACK)
+        a_by_quad = a.rearrange("(p d) t -> p d t", d=PACK)
         w2_rows = w2t_scales.rearrange("e s b i -> b (e s) i")
 
         nc.sync.dma_start(offs_sb[:], offs)
-        for q in range(4):
-            nc.sync.dma_start(
-                out=dy_sc[0][32 * q : 32 * q + 8, :].bitcast(I32), in_=dy_scales[:, 4 * q : 4 * q + 4, :].bitcast(I32)
-            )
-        for q in range(4):
-            nc.sync.dma_start(
-                out=dy_sc[1][32 * q : 32 * q + 4, :].bitcast(I32), in_=dy_scales[1, 4 * q : 4 * q + 4, :].bitcast(I32)
-            )
-        for q in range(4):
-            nc.sync.dma_start(
-                out=w2_sc[32 * q : 32 * q + 4, :, :].bitcast(I32), in_=w2_rows[4 * q : 4 * q + 4, :, :].bitcast(I32)
-            )
+        load_scale_rows(dy_sc[0], PASSES * SCALE_ROWS, lambda b0, b1: dy_scales[:, b0:b1, :])
+        load_scale_rows(dy_sc[1], SCALE_ROWS, lambda b0, b1: dy_scales[1, b0:b1, :])
+        load_scale_rows(w2_sc, SCALE_ROWS, lambda b0, b1: w2_rows[b0:b1, :, :])
         load_dy(0)
         load_dy(1)
         load_w2(0)
         for u in range(2):
-            nc.sync.dma_start(out=a_early[u][:], in_=a_by_tile[:, :, 256 * u : 256 * u + 256])
+            nc.sync.dma_start(out=a_early[u][:], in_=a_by_tile[:, :, QUARTER * u : QUARTER * (u + 1)])
         load_w2(1)
         nc.sync.dma_start(pos_sb[0][:], pos1)
         nc.sync.dma_start(pos_sb[1][:], pos2)
-        nc.sync.dma_start(out=gate_rows[0:16, :], in_=gate[:, 0, :].rearrange("r (c t) -> r c t", t=P))
+        nc.sync.dma_start(out=gate_rows[0 : LISTS * GATE_ROWS, :], in_=gate[:, 0, :].rearrange("r (c t) -> r c t", t=P))
         load_w2(2)
-        nc.sync.dma_start(out=a_late[:], in_=a_by_tile[:, :, 512:1024])
         load_w2(3)
-        nc.sync.dma_start(out=w1_raw[:], in_=w1t.rearrange("(p j) k -> p j k", j=PACK))
+        nc.sync.dma_start(out=w1_raw[:], in_=w1t.rearrange("(p d) k -> p d k", d=PACK))
+        nc.sync.dma_start(out=a_late[:], in_=a_by_tile[:, :, HALF:T])
         for h in range(2):
-            nc.sync.dma_start(out=a_quad[h][:], in_=a_by_quad[:, :, 512 * h : 512 * h + 512])
+            nc.sync.dma_start(out=a_quad[h][:], in_=a_by_quad[:, :, HALF * h : HALF * (h + 1)])
 
         def expert_offs(e):
-            return offs_sb[:, e * C // 16 : (e + 1) * C // 16]
+            return offs_sb[:, e * C // PER_COLUMN : (e + 1) * C // PER_COLUMN]
+
+        for u in range(E - DIRECT):
+            nc.vector.tensor_copy(late_sc[0][:, u * C : (u + 1) * C], dy_sc[0][:].indirect(expert_offs(DIRECT + u)))
+        nc.scalar.dma_start(
+            out=late_sc[1][0:MOVED_PARTITIONS, :].bitcast(I32),
+            in_=late_sc[0][SCALE_ROWS : SCALE_ROWS + MOVED_PARTITIONS, :].bitcast(I32),
+        )
 
         for u in range(2):
-            nc.vector.tensor_copy(late_sc[0][:, u * C : (u + 1) * C], dy_sc[0][:].indirect(expert_offs(2 + u)))
-        nc.scalar.dma_start(out=late_sc[1][0:SHIFTED, :].bitcast(I32), in_=late_sc[0][4 : 4 + SHIFTED, :].bitcast(I32))
-
-        for u in range(2):
-            nc.scalar.activation(out=sg[0][:, :, 256 * u : 256 * u + 256], in_=a_early[u][:], func=ACT.Sigmoid)
+            nc.scalar.activation(out=sigmoid[0][:, :, QUARTER * u : QUARTER * (u + 1)], in_=a_early[u][:], func=ACT.Sigmoid)
 
         for e in range(E):
-            accs = [bank((e * TILES + j) % 8) for j in range(TILES)]
+            accs = [bank((e * TILES + j) % BANKS) for j in range(TILES)]
             for s in range(PASSES):
-                if e < 2:
-                    slot_sc = slots.tile([P, C], U8, name="slot_sc", align_bytes=64)[:]
+                if e < DIRECT:
+                    slot_sc = scale_ring.tile([P, C], U8, name="slot_sc", align_bytes=64)[:]
                     nc.vector.tensor_copy(slot_sc, dy_sc[s][:].indirect(expert_offs(e)))
                 else:
-                    slot_sc = late_sc[s][:, (e - 2) * C : (e - 1) * C]
-                slot_w = ring3.tile([P, C], U32, name="slot_w", align_bytes=64)
+                    slot_sc = late_sc[s][:, (e - DIRECT) * C : (e - DIRECT + 1) * C]
+                slot_w = word_ring.tile([P, C], U32, name="slot_w", align_bytes=64)
                 nc.vector.tensor_copy(slot_w[:], dy_w[s][:].bitcast(U32).indirect(expert_offs(e)))
                 for j in range(TILES):
                     nc.tensor.matmul_mx(
@@ -143,53 +157,53 @@ def tile_moe_sub_silu_kernel(
             for j in range(TILES):
                 nc.scalar.copy(out=y[j][:, e * C : (e + 1) * C], in_=accs[j][:])
 
-        sg.append(keep.tile([P, TILES, 512], F32, name="w2_w3", align_bytes=64))
-        for jj in range(2):
-            nc.scalar.activation(out=sg[1][:, 2 * jj : 2 * jj + 2, :], in_=a_late[:, 2 * jj : 2 * jj + 2, :], func=ACT.Sigmoid)
+        sigmoid.append(keep.tile([P, TILES, HALF], F32, name="w2_w%d" % (E - 1), align_bytes=64))
+        for u in range(2):
+            nc.scalar.activation(out=sigmoid[1][:, 2 * u : 2 * u + 2, :], in_=a_late[:, 2 * u : 2 * u + 2, :], func=ACT.Sigmoid)
 
-        nc.vector.tensor_copy(out=w1_bf[:], in_=w1_raw[:].rearrange("p j k -> p k j"))
+        nc.vector.tensor_copy(out=w1_bf[:], in_=w1_raw[:].rearrange("p d k -> p k d"))
         gate_t = bank(6)
         nc.tensor.transpose(gate_t[:, 0:P], gate_rows[:], ident[:])
-        nc.scalar.activation(out=gate_neg[:], in_=gate_t[:, 0:16], func=ACT.Copy, scale=-1.0)
-        nc.vector.quantize_mx(out=w1_w[:].bitcast(E4M3), scales=w1_sc[:], in_=w1_bf[:].rearrange("p k j -> p (k j)"))
+        nc.scalar.activation(out=gate_neg[:], in_=gate_t[:, 0 : LISTS * GATE_ROWS], func=ACT.Copy, scale=-1.0)
+        nc.vector.quantize_mx(out=w1_w[:].bitcast(E4M3), scales=w1_sc[:], in_=w1_bf[:].rearrange("p k d -> p (k d)"))
 
         starts = [sum(BLOCKS[:b]) for b in range(len(BLOCKS))]
         last = len(BLOCKS) - 1
         turn_banks = [[[0, 1], [2, 3]]] * 3 + [[[0], [1]], [[2], [3]]]
         sum_banks = [[4, 5], [6, 7], [4, 5], [6], [7]]
         sums = {}
-        grouped = {}
+        rounded = {}
 
         def fetch(b, after):
             t0, width = starts[b], BLOCKS[b]
             subs = width // P
             for c in range(subs):
                 sums[b, c] = bank(sum_banks[b][c])
-            for r in range(2):
-                split = b == last and r == 1
+            for r in range(LISTS):
+                split = b == last and r == LISTS - 1
                 turned = [bank(turn_banks[b][r][c]) for c in range(subs)]
-                gated = [ring.tile([P, PACK, P], F32, name="gated") for c in range(subs)]
+                gated = [combine.tile([P, PACK, P], F32, name="gated") for c in range(subs)]
 
                 def weigh(c, source, j0, j1):
-                    col = 8 * r + t0 // P + c
+                    col = GATE_ROWS * r + t0 // P + c
                     nc.scalar.activation(
                         out=gated[c][:, :, 32 * j0 : 32 * j1],
-                        in_=source[:, j0 * P : j1 * P].rearrange("t (p j) -> t j p", j=PACK),
+                        in_=source[:, j0 * P : j1 * P].rearrange("t (p d) -> t d p", d=PACK),
                         func=ACT.Copy,
                         scale=gate_neg[:, col : col + 1],
                     )
 
                 for j in range(TILES):
-                    picked = ring.tile([P, width], F32, name="picked")
+                    picked = combine.tile([P, width], F32, name="picked")
                     nc.vector.tensor_tensor(
                         picked[:],
-                        y[j][:].indirect(pos_sb[r][:, t0 // 16 : (t0 + width) // 16]),
-                        sg[t0 // 512][:, j, t0 % 512 : t0 % 512 + width],
+                        y[j][:].indirect(pos_sb[r][:, t0 // PER_COLUMN : (t0 + width) // PER_COLUMN]),
+                        sigmoid[t0 // HALF][:, j, t0 % HALF : t0 % HALF + width],
                         ALU.mult,
                     )
                     if split and j == TILES - 1:
                         weigh(0, turned[0], 0, j)
-                        turned = [bank(0)]
+                        turned = [bank(turn_banks[b - 1][0][0])]
                     for c in range(subs):
                         nc.tensor.transpose(turned[c][:, j * P : (j + 1) * P], picked[:, c * P : (c + 1) * P], ident[:])
                     if j == TILES - 1:
@@ -198,27 +212,27 @@ def tile_moe_sub_silu_kernel(
                             for d in range(PACK):
                                 nc.tensor.matmul(
                                     sums[b, c][:, d * P : (d + 1) * P], gated[c][:, d, :], ident[:],
-                                    start=(r == 0 and d == 0), stop=(r == 1 and d == PACK - 1), is_transpose=True,
+                                    start=(r == 0 and d == 0), stop=(r == LISTS - 1 and d == PACK - 1), is_transpose=True,
                                 )
-                    for step in after.get(8 * b + 4 * r + j, []):
+                    for step in after.get(GATHERS * b + TILES * r + j, []):
                         step()
 
         def finish(b, c):
             t0 = starts[b] + c * P
-            silu_neg = ring.tile([P, P, PACK], F32, name="silu_neg")
+            silu_neg = combine.tile([P, P, PACK], F32, name="silu_neg")
             nc.scalar.activation(
                 out=silu_neg[:],
-                in_=a_quad[t0 // 512][:, :, t0 % 512 : t0 % 512 + P].rearrange("p j t -> p t j"),
+                in_=a_quad[t0 // HALF][:, :, t0 % HALF : t0 % HALF + P].rearrange("p d t -> p t d"),
                 func=ACT.Silu,
                 scale=-1.0,
             )
             if c == 0:
-                grouped[b] = ring4.tile([P, BLOCKS[b], PACK], BF16, name="da_bf", align_bytes=64)
+                rounded[b] = results.tile([P, BLOCKS[b], PACK], BF16, name="da_bf", align_bytes=64)
             nc.vector.scalar_tensor_tensor(
-                out=grouped[b][:, c * P : (c + 1) * P, :],
+                out=rounded[b][:, c * P : (c + 1) * P, :],
                 in0=silu_neg[:],
                 scalar=1.0,
-                in1=sums[b, c][:].rearrange("p (j t) -> p t j", j=PACK),
+                in1=sums[b, c][:].rearrange("p (d t) -> p t d", d=PACK),
                 op0=ALU.subtract,
                 op1=ALU.mult,
             )
@@ -228,43 +242,43 @@ def tile_moe_sub_silu_kernel(
             nc.vector.quantize_mx(
                 out=da_w[:, t0 : t0 + width].bitcast(E5M2),
                 scales=da_sc[:, t0 : t0 + width],
-                in_=grouped[b][:].rearrange("p t j -> p (t j)"),
+                in_=rounded[b][:].rearrange("p t d -> p (t d)"),
             )
 
         out_by_tile = out.rearrange("(m p) t -> p m t", p=P)
 
-        def project(t0, new, banks, both_engines):
-            res = ring4.tile([P, K // P, new], F32, name="res")
+        def project(end, new, banks, both_engines):
+            res = results.tile([P, K // P, new], F32, name="res")
             for m in range(K // P):
                 acc = bank(banks[m])
                 nc.tensor.matmul_mx(
                     out=acc[:],
                     lhsT=w1_w[:, m * P : (m + 1) * P].bitcast(E4M3),
                     lhsT_scale=w1_sc[:, m * P : (m + 1) * P],
-                    rhs=da_w[:, t0 : t0 + 512].bitcast(E5M2),
-                    rhs_scale=da_sc[:, t0 : t0 + 512],
+                    rhs=da_w[:, end - BANK : end].bitcast(E5M2),
+                    rhs_scale=da_sc[:, end - BANK : end],
                     start=True,
                     stop=True,
                 )
                 if m == 1 and both_engines:
-                    nc.vector.tensor_copy(out=res[:, m, :], in_=acc[:, 512 - new : 512])
+                    nc.vector.tensor_copy(out=res[:, m, :], in_=acc[:, BANK - new : BANK])
                 else:
-                    nc.scalar.copy(out=res[:, m, :], in_=acc[:, 512 - new : 512])
-            nc.sync.dma_start(out=out_by_tile[:, :, t0 + 512 - new : t0 + 512], in_=res[:])
+                    nc.scalar.copy(out=res[:, m, :], in_=acc[:, BANK - new : BANK])
+            nc.sync.dma_start(out=out_by_tile[:, :, end - new : end], in_=res[:])
 
         after = {
-            13: [lambda: finish(0, 0), lambda: finish(0, 1)],
-            15: [lambda: quantise(0)],
-            21: [lambda: finish(1, 0), lambda: finish(1, 1)],
-            23: [lambda: quantise(1), lambda: project(0, 512, [6, 7], False)],
-            31: [lambda: finish(2, 0)],
-            33: [lambda: finish(2, 1)],
-            35: [lambda: quantise(2)],
-            38: [lambda: finish(3, 0)],
-            39: [lambda: quantise(3), lambda: project(384, 384, [4, 5], False)],
+            GATHERS + 5: [lambda: finish(0, 0), lambda: finish(0, 1)],
+            GATHERS + 7: [lambda: quantise(0)],
+            2 * GATHERS + 5: [lambda: finish(1, 0), lambda: finish(1, 1)],
+            2 * GATHERS + 7: [lambda: quantise(1), lambda: project(starts[2], starts[2], sum_banks[1], False)],
+            3 * GATHERS + 7: [lambda: finish(2, 0)],
+            4 * GATHERS + 1: [lambda: finish(2, 1)],
+            4 * GATHERS + 3: [lambda: quantise(2)],
+            4 * GATHERS + 6: [lambda: finish(3, 0)],
+            4 * GATHERS + 7: [lambda: quantise(3), lambda: project(starts[last], starts[last] - starts[2], sum_banks[2], False)],
         }
         for b in range(len(BLOCKS)):
             fetch(b, after)
         finish(last, 0)
         quantise(last)
-        project(512, 128, [1, 6], True)
+        project(T, BLOCKS[last], [turn_banks[last - 1][1][0], sum_banks[last - 1][0]], True)

@@ -37,7 +37,7 @@ GATHERS = LISTS * TILES
 DIRECT = 2
 MOVED_PARTITIONS = 112
 SCALE_BUFS = 2
-WORD_BUFS = 3
+WORD_BUFS = 8
 COMBINE_BUFS = 10
 RESULT_BUFS = 4
 
@@ -49,7 +49,6 @@ def tile_moe_sub_silu_kernel(
     with ExitStack() as ctx:
         keep = ctx.enter_context(tc.tile_pool(name="keep", bufs=1))
         combine = ctx.enter_context(tc.tile_pool(name="combine", bufs=COMBINE_BUFS))
-        scale_ring = ctx.enter_context(tc.tile_pool(name="scale_ring", bufs=SCALE_BUFS))
         word_ring = ctx.enter_context(tc.tile_pool(name="word_ring", bufs=WORD_BUFS))
         results = ctx.enter_context(tc.tile_pool(name="results", bufs=RESULT_BUFS))
         psum = ctx.enter_context(tc.psum_pool(name="psum", bufs=1))
@@ -59,36 +58,32 @@ def tile_moe_sub_silu_kernel(
 
         offs_sb = keep.tile([P, SLOTS // PER_COLUMN], U16, name="offs_sb")
         pos_sb = [keep.tile([P, T // PER_COLUMN], U16, name="pos_sb%d" % r) for r in range(LISTS)]
-        dy_sc = [keep.tile([P, T], U8, name="dy_sc%d" % s, align_bytes=64) for s in range(PASSES)]
-        late_sc = [keep.tile([P, (E - DIRECT) * C], U8, name="late_sc%d" % s, align_bytes=64) for s in range(PASSES)]
-        dy_w = [keep.tile([P, T], I32, name="dy_w%d" % s, align_bytes=64) for s in range(PASSES)]
+        dy_sc = keep.tile([P, T], U8, name="buf_a", align_bytes=64)
+        slot_sc = [[keep.tile([P, 2 * C], U8, name="slot_sc%d%d" % (g, s), align_bytes=64) for s in range(PASSES)] for g in range(2)]
+        dy_w = keep.tile([P, PASSES, T], I32, name="buf_b", align_bytes=64)
         w2_sc = keep.tile([P, E * PASSES, H], U8, name="w2_sc", align_bytes=64)
-        w2_w = [keep.tile([P, PASSES, H], I32, name="w2_w%d" % e, align_bytes=64) for e in range(E)]
+        w2_first = keep.tile([P, PASSES * H], I32, name="w2_first", align_bytes=64)
         y = [keep.tile([P, SLOTS], F32, name="y%d" % j) for j in range(TILES)]
-        a_early = [keep.tile([P, TILES, QUARTER], F32, name="a_early%d" % u) for u in range(2)]
-        a_late = keep.tile([P, TILES, HALF], F32, name="a_late")
-        a_quad = [keep.tile([P, PACK, HALF], F32, name="a_quad%d" % h) for h in range(2)]
+        a_first = keep.tile([P, TILES, QUARTER], F32, name="buf_d")
         sigmoid = [keep.tile([P, TILES, HALF], F32, name="sigmoid_early")]
         gate_rows = keep.tile([P, P], F32, name="gate_rows")
         gate_neg = keep.tile([P, LISTS * GATE_ROWS], F32, name="gate_neg")
         ident = keep.tile([P, P], F32, name="ident")
-        w1_raw = keep.tile([P, PACK, K], F32, name="w1_raw")
         w1_bf = keep.tile([P, K, PACK], BF16, name="w1_bf", align_bytes=64)
         w1_w = keep.tile([P, K], U32, name="w1_w", align_bytes=64)
         w1_sc = keep.tile([P, K], U8, name="w1_sc", align_bytes=64)
         da_w = keep.tile([P, T], U32, name="da_w", align_bytes=64)
         da_sc = keep.tile([P, T], U8, name="da_sc", align_bytes=64)
 
-        for s in range(PASSES):
-            nc.gpsimd.memset(dy_sc[s][:].bitcast(I32), 0)
+        nc.gpsimd.memset(dy_sc[:].bitcast(I32), 0)
         nc.gpsimd.memset(gate_rows[:], 0.0)
         make_identity(nc, ident[:])
 
-        def load_dy(s):
-            nc.sync.dma_start(out=dy_w[s][:], in_=dy_words[s].rearrange("p t d -> p (t d)").bitcast(I32))
-
-        def load_w2(e):
-            nc.sync.dma_start(out=w2_w[e][:], in_=w2t_words[e].rearrange("s p i d -> p s (i d)").bitcast(I32))
+        def load_w2(words, e0, e1):
+            nc.sync.dma_start(
+                out=words.rearrange("p (g i) -> p g i", i=H),
+                in_=w2t_words[e0:e1].rearrange("e s p i d -> p (e s) (i d)").bitcast(I32),
+            )
 
         def load_scale_rows(tile, rows_a_quadrant, source):
             for q in range(QUADRANTS):
@@ -102,69 +97,78 @@ def tile_moe_sub_silu_kernel(
         w2_rows = w2t_scales.rearrange("e s b i -> b (e s) i")
 
         nc.sync.dma_start(offs_sb[:], offs)
-        load_scale_rows(dy_sc[0], PASSES * SCALE_ROWS, lambda b0, b1: dy_scales[:, b0:b1, :])
-        load_scale_rows(dy_sc[1], SCALE_ROWS, lambda b0, b1: dy_scales[1, b0:b1, :])
+        load_scale_rows(dy_sc, PASSES * SCALE_ROWS, lambda b0, b1: dy_scales[:, b0:b1, :])
         load_scale_rows(w2_sc, SCALE_ROWS, lambda b0, b1: w2_rows[b0:b1, :, :])
-        load_dy(0)
-        load_dy(1)
-        load_w2(0)
-        for u in range(2):
-            nc.sync.dma_start(out=a_early[u][:], in_=a_by_tile[:, :, QUARTER * u : QUARTER * (u + 1)])
-        load_w2(1)
+        nc.sync.dma_start(out=dy_w[:], in_=dy_words.rearrange("s p t d -> p s (t d)").bitcast(I32))
+        nc.sync.dma_start(out=gate_rows[0 : LISTS * GATE_ROWS, :], in_=gate[:, 0, :].rearrange("r (c t) -> r c t", t=P))
         nc.sync.dma_start(pos_sb[0][:], pos1)
         nc.sync.dma_start(pos_sb[1][:], pos2)
-        nc.sync.dma_start(out=gate_rows[0 : LISTS * GATE_ROWS, :], in_=gate[:, 0, :].rearrange("r (c t) -> r c t", t=P))
-        load_w2(2)
-        load_w2(3)
-        nc.sync.dma_start(out=w1_raw[:], in_=w1t.rearrange("(p d) k -> p d k", d=PACK))
-        nc.sync.dma_start(out=a_late[:], in_=a_by_tile[:, :, HALF:T])
-        for h in range(2):
-            nc.sync.dma_start(out=a_quad[h][:], in_=a_by_quad[:, :, HALF * h : HALF * (h + 1)])
+        load_w2(w2_first[:], 0, 1)
+        nc.sync.dma_start(out=a_first[:], in_=a_by_tile[:, :, 0:QUARTER])
 
         def expert_offs(e):
             return offs_sb[:, e * C // PER_COLUMN : (e + 1) * C // PER_COLUMN]
 
-        for u in range(E - DIRECT):
-            nc.vector.tensor_copy(late_sc[0][:, u * C : (u + 1) * C], dy_sc[0][:].indirect(expert_offs(DIRECT + u)))
-        nc.scalar.dma_start(
-            out=late_sc[1][0:MOVED_PARTITIONS, :].bitcast(I32),
-            in_=late_sc[0][SCALE_ROWS : SCALE_ROWS + MOVED_PARTITIONS, :].bitcast(I32),
-        )
+        for g in range(2):
+            for u in range(2):
+                nc.vector.tensor_copy(slot_sc[g][0][:, u * C : (u + 1) * C], dy_sc[:].indirect(expert_offs(2 * g + u)))
+            nc.sync.dma_start(
+                out=slot_sc[g][1][0:MOVED_PARTITIONS, :].bitcast(I32),
+                in_=slot_sc[g][0][SCALE_ROWS : SCALE_ROWS + MOVED_PARTITIONS, :].bitcast(I32),
+            )
+        w2_rest = keep.tile([P, (E - 1) * PASSES * H], I32, name="buf_a", align_bytes=64)
+        load_w2(w2_rest[:, 0 : PASSES * H], 1, 2)
+        load_w2(w2_rest[:, PASSES * H :], 2, E)
 
-        for u in range(2):
-            nc.scalar.activation(out=sigmoid[0][:, :, QUARTER * u : QUARTER * (u + 1)], in_=a_early[u][:], func=ACT.Sigmoid)
+        gate_t = bank(0)
+        nc.tensor.transpose(gate_t[:, 0:P], gate_rows[:], ident[:])
+        nc.vector.tensor_scalar(out=gate_neg[:], in0=gate_t[:, 0 : LISTS * GATE_ROWS], scalar1=-1.0, scalar2=None, op0=ALU.mult)
+        nc.scalar.activation(out=sigmoid[0][:, :, 0:QUARTER], in_=a_first[:], func=ACT.Sigmoid)
+        late = keep.tile([P, PACK * K + 3 * TILES * HALF + TILES * QUARTER], F32, name="buf_d")
+        a_second = late[:, PACK * K + 3 * TILES * HALF :].rearrange("p (j t) -> p j t", j=TILES)
+        nc.sync.dma_start(out=a_second, in_=a_by_tile[:, :, QUARTER:HALF])
+        w1_raw = late[:, 0 : PACK * K].rearrange("p (d k) -> p d k", d=PACK)
+        parts = [late[:, PACK * K + n * TILES * HALF : PACK * K + (n + 1) * TILES * HALF].rearrange("p (j t) -> p j t", j=TILES) for n in range(3)]
+        a_late, a_quad = parts[0], parts[1:]
+        nc.sync.dma_start(out=w1_raw, in_=w1t.rearrange("(p d) k -> p d k", d=PACK))
+        nc.sync.dma_start(out=a_late, in_=a_by_tile[:, :, HALF:T])
+        for h in range(2):
+            nc.sync.dma_start(out=a_quad[h], in_=a_by_quad[:, :, HALF * h : HALF * (h + 1)])
+
+
+        slot_w = {}
+
+        def product(e, j, b):
+            g, u = divmod(e, 2)
+            weights = w2_first if e == 0 else w2_rest[:, (e - 1) * PASSES * H : e * PASSES * H]
+            acc = bank(b)
+            for s in range(PASSES):
+                nc.tensor.matmul_mx(
+                    out=acc[:],
+                    lhsT=weights[:, s * H + j * P : s * H + (j + 1) * P].bitcast(E4M3),
+                    lhsT_scale=w2_sc[:, e * PASSES + s, j * P : (j + 1) * P],
+                    rhs=slot_w[e, s][:].bitcast(E5M2),
+                    rhs_scale=slot_sc[g][s][:, u * C : (u + 1) * C],
+                    start=(s == 0),
+                    stop=(s == PASSES - 1),
+                )
+            nc.scalar.copy(out=y[j][:, e * C : (e + 1) * C], in_=acc[:])
 
         for e in range(E):
-            accs = [bank((e * TILES + j) % BANKS) for j in range(TILES)]
             for s in range(PASSES):
-                if e < DIRECT:
-                    slot_sc = scale_ring.tile([P, C], U8, name="slot_sc", align_bytes=64)[:]
-                    nc.vector.tensor_copy(slot_sc, dy_sc[s][:].indirect(expert_offs(e)))
-                else:
-                    slot_sc = late_sc[s][:, (e - DIRECT) * C : (e - DIRECT + 1) * C]
-                slot_w = word_ring.tile([P, C], U32, name="slot_w", align_bytes=64)
-                nc.vector.tensor_copy(slot_w[:], dy_w[s][:].bitcast(U32).indirect(expert_offs(e)))
-                for j in range(TILES):
-                    nc.tensor.matmul_mx(
-                        out=accs[j][:],
-                        lhsT=w2_w[e][:, s, j * P : (j + 1) * P].bitcast(E4M3),
-                        lhsT_scale=w2_sc[:, e * PASSES + s, j * P : (j + 1) * P],
-                        rhs=slot_w[:].bitcast(E5M2),
-                        rhs_scale=slot_sc,
-                        start=(s == 0),
-                        stop=(s == PASSES - 1),
-                    )
-            for j in range(TILES):
-                nc.scalar.copy(out=y[j][:, e * C : (e + 1) * C], in_=accs[j][:])
+                slot_w[e, s] = word_ring.tile([P, C], U32, name="slot_w", align_bytes=64)
+                nc.vector.tensor_copy(slot_w[e, s][:], dy_w[:, s, :].bitcast(U32).indirect(expert_offs(e)))
+            for j in range(TILES - 1):
+                product(e, j, TILES + j)
+        for e in range(E):
+            product(e, TILES - 1, TILES + e % (TILES - 1))
+        nc.scalar.activation(out=sigmoid[0][:, :, QUARTER:HALF], in_=a_second, func=ACT.Sigmoid)
 
-        sigmoid.append(keep.tile([P, TILES, HALF], F32, name="w2_w%d" % (E - 1), align_bytes=64))
+        sigmoid.append(keep.tile([P, TILES, HALF], F32, name="buf_a", align_bytes=64))
         for u in range(2):
             nc.scalar.activation(out=sigmoid[1][:, 2 * u : 2 * u + 2, :], in_=a_late[:, 2 * u : 2 * u + 2, :], func=ACT.Sigmoid)
 
-        nc.vector.tensor_copy(out=w1_bf[:], in_=w1_raw[:].rearrange("p d k -> p k d"))
-        gate_t = bank(6)
-        nc.tensor.transpose(gate_t[:, 0:P], gate_rows[:], ident[:])
-        nc.scalar.activation(out=gate_neg[:], in_=gate_t[:, 0 : LISTS * GATE_ROWS], func=ACT.Copy, scale=-1.0)
+        nc.vector.tensor_copy(out=w1_bf[:], in_=w1_raw.rearrange("p d k -> p k d"))
         nc.vector.quantize_mx(out=w1_w[:].bitcast(E4M3), scales=w1_sc[:], in_=w1_bf[:].rearrange("p k d -> p (k d)"))
 
         starts = [sum(BLOCKS[:b]) for b in range(len(BLOCKS))]
@@ -179,43 +183,49 @@ def tile_moe_sub_silu_kernel(
             subs = width // P
             for c in range(subs):
                 sums[b, c] = bank(sum_banks[b][c])
-            for r in range(LISTS):
+            turned = {}
+            gated = {}
+            if b == 0:
+                order = [(r, j) for j in range(TILES) for r in range(LISTS)]
+            else:
+                order = [(r, j) for r in range(LISTS) for j in range(TILES)]
+
+            def weigh(r, c, j0, j1):
+                col = GATE_ROWS * r + t0 // P + c
+                nc.scalar.activation(
+                    out=gated[r][c][:, :, 32 * j0 : 32 * j1],
+                    in_=turned[r][c][:, j0 * P : j1 * P].rearrange("t (p d) -> t d p", d=PACK),
+                    func=ACT.Copy,
+                    scale=gate_neg[:, col : col + 1],
+                )
+
+            for n, (r, j) in enumerate(order):
                 split = b == last and r == LISTS - 1
-                turned = [bank(turn_banks[b][r][c]) for c in range(subs)]
-                gated = [combine.tile([P, PACK, P], F32, name="gated") for c in range(subs)]
-
-                def weigh(c, source, j0, j1):
-                    col = GATE_ROWS * r + t0 // P + c
-                    nc.scalar.activation(
-                        out=gated[c][:, :, 32 * j0 : 32 * j1],
-                        in_=source[:, j0 * P : j1 * P].rearrange("t (p d) -> t d p", d=PACK),
-                        func=ACT.Copy,
-                        scale=gate_neg[:, col : col + 1],
-                    )
-
-                for j in range(TILES):
-                    picked = combine.tile([P, width], F32, name="picked")
-                    nc.vector.tensor_tensor(
-                        picked[:],
-                        y[j][:].indirect(pos_sb[r][:, t0 // PER_COLUMN : (t0 + width) // PER_COLUMN]),
-                        sigmoid[t0 // HALF][:, j, t0 % HALF : t0 % HALF + width],
-                        ALU.mult,
-                    )
-                    if split and j == TILES - 1:
-                        weigh(0, turned[0], 0, j)
-                        turned = [bank(turn_banks[b - 1][0][0])]
+                if j == 0:
+                    turned[r] = [bank(turn_banks[b][r][c]) for c in range(subs)]
+                    gated[r] = [combine.tile([P, PACK, P], F32, name="gated") for c in range(subs)]
+                picked = combine.tile([P, width], F32, name="picked")
+                nc.vector.tensor_tensor(
+                    picked[:],
+                    y[j][:].indirect(pos_sb[r][:, t0 // PER_COLUMN : (t0 + width) // PER_COLUMN]),
+                    sigmoid[t0 // HALF][:, j, t0 % HALF : t0 % HALF + width],
+                    ALU.mult,
+                )
+                if split and j == TILES - 1:
+                    weigh(r, 0, 0, j)
+                    turned[r] = [bank(turn_banks[b - 1][0][0])]
+                for c in range(subs):
+                    nc.tensor.transpose(turned[r][c][:, j * P : (j + 1) * P], picked[:, c * P : (c + 1) * P], ident[:])
+                if j == TILES - 1:
                     for c in range(subs):
-                        nc.tensor.transpose(turned[c][:, j * P : (j + 1) * P], picked[:, c * P : (c + 1) * P], ident[:])
-                    if j == TILES - 1:
-                        for c in range(subs):
-                            weigh(c, turned[c], j if split else 0, TILES)
-                            for d in range(PACK):
-                                nc.tensor.matmul(
-                                    sums[b, c][:, d * P : (d + 1) * P], gated[c][:, d, :], ident[:],
-                                    start=(r == 0 and d == 0), stop=(r == LISTS - 1 and d == PACK - 1), is_transpose=True,
-                                )
-                    for step in after.get(GATHERS * b + TILES * r + j, []):
-                        step()
+                        weigh(r, c, j if split else 0, TILES)
+                        for d in range(PACK):
+                            nc.tensor.matmul(
+                                sums[b, c][:, d * P : (d + 1) * P], gated[r][c][:, d, :], ident[:],
+                                start=(r == 0 and d == 0), stop=(r == LISTS - 1 and d == PACK - 1), is_transpose=True,
+                            )
+                for step in after.get(GATHERS * b + n, []):
+                    step()
 
         def finish(b, c):
             t0 = starts[b] + c * P

@@ -38,7 +38,8 @@ DIRECT = 2
 MOVED_PARTITIONS = 112
 SCALE_BUFS = 2
 WORD_BUFS = 8
-COMBINE_BUFS = 10
+COMBINE_BUFS = 8
+PICKED_BUFS = 8
 RESULT_BUFS = 4
 
 
@@ -152,12 +153,18 @@ def tile_moe_sub_silu_kernel(
                     start=(s == 0),
                     stop=(s == PASSES - 1),
                 )
-            nc.scalar.copy(out=y[j][:, e * C : (e + 1) * C], in_=acc[:])
+            if (e, j) == (E - 1, 1):
+                nc.vector.tensor_copy(out=y[j][:, e * C : (e + 1) * C], in_=acc[:])
+            else:
+                nc.scalar.copy(out=y[j][:, e * C : (e + 1) * C], in_=acc[:])
 
         for e in range(E):
             for s in range(PASSES):
                 slot_w[e, s] = word_ring.tile([P, C], U32, name="slot_w", align_bytes=64)
                 nc.vector.tensor_copy(slot_w[e, s][:], dy_w[:, s, :].bitcast(U32).indirect(expert_offs(e)))
+            if e == E - 1:
+                nc.vector.tensor_copy(out=w1_bf[:], in_=w1_raw.rearrange("p d k -> p k d"))
+                nc.vector.quantize_mx(out=w1_w[:].bitcast(E4M3), scales=w1_sc[:], in_=w1_bf[:].rearrange("p k d -> p (k d)"))
             for j in range(TILES - 1):
                 product(e, j, TILES + j)
         for e in range(E):
@@ -165,11 +172,11 @@ def tile_moe_sub_silu_kernel(
         nc.scalar.activation(out=sigmoid[0][:, :, QUARTER:HALF], in_=a_second, func=ACT.Sigmoid)
 
         sigmoid.append(keep.tile([P, TILES, HALF], F32, name="buf_a", align_bytes=64))
-        for u in range(2):
-            nc.scalar.activation(out=sigmoid[1][:, 2 * u : 2 * u + 2, :], in_=a_late[:, 2 * u : 2 * u + 2, :], func=ACT.Sigmoid)
 
-        nc.vector.tensor_copy(out=w1_bf[:], in_=w1_raw.rearrange("p d k -> p k d"))
-        nc.vector.quantize_mx(out=w1_w[:].bitcast(E4M3), scales=w1_sc[:], in_=w1_bf[:].rearrange("p k d -> p (k d)"))
+        def late_sigmoid():
+            for u in range(2):
+                nc.scalar.activation(out=sigmoid[1][:, 2 * u : 2 * u + 2, :], in_=a_late[:, 2 * u : 2 * u + 2, :], func=ACT.Sigmoid)
+
 
         starts = [sum(BLOCKS[:b]) for b in range(len(BLOCKS))]
         last = len(BLOCKS) - 1
@@ -177,6 +184,7 @@ def tile_moe_sub_silu_kernel(
         sum_banks = [[4, 5], [6, 7], [4, 5], [6], [7]]
         sums = {}
         rounded = {}
+        silu_neg = {}
 
         def fetch(b, after):
             t0, width = starts[b], BLOCKS[b]
@@ -204,7 +212,7 @@ def tile_moe_sub_silu_kernel(
                 if j == 0:
                     turned[r] = [bank(turn_banks[b][r][c]) for c in range(subs)]
                     gated[r] = [combine.tile([P, PACK, P], F32, name="gated") for c in range(subs)]
-                picked = combine.tile([P, width], F32, name="picked")
+                picked = keep.tile([P, width], F32, name="picked%d" % ((GATHERS * b + n) % PICKED_BUFS), align_bytes=64)
                 nc.vector.tensor_tensor(
                     picked[:],
                     y[j][:].indirect(pos_sb[r][:, t0 // PER_COLUMN : (t0 + width) // PER_COLUMN]),
@@ -229,18 +237,22 @@ def tile_moe_sub_silu_kernel(
 
         def finish(b, c):
             t0 = starts[b] + c * P
-            silu_neg = combine.tile([P, P, PACK], F32, name="silu_neg")
-            nc.scalar.activation(
-                out=silu_neg[:],
-                in_=a_quad[t0 // HALF][:, :, t0 % HALF : t0 % HALF + P].rearrange("p d t -> p t d"),
-                func=ACT.Silu,
-                scale=-1.0,
-            )
-            if c == 0:
+            quarter = t0 // QUARTER
+            if t0 % QUARTER == 0:
+                silu_neg[quarter] = keep.tile([P, QUARTER, PACK], F32, name="slot_sc1%d" % (1 - quarter % 2), align_bytes=64)
+                nc.scalar.activation(
+                    out=silu_neg[quarter][:].rearrange("p (c i) d -> p c d i", i=4),
+                    in_=a_quad[t0 // HALF][:, :, t0 % HALF : t0 % HALF + QUARTER].rearrange("p d (c i) -> p c d i", i=4),
+                    func=ACT.Silu,
+                    scale=-1.0,
+                )
+            if b == last - 1:
+                rounded[b] = keep.tile([P, BLOCKS[b], PACK], BF16, name="picked%d" % ((GATHERS * len(BLOCKS) - 2) % PICKED_BUFS), align_bytes=64)
+            elif c == 0:
                 rounded[b] = results.tile([P, BLOCKS[b], PACK], BF16, name="da_bf", align_bytes=64)
             nc.vector.scalar_tensor_tensor(
                 out=rounded[b][:, c * P : (c + 1) * P, :],
-                in0=silu_neg[:],
+                in0=silu_neg[quarter][:, t0 % QUARTER : t0 % QUARTER + P, :],
                 scalar=1.0,
                 in1=sums[b, c][:].rearrange("p (d t) -> p t d", d=PACK),
                 op0=ALU.subtract,
@@ -277,6 +289,7 @@ def tile_moe_sub_silu_kernel(
             nc.sync.dma_start(out=out_by_tile[:, :, end - new : end], in_=res[:])
 
         after = {
+            GATHERS - 1: [late_sigmoid],
             GATHERS + 5: [lambda: finish(0, 0), lambda: finish(0, 1)],
             GATHERS + 7: [lambda: quantise(0)],
             2 * GATHERS + 5: [lambda: finish(1, 0), lambda: finish(1, 1)],
@@ -284,11 +297,12 @@ def tile_moe_sub_silu_kernel(
             3 * GATHERS + 7: [lambda: finish(2, 0)],
             4 * GATHERS + 1: [lambda: finish(2, 1)],
             4 * GATHERS + 3: [lambda: quantise(2)],
-            4 * GATHERS + 6: [lambda: finish(3, 0)],
-            4 * GATHERS + 7: [lambda: quantise(3), lambda: project(starts[last], starts[last] - starts[2], sum_banks[2], False)],
         }
         for b in range(len(BLOCKS)):
             fetch(b, after)
+        finish(last - 1, 0)
+        quantise(last - 1)
+        project(starts[last], starts[last] - starts[2], [turn_banks[last - 1][0][0], sum_banks[last - 1][0]], False)
         finish(last, 0)
         quantise(last)
-        project(T, BLOCKS[last], [turn_banks[last - 1][1][0], sum_banks[last - 1][0]], True)
+        project(T, BLOCKS[last], [turn_banks[last - 1][1][0], sum_banks[2][0]], True)

@@ -66,7 +66,7 @@ def tile_moe_sub_silu_kernel(
         w2_first = keep.tile([P, PASSES * H], I32, name="w2_first", align_bytes=64)
         y = [keep.tile([P, SLOTS], F32, name="y%d" % j) for j in range(TILES)]
         a_first = keep.tile([P, TILES, QUARTER], F32, name="buf_d")
-        sigmoid = [keep.tile([P, TILES, HALF], F32, name="sigmoid_early")]
+        sigmoid = [keep.tile([P, TILES, QUARTER], F32, name="sigmoid_early")]
         gate_rows = keep.tile([P, P], F32, name="gate_rows")
         gate_neg = keep.tile([P, LISTS * GATE_ROWS], F32, name="gate_neg")
         ident = keep.tile([P, P], F32, name="ident")
@@ -104,8 +104,8 @@ def tile_moe_sub_silu_kernel(
         nc.sync.dma_start(out=gate_rows[0 : LISTS * GATE_ROWS, :], in_=gate[:, 0, :].rearrange("r (c t) -> r c t", t=P))
         nc.sync.dma_start(pos_sb[0][:], pos1)
         nc.sync.dma_start(pos_sb[1][:], pos2)
+        nc.sync.dma_start(out=a_first[:], in_=a_by_quad[:, :, T - QUARTER : T])
         load_w2(w2_first[:], 0, 1)
-        nc.sync.dma_start(out=a_first[:], in_=a_by_tile[:, :, 0:QUARTER])
 
         def expert_offs(e):
             return offs_sb[:, e * C // PER_COLUMN : (e + 1) * C // PER_COLUMN]
@@ -124,18 +124,28 @@ def tile_moe_sub_silu_kernel(
         gate_t = bank(0)
         nc.tensor.transpose(gate_t[:, 0:P], gate_rows[:], ident[:])
         nc.vector.tensor_scalar(out=gate_neg[:], in0=gate_t[:, 0 : LISTS * GATE_ROWS], scalar1=-1.0, scalar2=None, op0=ALU.mult)
-        nc.scalar.activation(out=sigmoid[0][:, :, 0:QUARTER], in_=a_first[:], func=ACT.Sigmoid)
-        late = keep.tile([P, PACK * K + 3 * TILES * HALF + TILES * QUARTER], F32, name="buf_d")
-        a_second = late[:, PACK * K + 3 * TILES * HALF :].rearrange("p (j t) -> p j t", j=TILES)
-        nc.sync.dma_start(out=a_second, in_=a_by_tile[:, :, QUARTER:HALF])
-        w1_raw = late[:, 0 : PACK * K].rearrange("p (d k) -> p d k", d=PACK)
-        parts = [late[:, PACK * K + n * TILES * HALF : PACK * K + (n + 1) * TILES * HALF].rearrange("p (j t) -> p j t", j=TILES) for n in range(3)]
-        a_late, a_quad = parts[0], parts[1:]
+        silu_last = keep.tile([P, QUARTER, PACK], F32, name="silu_last")
+        sigmoid_last = keep.tile([P, QUARTER, PACK], F32, name="sigmoid_last")
+        less_one = keep.tile([P, QUARTER, PACK], F32, name="less_one")
+        slope_neg = keep.tile([P, QUARTER, PACK], F32, name="slope_neg")
+        lines = a_first[:].rearrange("p d (c i) -> p c d i", i=4)
+        nc.scalar.activation(out=silu_last[:].rearrange("p (c i) d -> p c d i", i=4), in_=lines, func=ACT.Silu, scale=-1.0)
+        nc.scalar.activation(out=sigmoid_last[:].rearrange("p (c i) d -> p c d i", i=4), in_=lines, func=ACT.Sigmoid)
+        nc.gpsimd.tensor_scalar(out=less_one[:], in0=silu_last[:], scalar1=1.0, scalar2=-1.0, op0=ALU.mult, op1=ALU.add)
+        nc.gpsimd.tensor_tensor(slope_neg[:], less_one[:], sigmoid_last[:], ALU.mult)
+        part = TILES * QUARTER
+        late = keep.tile([P, 7 * part + LISTS * QUARTER], F32, name="buf_d")
+        w1_raw = late[:, 0:part].rearrange("p (d k) -> p d k", d=PACK)
+        a_tile = [late[:, (1 + n) * part : (2 + n) * part].rearrange("p (j t) -> p j t", j=TILES) for n in range(3)]
+        a_quad = [late[:, (4 + n) * part : (5 + n) * part].rearrange("p (d t) -> p d t", d=PACK) for n in range(3)]
+        gate_wide = late[:, 7 * part :].rearrange("p (r t) -> p r t", r=LISTS)
+        nc.sync.dma_start(out=a_tile[0], in_=a_by_tile[:, :, 0:QUARTER])
         nc.sync.dma_start(out=w1_raw, in_=w1t.rearrange("(p d) k -> p d k", d=PACK))
-        nc.sync.dma_start(out=a_late, in_=a_by_tile[:, :, HALF:T])
-        for h in range(2):
-            nc.sync.dma_start(out=a_quad[h], in_=a_by_quad[:, :, HALF * h : HALF * (h + 1)])
-
+        for n in (1, 2):
+            nc.sync.dma_start(out=a_tile[n], in_=a_by_tile[:, :, QUARTER * n : QUARTER * (n + 1)])
+        for n in range(3):
+            nc.sync.dma_start(out=a_quad[n], in_=a_by_quad[:, :, QUARTER * n : QUARTER * (n + 1)])
+        nc.sync.dma_start(out=gate_wide, in_=gate[:, :, T - QUARTER : T].rearrange("r p t -> p r t"))
 
         slot_w = {}
 
@@ -167,16 +177,20 @@ def tile_moe_sub_silu_kernel(
                 nc.vector.quantize_mx(out=w1_w[:].bitcast(E4M3), scales=w1_sc[:], in_=w1_bf[:].rearrange("p k d -> p (k d)"))
             for j in range(TILES - 1):
                 product(e, j, TILES + j)
+            if e == 1:
+                nc.scalar.activation(out=sigmoid[0][:], in_=a_tile[0], func=ACT.Sigmoid)
         for e in range(E):
             product(e, TILES - 1, TILES + e % (TILES - 1))
-        nc.scalar.activation(out=sigmoid[0][:, :, QUARTER:HALF], in_=a_second, func=ACT.Sigmoid)
 
-        sigmoid.append(keep.tile([P, TILES, HALF], F32, name="buf_a", align_bytes=64))
+        later = keep.tile([P, 2 * part], F32, name="buf_a", align_bytes=64)
+        sigmoid.extend([later[:, n * part : (n + 1) * part].rearrange("p (j t) -> p j t", j=TILES) for n in range(2)])
+        nc.scalar.activation(out=sigmoid[1], in_=a_tile[1], func=ACT.Sigmoid)
+
+        def by_lines(tile, quarter):
+            return tile.rearrange("p (c i) d -> p c d i", i=4), a_quad[quarter].rearrange("p d (c i) -> p c d i", i=4)
 
         def late_sigmoid():
-            for u in range(2):
-                nc.scalar.activation(out=sigmoid[1][:, 2 * u : 2 * u + 2, :], in_=a_late[:, 2 * u : 2 * u + 2, :], func=ACT.Sigmoid)
-
+            nc.scalar.activation(out=sigmoid[2], in_=a_tile[2], func=ACT.Sigmoid)
 
         starts = [sum(BLOCKS[:b]) for b in range(len(BLOCKS))]
         last = len(BLOCKS) - 1
@@ -189,6 +203,7 @@ def tile_moe_sub_silu_kernel(
         def fetch(b, after):
             t0, width = starts[b], BLOCKS[b]
             subs = width // P
+            narrow = b >= last - 1
             for c in range(subs):
                 sums[b, c] = bank(sum_banks[b][c])
             turned = {}
@@ -198,63 +213,85 @@ def tile_moe_sub_silu_kernel(
             else:
                 order = [(r, j) for r in range(LISTS) for j in range(TILES)]
 
-            def weigh(r, c, j0, j1):
-                col = GATE_ROWS * r + t0 // P + c
+            def regroup(dst, source, j0, j1, scale):
                 nc.scalar.activation(
-                    out=gated[r][c][:, :, 32 * j0 : 32 * j1],
-                    in_=turned[r][c][:, j0 * P : j1 * P].rearrange("t (p d) -> t d p", d=PACK),
+                    out=dst[:, :, 32 * j0 : 32 * j1],
+                    in_=source[:, j0 * P : j1 * P].rearrange("t (p d) -> t d p", d=PACK),
                     func=ACT.Copy,
-                    scale=gate_neg[:, col : col + 1],
+                    scale=scale,
                 )
 
+            if narrow:
+                main = bank(0 if b < last else 2)
+                side = bank(1) if b == last else main
+                summed = combine.tile([P, PACK, P], F32, name="gated")
             for n, (r, j) in enumerate(order):
-                split = b == last and r == LISTS - 1
-                if j == 0:
+                if j == 0 and not narrow:
                     turned[r] = [bank(turn_banks[b][r][c]) for c in range(subs)]
                     gated[r] = [combine.tile([P, PACK, P], F32, name="gated") for c in range(subs)]
                 picked = keep.tile([P, width], F32, name="picked%d" % ((GATHERS * b + n) % PICKED_BUFS), align_bytes=64)
+                if narrow:
+                    factor = gate_wide[:, r, t0 - (T - QUARTER) : t0 - (T - QUARTER) + width]
+                else:
+                    factor = sigmoid[b][:, j, :]
                 nc.vector.tensor_tensor(
                     picked[:],
                     y[j][:].indirect(pos_sb[r][:, t0 // PER_COLUMN : (t0 + width) // PER_COLUMN]),
-                    sigmoid[t0 // HALF][:, j, t0 % HALF : t0 % HALF + width],
+                    factor,
                     ALU.mult,
                 )
-                if split and j == TILES - 1:
-                    weigh(r, 0, 0, j)
-                    turned[r] = [bank(turn_banks[b - 1][0][0])]
-                for c in range(subs):
-                    nc.tensor.transpose(turned[r][c][:, j * P : (j + 1) * P], picked[:, c * P : (c + 1) * P], ident[:])
-                if j == TILES - 1:
-                    for c in range(subs):
-                        weigh(r, c, j if split else 0, TILES)
+                if narrow:
+                    alone = b == last and j == TILES - 1
+                    closing = TILES - 2 if b == last else TILES - 1
+                    nc.tensor.matmul(
+                        (side if alone else main)[:, j * P : (j + 1) * P], picked[:], ident[:],
+                        start=(r == 0 and (j == 0 or alone)), stop=(r == LISTS - 1 and (j == closing or alone)), is_transpose=True,
+                    )
+                    if r == LISTS - 1 and j == closing:
+                        regroup(summed, main, 0, j + 1, -1.0)
+                    if r == LISTS - 1 and alone:
+                        regroup(summed, side, j, j + 1, -1.0)
+                    if r == LISTS - 1 and j == TILES - 1:
                         for d in range(PACK):
-                            nc.tensor.matmul(
-                                sums[b, c][:, d * P : (d + 1) * P], gated[r][c][:, d, :], ident[:],
-                                start=(r == 0 and d == 0), stop=(r == LISTS - 1 and d == PACK - 1), is_transpose=True,
-                            )
+                            nc.tensor.transpose(sums[b, 0][:, d * P : (d + 1) * P], summed[:, d, :], ident[:])
+                else:
+                    for c in range(subs):
+                        nc.tensor.transpose(turned[r][c][:, j * P : (j + 1) * P], picked[:, c * P : (c + 1) * P], ident[:])
+                    if j == TILES - 1:
+                        for c in range(subs):
+                            col = GATE_ROWS * r + t0 // P + c
+                            regroup(gated[r][c], turned[r][c], 0, TILES, gate_neg[:, col : col + 1])
+                            for d in range(PACK):
+                                nc.tensor.matmul(
+                                    sums[b, c][:, d * P : (d + 1) * P], gated[r][c][:, d, :], ident[:],
+                                    start=(r == 0 and d == 0), stop=(r == LISTS - 1 and d == PACK - 1), is_transpose=True,
+                                )
                 for step in after.get(GATHERS * b + n, []):
                     step()
 
+        def silu(quarter):
+            silu_neg[quarter] = keep.tile([P, QUARTER, PACK], F32, name="slot_sc1%d" % (1 - quarter % 2), align_bytes=64)
+            dst, src = by_lines(silu_neg[quarter][:], quarter)
+            nc.scalar.activation(out=dst, in_=src, func=ACT.Silu, scale=-1.0)
+
         def finish(b, c):
             t0 = starts[b] + c * P
-            quarter = t0 // QUARTER
-            if t0 % QUARTER == 0:
-                silu_neg[quarter] = keep.tile([P, QUARTER, PACK], F32, name="slot_sc1%d" % (1 - quarter % 2), align_bytes=64)
-                nc.scalar.activation(
-                    out=silu_neg[quarter][:].rearrange("p (c i) d -> p c d i", i=4),
-                    in_=a_quad[t0 // HALF][:, :, t0 % HALF : t0 % HALF + QUARTER].rearrange("p d (c i) -> p c d i", i=4),
-                    func=ACT.Silu,
-                    scale=-1.0,
-                )
+            quarter, u = divmod(t0, QUARTER)
             if b == last - 1:
                 rounded[b] = keep.tile([P, BLOCKS[b], PACK], BF16, name="picked%d" % ((GATHERS * len(BLOCKS) - 2) % PICKED_BUFS), align_bytes=64)
             elif c == 0:
                 rounded[b] = results.tile([P, BLOCKS[b], PACK], BF16, name="da_bf", align_bytes=64)
+            total = sums[b, c][:].rearrange("p (d t) -> p t d", d=PACK)
+            if b >= last - 1:
+                nc.vector.tensor_tensor(rounded[b][:], slope_neg[:, u : u + P, :], total, ALU.mult)
+                return
+            if c == 0:
+                silu(quarter)
             nc.vector.scalar_tensor_tensor(
                 out=rounded[b][:, c * P : (c + 1) * P, :],
-                in0=silu_neg[quarter][:, t0 % QUARTER : t0 % QUARTER + P, :],
+                in0=silu_neg[quarter][:, u : u + P, :],
                 scalar=1.0,
-                in1=sums[b, c][:].rearrange("p (d t) -> p t d", d=PACK),
+                in1=total,
                 op0=ALU.subtract,
                 op1=ALU.mult,
             )
@@ -302,7 +339,7 @@ def tile_moe_sub_silu_kernel(
             fetch(b, after)
         finish(last - 1, 0)
         quantise(last - 1)
-        project(starts[last], starts[last] - starts[2], [turn_banks[last - 1][0][0], sum_banks[last - 1][0]], False)
+        project(starts[last], starts[last] - starts[2], [1, sum_banks[last - 1][0]], False)
         finish(last, 0)
         quantise(last)
-        project(T, BLOCKS[last], [turn_banks[last - 1][1][0], sum_banks[2][0]], True)
+        project(T, BLOCKS[last], [3, sum_banks[2][0]], True)

@@ -30,7 +30,7 @@ TILES = H // P
 SLOTS = E * C
 HALF = T // 2
 QUARTER = T // 4
-GATE_ROWS = T // P
+GATE_ROWS = (T - QUARTER) // P
 
 BLOCKS = [256, 256, 256, 128, 128]
 GATHERS = LISTS * TILES
@@ -65,9 +65,9 @@ def tile_moe_sub_silu_kernel(
         w2_sc = keep.tile([P, E * PASSES, H], U8, name="w2_sc", align_bytes=64)
         w2_first = keep.tile([P, PASSES * H], I32, name="w2_first", align_bytes=64)
         y = [keep.tile([P, SLOTS], F32, name="y%d" % j) for j in range(TILES)]
-        a_first = keep.tile([P, TILES, QUARTER], F32, name="buf_d")
+        a_first = keep.tile([P, TILES, QUARTER], F32, name="a_first")
         sigmoid = [keep.tile([P, TILES, QUARTER], F32, name="sigmoid_early")]
-        gate_rows = keep.tile([P, P], F32, name="gate_rows")
+        gate_rows = keep.tile([P, P], F32, name="buf_d")
         gate_neg = keep.tile([P, LISTS * GATE_ROWS], F32, name="gate_neg")
         ident = keep.tile([P, P], F32, name="ident")
         w1_bf = keep.tile([P, K, PACK], BF16, name="w1_bf", align_bytes=64)
@@ -101,7 +101,7 @@ def tile_moe_sub_silu_kernel(
         load_scale_rows(dy_sc, PASSES * SCALE_ROWS, lambda b0, b1: dy_scales[:, b0:b1, :])
         load_scale_rows(w2_sc, SCALE_ROWS, lambda b0, b1: w2_rows[b0:b1, :, :])
         nc.sync.dma_start(out=dy_w[:], in_=dy_words.rearrange("s p t d -> p s (t d)").bitcast(I32))
-        nc.sync.dma_start(out=gate_rows[0 : LISTS * GATE_ROWS, :], in_=gate[:, 0, :].rearrange("r (c t) -> r c t", t=P))
+        nc.sync.dma_start(out=gate_rows[0 : LISTS * GATE_ROWS, :], in_=gate[:, 0, 0 : GATE_ROWS * P].rearrange("r (c t) -> r c t", t=P))
         nc.sync.dma_start(pos_sb[0][:], pos1)
         nc.sync.dma_start(pos_sb[1][:], pos2)
         nc.sync.dma_start(out=a_first[:], in_=a_by_quad[:, :, T - QUARTER : T])
@@ -124,15 +124,24 @@ def tile_moe_sub_silu_kernel(
         gate_t = bank(0)
         nc.tensor.transpose(gate_t[:, 0:P], gate_rows[:], ident[:])
         nc.vector.tensor_scalar(out=gate_neg[:], in0=gate_t[:, 0 : LISTS * GATE_ROWS], scalar1=-1.0, scalar2=None, op0=ALU.mult)
-        silu_last = keep.tile([P, QUARTER, PACK], F32, name="silu_last")
-        sigmoid_last = keep.tile([P, QUARTER, PACK], F32, name="sigmoid_last")
-        less_one = keep.tile([P, QUARTER, PACK], F32, name="less_one")
-        slope_neg = keep.tile([P, QUARTER, PACK], F32, name="slope_neg")
-        lines = a_first[:].rearrange("p d (c i) -> p c d i", i=4)
-        nc.scalar.activation(out=silu_last[:].rearrange("p (c i) d -> p c d i", i=4), in_=lines, func=ACT.Silu, scale=-1.0)
-        nc.scalar.activation(out=sigmoid_last[:].rearrange("p (c i) d -> p c d i", i=4), in_=lines, func=ACT.Sigmoid)
-        nc.gpsimd.tensor_scalar(out=less_one[:], in0=silu_last[:], scalar1=1.0, scalar2=-1.0, op0=ALU.mult, op1=ALU.add)
-        nc.gpsimd.tensor_tensor(slope_neg[:], less_one[:], sigmoid_last[:], ALU.mult)
+        sigmoid_neg = keep.tile([P, PACK, QUARTER], F32, name="sigmoid_neg")
+        sigmoid_pos = keep.tile([P, QUARTER, PACK], F32, name="sigmoid_pos")
+        inner = keep.tile([P, PACK, QUARTER], F32, name="inner")
+        bracket = keep.tile([P, QUARTER, PACK], F32, name="bracket")
+        slope = keep.tile([P, QUARTER, PACK], F32, name="slope")
+        nc.scalar.activation(out=sigmoid_neg[:], in_=a_first[:], func=ACT.Sigmoid, scale=-1.0)
+        nc.scalar.activation(
+            out=sigmoid_pos[:].rearrange("p (c i) d -> p c d i", i=4),
+            in_=a_first[:].rearrange("p d (c i) -> p c d i", i=4),
+            func=ACT.Sigmoid,
+        )
+        nc.gpsimd.tensor_tensor(inner[:], sigmoid_neg[:], a_first[:], ALU.mult)
+        for u in range(2):
+            ts = slice(u * P, (u + 1) * P)
+            nc.gpsimd.tensor_scalar(
+                out=bracket[:, ts, :], in0=inner[:, :, ts].rearrange("p d t -> p t d"), scalar1=1.0, scalar2=1.0, op0=ALU.mult, op1=ALU.add
+            )
+            nc.gpsimd.tensor_tensor(slope[:, ts, :], bracket[:, ts, :], sigmoid_pos[:, ts, :], ALU.mult)
         part = TILES * QUARTER
         late = keep.tile([P, 7 * part + LISTS * QUARTER], F32, name="buf_d")
         w1_raw = late[:, 0:part].rearrange("p (d k) -> p d k", d=PACK)
@@ -248,9 +257,9 @@ def tile_moe_sub_silu_kernel(
                         start=(r == 0 and (j == 0 or alone)), stop=(r == LISTS - 1 and (j == closing or alone)), is_transpose=True,
                     )
                     if r == LISTS - 1 and j == closing:
-                        regroup(summed, main, 0, j + 1, -1.0)
+                        regroup(summed, main, 0, j + 1, 1.0)
                     if r == LISTS - 1 and alone:
-                        regroup(summed, side, j, j + 1, -1.0)
+                        regroup(summed, side, j, j + 1, 1.0)
                     if r == LISTS - 1 and j == TILES - 1:
                         for d in range(PACK):
                             nc.tensor.transpose(sums[b, 0][:, d * P : (d + 1) * P], summed[:, d, :], ident[:])
@@ -277,31 +286,30 @@ def tile_moe_sub_silu_kernel(
         def finish(b, c):
             t0 = starts[b] + c * P
             quarter, u = divmod(t0, QUARTER)
-            if b == last - 1:
-                rounded[b] = keep.tile([P, BLOCKS[b], PACK], BF16, name="picked%d" % ((GATHERS * len(BLOCKS) - 2) % PICKED_BUFS), align_bytes=64)
-            elif c == 0:
-                rounded[b] = results.tile([P, BLOCKS[b], PACK], BF16, name="da_bf", align_bytes=64)
+            if (b, c) == (2, 1):
+                rounded["tail"] = keep.tile([P, QUARTER, PACK], BF16, name="picked%d" % ((GATHERS * len(BLOCKS) - 2) % PICKED_BUFS), align_bytes=64)
+                dst = rounded["tail"][:, 0:P, :]
+            elif b == 3:
+                dst = rounded["tail"][:, P:QUARTER, :]
+            else:
+                if c == 0:
+                    rounded[b] = results.tile([P, P if b == 2 else BLOCKS[b], PACK], BF16, name="da_bf", align_bytes=64)
+                dst = rounded[b][:, c * P : (c + 1) * P, :]
             total = sums[b, c][:].rearrange("p (d t) -> p t d", d=PACK)
             if b >= last - 1:
-                nc.vector.tensor_tensor(rounded[b][:], slope_neg[:, u : u + P, :], total, ALU.mult)
+                nc.vector.tensor_tensor(dst, slope[:, u : u + P, :], total, ALU.mult)
                 return
             if c == 0:
                 silu(quarter)
             nc.vector.scalar_tensor_tensor(
-                out=rounded[b][:, c * P : (c + 1) * P, :],
-                in0=silu_neg[quarter][:, u : u + P, :],
-                scalar=1.0,
-                in1=total,
-                op0=ALU.subtract,
-                op1=ALU.mult,
+                out=dst, in0=silu_neg[quarter][:, u : u + P, :], scalar=1.0, in1=total, op0=ALU.subtract, op1=ALU.mult
             )
 
-        def quantise(b):
-            t0, width = starts[b], BLOCKS[b]
+        def quantise(key, t0, width):
             nc.vector.quantize_mx(
                 out=da_w[:, t0 : t0 + width].bitcast(E5M2),
                 scales=da_sc[:, t0 : t0 + width],
-                in_=rounded[b][:].rearrange("p t d -> p (t d)"),
+                in_=rounded[key][:].rearrange("p t d -> p (t d)"),
             )
 
         out_by_tile = out.rearrange("(m p) t -> p m t", p=P)
@@ -323,23 +331,26 @@ def tile_moe_sub_silu_kernel(
                     nc.vector.tensor_copy(out=res[:, m, :], in_=acc[:, BANK - new : BANK])
                 else:
                     nc.scalar.copy(out=res[:, m, :], in_=acc[:, BANK - new : BANK])
-            nc.sync.dma_start(out=out_by_tile[:, :, end - new : end], in_=res[:])
+                if not both_engines:
+                    nc.sync.dma_start(out=out_by_tile[:, m, end - new : end], in_=res[:, m, :])
+            if both_engines:
+                nc.sync.dma_start(out=out_by_tile[:, :, end - new : end], in_=res[:])
 
         after = {
             GATHERS - 1: [late_sigmoid],
             GATHERS + 5: [lambda: finish(0, 0), lambda: finish(0, 1)],
-            GATHERS + 7: [lambda: quantise(0)],
+            GATHERS + 7: [lambda: quantise(0, 0, QUARTER)],
             2 * GATHERS + 5: [lambda: finish(1, 0), lambda: finish(1, 1)],
-            2 * GATHERS + 7: [lambda: quantise(1), lambda: project(starts[2], starts[2], sum_banks[1], False)],
+            2 * GATHERS + 7: [lambda: quantise(1, QUARTER, QUARTER), lambda: project(starts[2], starts[2], sum_banks[1], False)],
             3 * GATHERS + 7: [lambda: finish(2, 0)],
-            4 * GATHERS + 1: [lambda: finish(2, 1)],
-            4 * GATHERS + 3: [lambda: quantise(2)],
+            4 * GATHERS + 1: [lambda: quantise(2, HALF, P)],
         }
         for b in range(len(BLOCKS)):
             fetch(b, after)
+        finish(2, 1)
         finish(last - 1, 0)
-        quantise(last - 1)
+        quantise("tail", HALF + P, QUARTER)
         project(starts[last], starts[last] - starts[2], [1, sum_banks[last - 1][0]], False)
         finish(last, 0)
-        quantise(last)
+        quantise(last, starts[last], P)
         project(T, BLOCKS[last], [3, sum_banks[2][0]], True)

@@ -22,7 +22,6 @@ PACK = 4
 QUADRANTS = 4
 SCALE_ROWS = 4
 BANK = 512
-BANKS = 8
 LISTS = 2
 PER_COLUMN = 16
 PASSES = N // (P * PACK)
@@ -30,17 +29,15 @@ TILES = H // P
 SLOTS = E * C
 HALF = T // 2
 QUARTER = T // 4
-GATE_ROWS = (T - QUARTER) // P
-
-BLOCKS = [256, 256, 256, 128, 128]
-GATHERS = LISTS * TILES
-DIRECT = 2
 MOVED_PARTITIONS = 112
-SCALE_BUFS = 2
-WORD_BUFS = 8
-COMBINE_BUFS = 8
+BLOCKS = [256, 256, 256, 128, 128]
+STARTS = [512, 0, 256, 768, 896]
+WHOLE = (0, 1)
+GATE_ROWS = len(WHOLE) * QUARTER // P
+GATHERS = LISTS * TILES
 PICKED_BUFS = 8
-RESULT_BUFS = 4
+WIDE = H // 2
+W2_MAIN = (2 * E - 1) * PASSES * WIDE
 
 
 def tile_moe_sub_silu_kernel(
@@ -49,9 +46,9 @@ def tile_moe_sub_silu_kernel(
     nc = tc.nc
     with ExitStack() as ctx:
         keep = ctx.enter_context(tc.tile_pool(name="keep", bufs=1))
-        combine = ctx.enter_context(tc.tile_pool(name="combine", bufs=COMBINE_BUFS))
-        word_ring = ctx.enter_context(tc.tile_pool(name="word_ring", bufs=WORD_BUFS))
-        results = ctx.enter_context(tc.tile_pool(name="results", bufs=RESULT_BUFS))
+        shared = ctx.enter_context(tc.tile_pool(name="shared", bufs=1))
+        results = ctx.enter_context(tc.tile_pool(name="results", bufs=4))
+        combine = ctx.enter_context(tc.tile_pool(name="combine", bufs=8))
         psum = ctx.enter_context(tc.psum_pool(name="psum", bufs=1))
 
         def bank(b):
@@ -59,18 +56,16 @@ def tile_moe_sub_silu_kernel(
 
         offs_sb = keep.tile([P, SLOTS // PER_COLUMN], U16, name="offs_sb")
         pos_sb = [keep.tile([P, T // PER_COLUMN], U16, name="pos_sb%d" % r) for r in range(LISTS)]
-        dy_sc = keep.tile([P, T], U8, name="buf_a", align_bytes=64)
+        dy_sc = shared.tile([P, T], U8, name="dy_sc", align_bytes=64, offset=W2_MAIN * PACK - T // 2)
         slot_sc = [[keep.tile([P, 2 * C], U8, name="slot_sc%d%d" % (g, s), align_bytes=64) for s in range(PASSES)] for g in range(2)]
-        dy_w = keep.tile([P, PASSES, T], I32, name="buf_b", align_bytes=64)
+        dy_w = [keep.tile([P, T], I32, name="dy_w%d" % s, align_bytes=64) for s in range(PASSES)]
         w2_sc = keep.tile([P, E * PASSES, H], U8, name="w2_sc", align_bytes=64)
-        w2_first = keep.tile([P, PASSES * H], I32, name="w2_first", align_bytes=64)
+        w2_first = keep.tile([P, PASSES * WIDE], I32, name="w2_first", align_bytes=64)
         y = [keep.tile([P, SLOTS], F32, name="y%d" % j) for j in range(TILES)]
-        a_first = keep.tile([P, TILES, QUARTER], F32, name="a_first")
-        sigmoid = [keep.tile([P, TILES, QUARTER], F32, name="sigmoid_early")]
-        gate_rows = keep.tile([P, P], F32, name="buf_d")
-        gate_neg = keep.tile([P, LISTS * GATE_ROWS], F32, name="gate_neg")
+        a_sb = [keep.tile([P, TILES, QUARTER], F32, name="a%d" % n)[:] for n in range(3)]
+        gate_rows = keep.tile([P, P], F32, name="gate_rows")
+        gate_col = keep.tile([P, LISTS * GATE_ROWS], F32, name="gate_col")
         ident = keep.tile([P, P], F32, name="ident")
-        w1_bf = keep.tile([P, K, PACK], BF16, name="w1_bf", align_bytes=64)
         w1_w = keep.tile([P, K], U32, name="w1_w", align_bytes=64)
         w1_sc = keep.tile([P, K], U8, name="w1_sc", align_bytes=64)
         da_w = keep.tile([P, T], U32, name="da_w", align_bytes=64)
@@ -79,12 +74,6 @@ def tile_moe_sub_silu_kernel(
         nc.gpsimd.memset(dy_sc[:].bitcast(I32), 0)
         nc.gpsimd.memset(gate_rows[:], 0.0)
         make_identity(nc, ident[:])
-
-        def load_w2(words, e0, e1):
-            nc.sync.dma_start(
-                out=words.rearrange("p (g i) -> p g i", i=H),
-                in_=w2t_words[e0:e1].rearrange("e s p i d -> p (e s) (i d)").bitcast(I32),
-            )
 
         def load_scale_rows(tile, rows_a_quadrant, source):
             for q in range(QUADRANTS):
@@ -96,16 +85,28 @@ def tile_moe_sub_silu_kernel(
         a_by_tile = a.rearrange("(j p) t -> p j t", p=P)
         a_by_quad = a.rearrange("(p d) t -> p d t", d=PACK)
         w2_rows = w2t_scales.rearrange("e s b i -> b (e s) i")
+        w2_by_pass = w2t_words.rearrange("e s p i d -> p (e s) (i d)").bitcast(I32)
+
+        def load_a(n):
+            nc.sync.dma_start(out=a_sb[n], in_=(a_by_tile if n in WHOLE else a_by_quad)[:, :, QUARTER * n : QUARTER * (n + 1)])
+
+        def load_dy(s):
+            nc.sync.dma_start(out=dy_w[s][:], in_=dy_words[s].rearrange("p t d -> p (t d)").bitcast(I32))
 
         nc.sync.dma_start(offs_sb[:], offs)
         load_scale_rows(dy_sc, PASSES * SCALE_ROWS, lambda b0, b1: dy_scales[:, b0:b1, :])
-        load_scale_rows(w2_sc, SCALE_ROWS, lambda b0, b1: w2_rows[b0:b1, :, :])
-        nc.sync.dma_start(out=dy_w[:], in_=dy_words.rearrange("s p t d -> p s (t d)").bitcast(I32))
-        nc.sync.dma_start(out=gate_rows[0 : LISTS * GATE_ROWS, :], in_=gate[:, 0, 0 : GATE_ROWS * P].rearrange("r (c t) -> r c t", t=P))
         nc.sync.dma_start(pos_sb[0][:], pos1)
         nc.sync.dma_start(pos_sb[1][:], pos2)
-        nc.sync.dma_start(out=a_first[:], in_=a_by_quad[:, :, T - QUARTER : T])
-        load_w2(w2_first[:], 0, 1)
+        load_a(0)
+        load_dy(0)
+        load_a(1)
+        load_dy(1)
+        nc.sync.dma_start(
+            out=gate_rows[0 : LISTS * GATE_ROWS, :], in_=gate[:, 0, 0:HALF].rearrange("r (c t) -> r c t", t=P)
+        )
+        load_a(2)
+        nc.sync.dma_start(out=w2_first[:].rearrange("p (s i) -> p s i", s=PASSES), in_=w2_by_pass[:, 0:PASSES, 0:WIDE])
+        load_scale_rows(w2_sc, SCALE_ROWS, lambda b0, b1: w2_rows[b0:b1, :, :])
 
         def expert_offs(e):
             return offs_sb[:, e * C // PER_COLUMN : (e + 1) * C // PER_COLUMN]
@@ -117,200 +118,181 @@ def tile_moe_sub_silu_kernel(
                 out=slot_sc[g][1][0:MOVED_PARTITIONS, :].bitcast(I32),
                 in_=slot_sc[g][0][SCALE_ROWS : SCALE_ROWS + MOVED_PARTITIONS, :].bitcast(I32),
             )
-        w2_rest = keep.tile([P, (E - 1) * PASSES * H], I32, name="buf_a", align_bytes=64)
-        load_w2(w2_rest[:, 0 : PASSES * H], 1, 2)
-        load_w2(w2_rest[:, PASSES * H :], 2, E)
+        w2_main = shared.tile([P, W2_MAIN], I32, name="w2_main", align_bytes=64, offset=0)
+        late = shared.tile([P, PACK * K + 2 * T], F32, name="late", align_bytes=64, offset=W2_MAIN * PACK)
+        w1_raw = late[:, 0 : PACK * K].rearrange("p (d k) -> p d k", d=PACK)
+        a_sb.append(late[:, PACK * K : PACK * K + T].rearrange("p (d t) -> p d t", d=PACK))
+        gate_wide = late[:, PACK * K + T :].rearrange("p (r t) -> p r t", r=LISTS)
+        gate_by_row = gate.rearrange("r p t -> p r t")
+        early = (E - 1) * PASSES * WIDE
+        nc.sync.dma_start(out=w2_main[:, 0:early].rearrange("p (g i) -> p g i", i=WIDE), in_=w2_by_pass[:, PASSES:, 0:WIDE])
+        nc.sync.dma_start(out=w1_raw, in_=w1t.rearrange("(p d) k -> p d k", d=PACK))
+        nc.sync.dma_start(out=gate_wide, in_=gate_by_row[:, :, HALF:T])
+        nc.sync.dma_start(out=w2_main[:, early:].rearrange("p (g i) -> p g i", i=WIDE), in_=w2_by_pass[:, :, WIDE:H])
+        load_a(3)
+
+        def weights(e, s, j):
+            if e == 0 and j < 2:
+                return w2_first[:, s * WIDE + j * P : s * WIDE + (j + 1) * P]
+            first = ((E * (j // 2) + e - 1) * PASSES + s) * WIDE + j % 2 * P
+            return w2_main[:, first : first + P]
+
+        slope = {n: keep.tile([P, QUARTER * PACK], F32, name="slope%d" % n) for n in range(3)}
+        right = {n: keep.tile([P, QUARTER * PACK], F32, name="right%d" % n) for n in range(3)}
+        left = {n: keep.tile([P, QUARTER * PACK], F32, name="left%d" % n) for n in range(3)}
+
+        def activate(n):
+            if n in WHOLE:
+                src, pattern = a_sb[n].rearrange("p j (c i) -> p j c i", i=4), "p (d c i) -> p d c i"
+            else:
+                src, pattern = a_sb[n].rearrange("p d (c i) -> p c d i", i=4), "p (c i d) -> p c d i"
+            nc.scalar.activation(out=right[n][:].rearrange(pattern, i=4, d=PACK), in_=src, func=ACT.Silu, scale=-1.0)
+            nc.scalar.activation(out=left[n][:].rearrange(pattern, i=4, d=PACK), in_=src, func=ACT.Tanh, scale=0.5)
 
         gate_t = bank(0)
-        nc.tensor.transpose(gate_t[:, 0:P], gate_rows[:], ident[:])
-        nc.vector.tensor_scalar(out=gate_neg[:], in0=gate_t[:, 0 : LISTS * GATE_ROWS], scalar1=-1.0, scalar2=None, op0=ALU.mult)
-        sigmoid_neg = keep.tile([P, PACK, QUARTER], F32, name="sigmoid_neg")
-        sigmoid_pos = keep.tile([P, QUARTER, PACK], F32, name="sigmoid_pos")
-        inner = keep.tile([P, PACK, QUARTER], F32, name="inner")
-        bracket = keep.tile([P, QUARTER, PACK], F32, name="bracket")
-        slope = keep.tile([P, QUARTER, PACK], F32, name="slope")
-        nc.scalar.activation(out=sigmoid_neg[:], in_=a_first[:], func=ACT.Sigmoid, scale=-1.0)
-        nc.scalar.activation(
-            out=sigmoid_pos[:].rearrange("p (c i) d -> p c d i", i=4),
-            in_=a_first[:].rearrange("p d (c i) -> p c d i", i=4),
-            func=ACT.Sigmoid,
-        )
-        nc.gpsimd.tensor_tensor(inner[:], sigmoid_neg[:], a_first[:], ALU.mult)
-        for u in range(2):
-            ts = slice(u * P, (u + 1) * P)
-            nc.gpsimd.tensor_scalar(
-                out=bracket[:, ts, :], in0=inner[:, :, ts].rearrange("p d t -> p t d"), scalar1=1.0, scalar2=1.0, op0=ALU.mult, op1=ALU.add
-            )
-            nc.gpsimd.tensor_tensor(slope[:, ts, :], bracket[:, ts, :], sigmoid_pos[:, ts, :], ALU.mult)
-        part = TILES * QUARTER
-        late = keep.tile([P, 7 * part + LISTS * QUARTER], F32, name="buf_d")
-        w1_raw = late[:, 0:part].rearrange("p (d k) -> p d k", d=PACK)
-        a_tile = [late[:, (1 + n) * part : (2 + n) * part].rearrange("p (j t) -> p j t", j=TILES) for n in range(3)]
-        a_quad = [late[:, (4 + n) * part : (5 + n) * part].rearrange("p (d t) -> p d t", d=PACK) for n in range(3)]
-        gate_wide = late[:, 7 * part :].rearrange("p (r t) -> p r t", r=LISTS)
-        nc.sync.dma_start(out=a_tile[0], in_=a_by_tile[:, :, 0:QUARTER])
-        nc.sync.dma_start(out=w1_raw, in_=w1t.rearrange("(p d) k -> p d k", d=PACK))
-        for n in (1, 2):
-            nc.sync.dma_start(out=a_tile[n], in_=a_by_tile[:, :, QUARTER * n : QUARTER * (n + 1)])
-        for n in range(3):
-            nc.sync.dma_start(out=a_quad[n], in_=a_by_quad[:, :, QUARTER * n : QUARTER * (n + 1)])
-        nc.sync.dma_start(out=gate_wide, in_=gate[:, :, T - QUARTER : T].rearrange("r p t -> p r t"))
+        for n in WHOLE + (2,):
+            activate(n)
+            nc.gpsimd.tensor_scalar(out=right[n][:], in0=right[n][:], scalar1=-0.5, scalar2=0.5, op0=ALU.mult, op1=ALU.add)
+            if n in WHOLE:
+                nc.scalar.activation(out=left[n][:], in_=left[n][:], func=ACT.Identity, bias=1.0)
+                nc.gpsimd.tensor_tensor(slope[n][:], left[n][:], right[n][:], ALU.mult)
+            if n == WHOLE[-1]:
+                nc.tensor.transpose(gate_t[:, 0:P], gate_rows[:], ident[:])
+                nc.scalar.copy(out=gate_col[:], in_=gate_t[:, 0 : LISTS * GATE_ROWS])
+
+        def product_of_halves(n):
+            nc.vector.scalar_tensor_tensor(out=slope[n][:], in0=left[n][:], scalar=1.0, in1=right[n][:], op0=ALU.add, op1=ALU.mult)
 
         slot_w = {}
 
-        def product(e, j, b):
-            g, u = divmod(e, 2)
-            weights = w2_first if e == 0 else w2_rest[:, (e - 1) * PASSES * H : e * PASSES * H]
-            acc = bank(b)
+        def product(e, j):
+            acc = bank(E * (j % 2) + e)
             for s in range(PASSES):
                 nc.tensor.matmul_mx(
                     out=acc[:],
-                    lhsT=weights[:, s * H + j * P : s * H + (j + 1) * P].bitcast(E4M3),
+                    lhsT=weights(e, s, j).bitcast(E4M3),
                     lhsT_scale=w2_sc[:, e * PASSES + s, j * P : (j + 1) * P],
                     rhs=slot_w[e, s][:].bitcast(E5M2),
-                    rhs_scale=slot_sc[g][s][:, u * C : (u + 1) * C],
+                    rhs_scale=slot_sc[e // 2][s][:, e % 2 * C : (e % 2 + 1) * C],
                     start=(s == 0),
                     stop=(s == PASSES - 1),
                 )
-            if (e, j) == (E - 1, 1):
-                nc.vector.tensor_copy(out=y[j][:, e * C : (e + 1) * C], in_=acc[:])
-            else:
-                nc.scalar.copy(out=y[j][:, e * C : (e + 1) * C], in_=acc[:])
+            nc.scalar.copy(out=y[j][:, e * C : (e + 1) * C], in_=acc[:])
 
         for e in range(E):
             for s in range(PASSES):
-                slot_w[e, s] = word_ring.tile([P, C], U32, name="slot_w", align_bytes=64)
-                nc.vector.tensor_copy(slot_w[e, s][:], dy_w[:, s, :].bitcast(U32).indirect(expert_offs(e)))
-            if e == E - 1:
-                nc.vector.tensor_copy(out=w1_bf[:], in_=w1_raw.rearrange("p d k -> p k d"))
-                nc.vector.quantize_mx(out=w1_w[:].bitcast(E4M3), scales=w1_sc[:], in_=w1_bf[:].rearrange("p k d -> p (k d)"))
-            for j in range(TILES - 1):
-                product(e, j, TILES + j)
-            if e == 1:
-                nc.scalar.activation(out=sigmoid[0][:], in_=a_tile[0], func=ACT.Sigmoid)
-        for e in range(E):
-            product(e, TILES - 1, TILES + e % (TILES - 1))
+                slot_w[e, s] = keep.tile([P, C], U32, name="slot_w%d%d" % (e, s), align_bytes=64)
+                nc.vector.tensor_copy(slot_w[e, s][:], dy_w[s][:].bitcast(U32).indirect(expert_offs(e)))
+            product(e, 0)
+            product(e, 1)
+        w1_bf = keep.tile([P, K, PACK], BF16, name="dy_w1", align_bytes=64)
+        nc.vector.tensor_copy(out=w1_bf[:], in_=w1_raw.rearrange("p d k -> p k d"))
+        product_of_halves(2)
+        nc.vector.quantize_mx(out=w1_w[:].bitcast(E4M3), scales=w1_sc[:], in_=w1_bf[:].rearrange("p k d -> p (k d)"))
+        for j in range(2, TILES):
+            for e in range(E):
+                product(e, j)
 
-        later = keep.tile([P, 2 * part], F32, name="buf_a", align_bytes=64)
-        sigmoid.extend([later[:, n * part : (n + 1) * part].rearrange("p (j t) -> p j t", j=TILES) for n in range(2)])
-        nc.scalar.activation(out=sigmoid[1], in_=a_tile[1], func=ACT.Sigmoid)
+        right.update({3: keep.tile([P, QUARTER * PACK], F32, name="slot_w31", align_bytes=64)})
+        left.update({3: keep.tile([P, QUARTER * PACK], F32, name="slot_sc11", align_bytes=64)})
 
-        def by_lines(tile, quarter):
-            return tile.rearrange("p (c i) d -> p c d i", i=4), a_quad[quarter].rearrange("p d (c i) -> p c d i", i=4)
-
-        def late_sigmoid():
-            nc.scalar.activation(out=sigmoid[2], in_=a_tile[2], func=ACT.Sigmoid)
-
-        starts = [sum(BLOCKS[:b]) for b in range(len(BLOCKS))]
+        starts = STARTS
         last = len(BLOCKS) - 1
-        turn_banks = [[[0, 1], [2, 3]]] * 3 + [[[0], [1]], [[2], [3]]]
-        sum_banks = [[4, 5], [6, 7], [4, 5], [6], [7]]
+        turn_banks = [[[0, 1]], [[2, 3], [4, 5]], [[6, 7], [4, 5]], [[2]], [[3]]]
+        SIDE = 4
+        turned = {}
         sums = {}
         rounded = {}
-        silu_neg = {}
 
-        def fetch(b, after):
-            t0, width = starts[b], BLOCKS[b]
-            subs = width // P
-            narrow = b >= last - 1
-            for c in range(subs):
-                sums[b, c] = bank(sum_banks[b][c])
-            turned = {}
-            gated = {}
-            if b == 0:
-                order = [(r, j) for j in range(TILES) for r in range(LISTS)]
-            else:
-                order = [(r, j) for r in range(LISTS) for j in range(TILES)]
-
-            def regroup(dst, source, j0, j1, scale):
-                nc.scalar.activation(
-                    out=dst[:, :, 32 * j0 : 32 * j1],
-                    in_=source[:, j0 * P : j1 * P].rearrange("t (p d) -> t d p", d=PACK),
-                    func=ACT.Copy,
-                    scale=scale,
-                )
-
-            if narrow:
-                main = bank(0 if b < last else 2)
-                side = bank(1) if b == last else main
-                summed = combine.tile([P, PACK, P], F32, name="gated")
-            for n, (r, j) in enumerate(order):
-                if j == 0 and not narrow:
-                    turned[r] = [bank(turn_banks[b][r][c]) for c in range(subs)]
-                    gated[r] = [combine.tile([P, PACK, P], F32, name="gated") for c in range(subs)]
-                picked = keep.tile([P, width], F32, name="picked%d" % ((GATHERS * b + n) % PICKED_BUFS), align_bytes=64)
-                if narrow:
-                    factor = gate_wide[:, r, t0 - (T - QUARTER) : t0 - (T - QUARTER) + width]
-                else:
-                    factor = sigmoid[b][:, j, :]
-                nc.vector.tensor_tensor(
-                    picked[:],
-                    y[j][:].indirect(pos_sb[r][:, t0 // PER_COLUMN : (t0 + width) // PER_COLUMN]),
-                    factor,
-                    ALU.mult,
-                )
-                if narrow:
-                    alone = b == last and j == TILES - 1
-                    closing = TILES - 2 if b == last else TILES - 1
-                    nc.tensor.matmul(
-                        (side if alone else main)[:, j * P : (j + 1) * P], picked[:], ident[:],
-                        start=(r == 0 and (j == 0 or alone)), stop=(r == LISTS - 1 and (j == closing or alone)), is_transpose=True,
-                    )
-                    if r == LISTS - 1 and j == closing:
-                        regroup(summed, main, 0, j + 1, 1.0)
-                    if r == LISTS - 1 and alone:
-                        regroup(summed, side, j, j + 1, 1.0)
-                    if r == LISTS - 1 and j == TILES - 1:
-                        for d in range(PACK):
-                            nc.tensor.transpose(sums[b, 0][:, d * P : (d + 1) * P], summed[:, d, :], ident[:])
-                else:
-                    for c in range(subs):
-                        nc.tensor.transpose(turned[r][c][:, j * P : (j + 1) * P], picked[:, c * P : (c + 1) * P], ident[:])
-                    if j == TILES - 1:
-                        for c in range(subs):
-                            col = GATE_ROWS * r + t0 // P + c
-                            regroup(gated[r][c], turned[r][c], 0, TILES, gate_neg[:, col : col + 1])
-                            for d in range(PACK):
-                                nc.tensor.matmul(
-                                    sums[b, c][:, d * P : (d + 1) * P], gated[r][c][:, d, :], ident[:],
-                                    start=(r == 0 and d == 0), stop=(r == LISTS - 1 and d == PACK - 1), is_transpose=True,
-                                )
-                for step in after.get(GATHERS * b + n, []):
-                    step()
-
-        def silu(quarter):
-            silu_neg[quarter] = keep.tile([P, QUARTER, PACK], F32, name="slot_sc1%d" % (1 - quarter % 2), align_bytes=64)
-            dst, src = by_lines(silu_neg[quarter][:], quarter)
-            nc.scalar.activation(out=dst, in_=src, func=ACT.Silu, scale=-1.0)
-
-        def finish(b, c):
-            t0 = starts[b] + c * P
-            quarter, u = divmod(t0, QUARTER)
-            if (b, c) == (2, 1):
-                rounded["tail"] = keep.tile([P, QUARTER, PACK], BF16, name="picked%d" % ((GATHERS * len(BLOCKS) - 2) % PICKED_BUFS), align_bytes=64)
-                dst = rounded["tail"][:, 0:P, :]
-            elif b == 3:
-                dst = rounded["tail"][:, P:QUARTER, :]
-            else:
-                if c == 0:
-                    rounded[b] = results.tile([P, P if b == 2 else BLOCKS[b], PACK], BF16, name="da_bf", align_bytes=64)
-                dst = rounded[b][:, c * P : (c + 1) * P, :]
-            total = sums[b, c][:].rearrange("p (d t) -> p t d", d=PACK)
-            if b >= last - 1:
-                nc.vector.tensor_tensor(dst, slope[:, u : u + P, :], total, ALU.mult)
-                return
-            if c == 0:
-                silu(quarter)
-            nc.vector.scalar_tensor_tensor(
-                out=dst, in0=silu_neg[quarter][:, u : u + P, :], scalar=1.0, in1=total, op0=ALU.subtract, op1=ALU.mult
+        def regroup(dst, source, j0, j1, scale):
+            nc.scalar.activation(
+                out=dst[:, :, 32 * j0 : 32 * j1],
+                in_=source[:, j0 * P : j1 * P].rearrange("t (p d) -> t d p", d=PACK),
+                func=ACT.Copy,
+                scale=scale,
             )
 
-        def quantise(key, t0, width):
+        def fetch(n, b, r, j):
+            t0, width = starts[b], BLOCKS[b]
+            subs = range(width // P)
+            quarter = t0 // QUARTER
+            whole = quarter in WHOLE
+            picked = keep.tile([P, width], F32, name="picked%d" % (n % PICKED_BUFS), align_bytes=64)
+            nc.vector.tensor_tensor(
+                picked[:],
+                y[j][:].indirect(pos_sb[r][:, t0 // PER_COLUMN : (t0 + width) // PER_COLUMN]),
+                slope[quarter][:, j * width : (j + 1) * width] if whole else gate_wide[:, r, t0 - HALF : t0 - HALF + width],
+                ALU.mult,
+            )
+            alone = b == last and j == TILES - 1
+            if whole:
+                for c in subs:
+                    if j == 0:
+                        turned.update({(b, r, c): bank(turn_banks[b][r][c])})
+                    nc.tensor.transpose(turned[b, r, c][:, j * P : (j + 1) * P], picked[:, c * P : (c + 1) * P], ident[:])
+                if j == TILES - 1:
+                    if r == LISTS - 1:
+                        rounded.update({b: results.tile([P, width, PACK], BF16, name="da_bf", align_bytes=64)})
+                    for c in subs:
+                        col = GATE_ROWS * r + t0 // P + c
+                        gated = combine.tile([P, PACK, P], F32, name="gated")
+                        regroup(gated, turned[b, r, c], 0, TILES, gate_col[:, col : col + 1])
+                        if r == 0:
+                            sums.update({(b, c): bank(turn_banks[b][0][c])})
+                        for d in range(PACK):
+                            nc.tensor.matmul(
+                                sums[b, c][:, d * P : (d + 1) * P], gated[:, d, :], ident[:],
+                                start=(r == 0 and d == 0), stop=(r == LISTS - 1 and d == PACK - 1), is_transpose=True,
+                            )
+                    if r == LISTS - 1:
+                        for c in subs:
+                            nc.scalar.copy(
+                                out=rounded[b][:, c * P : (c + 1) * P, :], in_=sums[b, c][:].rearrange("p (d t) -> p t d", d=PACK)
+                            )
+                return
+            closing = TILES - 2 if b == last else TILES - 1
+            for c in subs:
+                if r == 0 and (j == 0 or alone):
+                    turned.update({(b, alone, c): bank(SIDE if alone else turn_banks[b][0][c])})
+                nc.tensor.matmul(
+                    turned[b, alone, c][:, j * P : (j + 1) * P], picked[:, c * P : (c + 1) * P], ident[:],
+                    start=(r == 0 and (j == 0 or alone)), stop=(r == LISTS - 1 and (j == closing or alone)), is_transpose=True,
+                )
+            if r == 0:
+                return
+            for c in subs:
+                if j == closing:
+                    sums.update({("summed", b, c): combine.tile([P, PACK, P], F32, name="gated")})
+                    regroup(sums["summed", b, c], turned[b, False, c], 0, j + 1, 1.0)
+                if alone:
+                    regroup(sums["summed", b, c], turned[b, True, c], j, j + 1, 1.0)
+                if j == TILES - 1:
+                    sums.update({(b, c): bank(turn_banks[b][0][c])})
+                    for d in range(PACK):
+                        nc.tensor.transpose(sums[b, c][:, d * P : (d + 1) * P], sums["summed", b, c][:, d, :], ident[:])
+
+        def finish(b, c):
+            quarter, u = divmod(starts[b] + c * P, QUARTER)
+            if c == 0:
+                rounded.update({b: keep.tile([P, BLOCKS[b], PACK], BF16, name="picked%d" % ((len(order) - 2) % PICKED_BUFS), align_bytes=64)})
+            nc.vector.tensor_tensor(
+                rounded[b][:, c * P : (c + 1) * P, :],
+                slope[quarter][:, u * PACK : (u + P) * PACK].rearrange("p (t d) -> p t d", d=PACK),
+                sums[b, c][:].rearrange("p (d t) -> p t d", d=PACK),
+                ALU.mult,
+            )
+
+        def quantise(b):
+            t0, width = starts[b], BLOCKS[b]
             nc.vector.quantize_mx(
                 out=da_w[:, t0 : t0 + width].bitcast(E5M2),
                 scales=da_sc[:, t0 : t0 + width],
-                in_=rounded[key][:].rearrange("p t d -> p (t d)"),
+                in_=rounded[b][:].rearrange("p t d -> p (t d)"),
             )
+
+        def last_quarter():
+            activate(3)
+            nc.scalar.activation(out=right[3][:], in_=right[3][:], func=ACT.Identity, scale=-0.5, bias=0.5)
 
         out_by_tile = out.rearrange("(m p) t -> p m t", p=P)
 
@@ -331,26 +313,41 @@ def tile_moe_sub_silu_kernel(
                     nc.vector.tensor_copy(out=res[:, m, :], in_=acc[:, BANK - new : BANK])
                 else:
                     nc.scalar.copy(out=res[:, m, :], in_=acc[:, BANK - new : BANK])
-                if not both_engines:
-                    nc.sync.dma_start(out=out_by_tile[:, m, end - new : end], in_=res[:, m, :])
-            if both_engines:
-                nc.sync.dma_start(out=out_by_tile[:, :, end - new : end], in_=res[:])
+                nc.sync.dma_start(out=out_by_tile[:, m, end - new : end], in_=res[:, m, :])
 
+        order = [(b, r, j) for j in range(TILES) for b in range(2) for r in range(LISTS)]
+        order.extend([(2, r, j) for r in range(LISTS) for j in range(TILES)])
+        order.extend([(b, r, j) for b in (3, 4) for j in range(TILES) for r in range(LISTS)])
         after = {
-            GATHERS - 1: [late_sigmoid],
-            GATHERS + 5: [lambda: finish(0, 0), lambda: finish(0, 1)],
-            GATHERS + 7: [lambda: quantise(0, 0, QUARTER)],
-            2 * GATHERS + 5: [lambda: finish(1, 0), lambda: finish(1, 1)],
-            2 * GATHERS + 7: [lambda: quantise(1, QUARTER, QUARTER), lambda: project(starts[2], starts[2], sum_banks[1], False)],
-            3 * GATHERS + 7: [lambda: finish(2, 0)],
-            4 * GATHERS + 1: [lambda: quantise(2, HALF, P)],
+            GATHERS: [last_quarter],
+            3 * GATHERS + 1: [lambda: quantise(1)],
+            4 * GATHERS + 3: [lambda: quantise(2), lambda: project(HALF, HALF, [6, 7], False)],
         }
-        for b in range(len(BLOCKS)):
-            fetch(b, after)
-        finish(2, 1)
-        finish(last - 1, 0)
-        quantise("tail", HALF + P, QUARTER)
-        project(starts[last], starts[last] - starts[2], [1, sum_banks[last - 1][0]], False)
-        finish(last, 0)
-        quantise(last, starts[last], P)
-        project(T, BLOCKS[last], [3, sum_banks[2][0]], True)
+        for n, (b, r, j) in enumerate(order):
+            fetch(n, b, r, j)
+            for step in after.get(n, []):
+                step()
+        finish(0, 0)
+        finish(0, 1)
+        quantise(0)
+        project(T - QUARTER, QUARTER, [0, 1], False)
+        slope.update({3: keep.tile([P, QUARTER * PACK], F32, name="picked%d" % ((len(order) - 3) % PICKED_BUFS), align_bytes=64)})
+        rounded.update({"tail": results.tile([P, QUARTER, PACK], BF16, name="da_bf", align_bytes=64)})
+        for c, b in enumerate((last - 1, last)):
+            cols = slice(c * BANK, (c + 1) * BANK)
+            nc.vector.scalar_tensor_tensor(
+                out=slope[3][:, cols], in0=left[3][:, cols], scalar=1.0, in1=right[3][:, cols], op0=ALU.add, op1=ALU.mult
+            )
+        for c, b in enumerate((last - 1, last)):
+            nc.vector.tensor_tensor(
+                rounded["tail"][:, c * P : (c + 1) * P, :],
+                slope[3][:, c * BANK : (c + 1) * BANK].rearrange("p (t d) -> p t d", d=PACK),
+                sums[b, 0][:].rearrange("p (d t) -> p t d", d=PACK),
+                ALU.mult,
+            )
+        nc.vector.quantize_mx(
+            out=da_w[:, T - QUARTER : T].bitcast(E5M2),
+            scales=da_sc[:, T - QUARTER : T],
+            in_=rounded["tail"][:].rearrange("p t d -> p (t d)"),
+        )
+        project(T, QUARTER, [5, 6], True)

@@ -186,7 +186,9 @@ def tile_moe_sub_silu_kernel(
             product(e, 0)
             product(e, 1)
         w1_bf = keep.tile([P, K, PACK], BF16, name="dy_w1", align_bytes=64)
-        nc.vector.tensor_copy(out=w1_bf[:], in_=w1_raw.rearrange("p d k -> p k d"))
+        nc.vector.tensor_copy(
+            out=w1_bf[:].rearrange("p (c i) d -> p c d i", i=4), in_=w1_raw.rearrange("p d (c i) -> p c d i", i=4)
+        )
         product_of_halves(2)
         nc.vector.quantize_mx(out=w1_w[:].bitcast(E4M3), scales=w1_sc[:], in_=w1_bf[:].rearrange("p k d -> p (k d)"))
         for j in range(2, TILES):
@@ -258,9 +260,13 @@ def tile_moe_sub_silu_kernel(
                     turned[b, alone, c][:, j * P : (j + 1) * P], picked[:, c * P : (c + 1) * P], ident[:],
                     start=(r == 0 and (j == 0 or alone)), stop=(r == LISTS - 1 and (j == closing or alone)), is_transpose=True,
                 )
-            if r == 0:
-                return
-            for c in subs:
+            if r == LISTS - 1:
+                turn_back(b, j)
+
+        def turn_back(b, j):
+            alone = b == last and j == TILES - 1
+            closing = TILES - 2 if b == last else TILES - 1
+            for c in range(BLOCKS[b] // P):
                 if j == closing:
                     sums.update({("summed", b, c): combine.tile([P, PACK, P], F32, name="gated")})
                     regroup(sums["summed", b, c], turned[b, False, c], 0, j + 1, 1.0)
@@ -315,12 +321,12 @@ def tile_moe_sub_silu_kernel(
                     nc.scalar.copy(out=res[:, m, :], in_=acc[:, BANK - new : BANK])
                 nc.sync.dma_start(out=out_by_tile[:, m, end - new : end], in_=res[:, m, :])
 
-        order = [(b, r, j) for j in range(TILES) for b in range(2) for r in range(LISTS)]
+        order = [(b, r, j) for j in range(TILES) for b in (1, 0) for r in range(LISTS)]
         order.extend([(2, r, j) for r in range(LISTS) for j in range(TILES)])
         order.extend([(b, r, j) for b in (3, 4) for j in range(TILES) for r in range(LISTS)])
         after = {
             GATHERS: [last_quarter],
-            3 * GATHERS + 1: [lambda: quantise(1)],
+            2 * GATHERS + 5: [lambda: quantise(1)],
             4 * GATHERS + 3: [lambda: quantise(2), lambda: project(HALF, HALF, [6, 7], False)],
         }
         for n, (b, r, j) in enumerate(order):

@@ -95,8 +95,6 @@ def tile_moe_sub_silu_kernel(
 
         nc.sync.dma_start(offs_sb[:], offs)
         load_scale_rows(dy_sc, PASSES * SCALE_ROWS, lambda b0, b1: dy_scales[:, b0:b1, :])
-        nc.sync.dma_start(pos_sb[0][:], pos1)
-        nc.sync.dma_start(pos_sb[1][:], pos2)
         load_a(0)
         load_dy(0)
         load_a(1)
@@ -107,6 +105,8 @@ def tile_moe_sub_silu_kernel(
         load_a(2)
         nc.sync.dma_start(out=w2_first[:].rearrange("p (s i) -> p s i", s=PASSES), in_=w2_by_pass[:, 0:PASSES, 0:WIDE])
         load_scale_rows(w2_sc, SCALE_ROWS, lambda b0, b1: w2_rows[b0:b1, :, :])
+        nc.sync.dma_start(pos_sb[0][:], pos1)
+        nc.sync.dma_start(pos_sb[1][:], pos2)
 
         def expert_offs(e):
             return offs_sb[:, e * C // PER_COLUMN : (e + 1) * C // PER_COLUMN]
@@ -156,12 +156,17 @@ def tile_moe_sub_silu_kernel(
             if n in WHOLE:
                 nc.scalar.activation(out=left[n][:], in_=left[n][:], func=ACT.Identity, bias=1.0)
                 nc.gpsimd.tensor_tensor(slope[n][:], left[n][:], right[n][:], ALU.mult)
+            else:
+                nc.scalar.activation(out=left[n][:, 0:BANK], in_=left[n][:, 0:BANK], func=ACT.Identity, bias=1.0)
+                nc.gpsimd.tensor_tensor(slope[n][:, 0:BANK], left[n][:, 0:BANK], right[n][:, 0:BANK], ALU.mult)
             if n == WHOLE[-1]:
                 nc.tensor.transpose(gate_t[:, 0:P], gate_rows[:], ident[:])
                 nc.scalar.copy(out=gate_col[:], in_=gate_t[:, 0 : LISTS * GATE_ROWS])
 
         def product_of_halves(n):
-            nc.vector.scalar_tensor_tensor(out=slope[n][:], in0=left[n][:], scalar=1.0, in1=right[n][:], op0=ALU.add, op1=ALU.mult)
+            nc.vector.scalar_tensor_tensor(
+                out=slope[n][:, BANK:], in0=left[n][:, BANK:], scalar=1.0, in1=right[n][:, BANK:], op0=ALU.add, op1=ALU.mult
+            )
 
         slot_w = {}
 

@@ -22,22 +22,22 @@ PACK = 4
 QUADRANTS = 4
 SCALE_ROWS = 4
 BANK = 512
+BANKS = 8
 LISTS = 2
 PER_COLUMN = 16
 PASSES = N // (P * PACK)
 TILES = H // P
 SLOTS = E * C
-HALF = T // 2
 QUARTER = T // 4
 MOVED_PARTITIONS = 112
-BLOCKS = [256, 256, 256, 128, 128]
-STARTS = [512, 0, 256, 768, 896]
-WHOLE = (0, 1)
-GATE_ROWS = len(WHOLE) * QUARTER // P
-GATHERS = LISTS * TILES
-PICKED_BUFS = 8
-WIDE = H // 2
-W2_MAIN = (2 * E - 1) * PASSES * WIDE
+FIRST = (0, 1, 2)
+SECOND = (5, 6)
+PLAIN = (3, 4, 7)
+BLOCK_BANK = {0: 0, 1: 1, 2: 2, 3: 3, 4: 4, 7: 5, 5: 6, 6: 7}
+VECTOR_RING = 4
+SCALAR_RING = 8
+WHOLE_ON_GPSIMD = 2
+W2_EXPERT = PASSES * H
 
 
 def tile_moe_sub_silu_kernel(
@@ -47,24 +47,23 @@ def tile_moe_sub_silu_kernel(
     with ExitStack() as ctx:
         keep = ctx.enter_context(tc.tile_pool(name="keep", bufs=1))
         shared = ctx.enter_context(tc.tile_pool(name="shared", bufs=1))
-        results = ctx.enter_context(tc.tile_pool(name="results", bufs=4))
-        combine = ctx.enter_context(tc.tile_pool(name="combine", bufs=8))
         psum = ctx.enter_context(tc.psum_pool(name="psum", bufs=1))
 
         def bank(b):
             return psum.tile([P, BANK], F32, name="bank%d" % b)
 
+        main_words = (E - 1) * W2_EXPERT
         offs_sb = keep.tile([P, SLOTS // PER_COLUMN], U16, name="offs_sb")
         pos_sb = [keep.tile([P, T // PER_COLUMN], U16, name="pos_sb%d" % r) for r in range(LISTS)]
-        dy_sc = shared.tile([P, T], U8, name="dy_sc", align_bytes=64, offset=W2_MAIN * PACK - T // 2)
+        dy_sc = shared.tile([P, T], U8, name="dy_sc", align_bytes=64, offset=main_words * PACK - T // 2)
         slot_sc = [[keep.tile([P, 2 * C], U8, name="slot_sc%d%d" % (g, s), align_bytes=64) for s in range(PASSES)] for g in range(2)]
         dy_w = [keep.tile([P, T], I32, name="dy_w%d" % s, align_bytes=64) for s in range(PASSES)]
         w2_sc = keep.tile([P, E * PASSES, H], U8, name="w2_sc", align_bytes=64)
-        w2_first = keep.tile([P, PASSES * WIDE], I32, name="w2_first", align_bytes=64)
+        w2_first = keep.tile([P, W2_EXPERT], I32, name="w2_first", align_bytes=64)
         y = [keep.tile([P, SLOTS], F32, name="y%d" % j) for j in range(TILES)]
-        a_sb = [keep.tile([P, TILES, QUARTER], F32, name="a%d" % n)[:] for n in range(3)]
+        a_sb = [keep.tile([P, PACK, QUARTER], F32, name="a%d" % n) for n in range(4)]
         gate_rows = keep.tile([P, P], F32, name="gate_rows")
-        gate_col = keep.tile([P, LISTS * GATE_ROWS], F32, name="gate_col")
+        gate_col = keep.tile([P, LISTS * len(PLAIN)], F32, name="gate_col")
         ident = keep.tile([P, P], F32, name="ident")
         w1_w = keep.tile([P, K], U32, name="w1_w", align_bytes=64)
         w1_sc = keep.tile([P, K], U8, name="w1_sc", align_bytes=64)
@@ -82,31 +81,31 @@ def tile_moe_sub_silu_kernel(
                     in_=source(SCALE_ROWS * q, SCALE_ROWS * (q + 1)).bitcast(I32),
                 )
 
-        a_by_tile = a.rearrange("(j p) t -> p j t", p=P)
         a_by_quad = a.rearrange("(p d) t -> p d t", d=PACK)
         w2_rows = w2t_scales.rearrange("e s b i -> b (e s) i")
         w2_by_pass = w2t_words.rearrange("e s p i d -> p (e s) (i d)").bitcast(I32)
 
         def load_a(n):
-            nc.sync.dma_start(out=a_sb[n], in_=(a_by_tile if n in WHOLE else a_by_quad)[:, :, QUARTER * n : QUARTER * (n + 1)])
+            nc.sync.dma_start(out=a_sb[n][:], in_=a_by_quad[:, :, QUARTER * n : QUARTER * (n + 1)])
 
         def load_dy(s):
             nc.sync.dma_start(out=dy_w[s][:], in_=dy_words[s].rearrange("p t d -> p (t d)").bitcast(I32))
 
+        def load_expert(e, words):
+            nc.sync.dma_start(out=words.rearrange("p (s i) -> p s i", s=PASSES), in_=w2_by_pass[:, e * PASSES : (e + 1) * PASSES, :])
+
         nc.sync.dma_start(offs_sb[:], offs)
         load_scale_rows(dy_sc, PASSES * SCALE_ROWS, lambda b0, b1: dy_scales[:, b0:b1, :])
         load_a(0)
-        load_dy(0)
         load_a(1)
-        load_dy(1)
-        nc.sync.dma_start(
-            out=gate_rows[0 : LISTS * GATE_ROWS, :], in_=gate[:, 0, 0:HALF].rearrange("r (c t) -> r c t", t=P)
-        )
-        load_a(2)
-        nc.sync.dma_start(out=w2_first[:].rearrange("p (s i) -> p s i", s=PASSES), in_=w2_by_pass[:, 0:PASSES, 0:WIDE])
+        load_dy(0)
         load_scale_rows(w2_sc, SCALE_ROWS, lambda b0, b1: w2_rows[b0:b1, :, :])
-        nc.sync.dma_start(pos_sb[0][:], pos1)
-        nc.sync.dma_start(pos_sb[1][:], pos2)
+        load_a(2)
+        load_dy(1)
+        load_a(3)
+        load_expert(0, w2_first[:])
+        nc.sync.dma_start(out=gate_rows[0:4, :], in_=gate[:, 0, PLAIN[0] * P : (PLAIN[1] + 1) * P].rearrange("r (c t) -> c r t", t=P))
+        nc.sync.dma_start(out=gate_rows[4:6, :], in_=gate[:, 0, PLAIN[2] * P : (PLAIN[2] + 1) * P])
 
         def expert_offs(e):
             return offs_sb[:, e * C // PER_COLUMN : (e + 1) * C // PER_COLUMN]
@@ -118,60 +117,57 @@ def tile_moe_sub_silu_kernel(
                 out=slot_sc[g][1][0:MOVED_PARTITIONS, :].bitcast(I32),
                 in_=slot_sc[g][0][SCALE_ROWS : SCALE_ROWS + MOVED_PARTITIONS, :].bitcast(I32),
             )
-        w2_main = shared.tile([P, W2_MAIN], I32, name="w2_main", align_bytes=64, offset=0)
-        late = shared.tile([P, PACK * K + 2 * T], F32, name="late", align_bytes=64, offset=W2_MAIN * PACK)
+        nc.sync.dma_start(pos_sb[0][:], pos1)
+        nc.sync.dma_start(pos_sb[1][:], pos2)
+        w2_main = shared.tile([P, main_words], I32, name="w2_main", align_bytes=64, offset=0)
+        wide = (len(FIRST) + len(SECOND)) * P
+        late = shared.tile([P, PACK * K + LISTS * wide], F32, name="late", align_bytes=64, offset=main_words * PACK)
         w1_raw = late[:, 0 : PACK * K].rearrange("p (d k) -> p d k", d=PACK)
-        a_sb.append(late[:, PACK * K : PACK * K + T].rearrange("p (d t) -> p d t", d=PACK))
-        gate_wide = late[:, PACK * K + T :].rearrange("p (r t) -> p r t", r=LISTS)
         gate_by_row = gate.rearrange("r p t -> p r t")
-        early = (E - 1) * PASSES * WIDE
-        nc.sync.dma_start(out=w2_main[:, 0:early].rearrange("p (g i) -> p g i", i=WIDE), in_=w2_by_pass[:, PASSES:, 0:WIDE])
+        gate_wide = {}
+        for e in range(1, E):
+            load_expert(e, w2_main[:, (e - 1) * W2_EXPERT : e * W2_EXPERT])
+        column = PACK * K
+        for group in (FIRST, SECOND):
+            width = len(group) * P
+            gate_wide.update({group: late[:, column : column + LISTS * width].rearrange("p (r t) -> p r t", r=LISTS)})
+            column = column + LISTS * width
         nc.sync.dma_start(out=w1_raw, in_=w1t.rearrange("(p d) k -> p d k", d=PACK))
-        nc.sync.dma_start(out=gate_wide, in_=gate_by_row[:, :, HALF:T])
-        nc.sync.dma_start(out=w2_main[:, early:].rearrange("p (g i) -> p g i", i=WIDE), in_=w2_by_pass[:, :, WIDE:H])
-        load_a(3)
+        for group in (FIRST, SECOND):
+            nc.sync.dma_start(out=gate_wide[group], in_=gate_by_row[:, :, group[0] * P : (group[-1] + 1) * P])
 
         def weights(e, s, j):
-            if e == 0 and j < 2:
-                return w2_first[:, s * WIDE + j * P : s * WIDE + (j + 1) * P]
-            first = ((E * (j // 2) + e - 1) * PASSES + s) * WIDE + j % 2 * P
+            if e == 0:
+                return w2_first[:, s * H + j * P : s * H + (j + 1) * P]
+            first = (e - 1) * W2_EXPERT + s * H + j * P
             return w2_main[:, first : first + P]
 
-        slope = {n: keep.tile([P, QUARTER * PACK], F32, name="slope%d" % n) for n in range(3)}
-        right = {n: keep.tile([P, QUARTER * PACK], F32, name="right%d" % n) for n in range(3)}
-        left = {n: keep.tile([P, QUARTER * PACK], F32, name="left%d" % n) for n in range(3)}
+        slope = [keep.tile([P, QUARTER * PACK], F32, name="slope%d" % n) for n in range(4)]
+        right = [keep.tile([P, QUARTER * PACK], F32, name="right%d" % n) for n in range(4)]
+        left = [keep.tile([P, QUARTER * PACK], F32, name="left%d" % n) for n in range(4)]
 
-        def activate(n):
-            if n in WHOLE:
-                src, pattern = a_sb[n].rearrange("p j (c i) -> p j c i", i=4), "p (d c i) -> p d c i"
-            else:
-                src, pattern = a_sb[n].rearrange("p d (c i) -> p c d i", i=4), "p (c i d) -> p c d i"
+        for n in range(4):
+            src, pattern = a_sb[n][:].rearrange("p d (c i) -> p c d i", i=4), "p (c i d) -> p c d i"
             nc.scalar.activation(out=right[n][:].rearrange(pattern, i=4, d=PACK), in_=src, func=ACT.Silu, scale=-1.0)
             nc.scalar.activation(out=left[n][:].rearrange(pattern, i=4, d=PACK), in_=src, func=ACT.Tanh, scale=0.5)
-
-        gate_t = bank(0)
-        for n in WHOLE + (2,):
-            activate(n)
             nc.gpsimd.tensor_scalar(out=right[n][:], in0=right[n][:], scalar1=-0.5, scalar2=0.5, op0=ALU.mult, op1=ALU.add)
-            if n in WHOLE:
-                nc.scalar.activation(out=left[n][:], in_=left[n][:], func=ACT.Identity, bias=1.0)
+            if n < WHOLE_ON_GPSIMD:
+                nc.gpsimd.tensor_scalar(out=left[n][:], in0=left[n][:], scalar1=1.0, scalar2=1.0, op0=ALU.mult, op1=ALU.add)
                 nc.gpsimd.tensor_tensor(slope[n][:], left[n][:], right[n][:], ALU.mult)
-            else:
-                nc.scalar.activation(out=left[n][:, 0:BANK], in_=left[n][:, 0:BANK], func=ACT.Identity, bias=1.0)
-                nc.gpsimd.tensor_tensor(slope[n][:, 0:BANK], left[n][:, 0:BANK], right[n][:, 0:BANK], ALU.mult)
-            if n == WHOLE[-1]:
-                nc.tensor.transpose(gate_t[:, 0:P], gate_rows[:], ident[:])
-                nc.scalar.copy(out=gate_col[:], in_=gate_t[:, 0 : LISTS * GATE_ROWS])
-
-        def product_of_halves(n):
-            nc.vector.scalar_tensor_tensor(
-                out=slope[n][:, BANK:], in0=left[n][:, BANK:], scalar=1.0, in1=right[n][:, BANK:], op0=ALU.add, op1=ALU.mult
-            )
+        gate_t = bank(BANKS - 1)
+        nc.tensor.transpose(gate_t[:, 0:P], gate_rows[:], ident[:])
+        nc.scalar.copy(out=gate_col[:], in_=gate_t[:, 0 : LISTS * len(PLAIN)])
 
         slot_w = {}
+        for e in range(E):
+            for s in range(PASSES):
+                slot_w[e, s] = keep.tile([P, C], U32, name="slot_w%d%d" % (e, s), align_bytes=64)
+                nc.vector.tensor_copy(slot_w[e, s][:], dy_w[s][:].bitcast(U32).indirect(expert_offs(e)))
 
-        def product(e, j):
-            acc = bank(E * (j % 2) + e)
+        products = [(e, j) for e in range(E) for j in range(TILES - e)]
+        products.extend([(e, j) for j in range(1, TILES) for e in range(E - j, E)])
+        for n, (e, j) in enumerate(products):
+            acc = bank(n % BANKS)
             for s in range(PASSES):
                 nc.tensor.matmul_mx(
                     out=acc[:],
@@ -184,181 +180,132 @@ def tile_moe_sub_silu_kernel(
                 )
             nc.scalar.copy(out=y[j][:, e * C : (e + 1) * C], in_=acc[:])
 
-        for e in range(E):
-            for s in range(PASSES):
-                slot_w[e, s] = keep.tile([P, C], U32, name="slot_w%d%d" % (e, s), align_bytes=64)
-                nc.vector.tensor_copy(slot_w[e, s][:], dy_w[s][:].bitcast(U32).indirect(expert_offs(e)))
-            product(e, 0)
-            product(e, 1)
-        w1_bf = keep.tile([P, K, PACK], BF16, name="dy_w1", align_bytes=64)
+        w1_bf = keep.tile([P, K, PACK], BF16, name="w1_bf", align_bytes=64)
         nc.vector.tensor_copy(
             out=w1_bf[:].rearrange("p (c i) d -> p c d i", i=4), in_=w1_raw.rearrange("p d (c i) -> p c d i", i=4)
         )
-        product_of_halves(2)
+        for n in range(WHOLE_ON_GPSIMD, 4):
+            nc.vector.scalar_tensor_tensor(
+                out=slope[n][:], in0=left[n][:], scalar=1.0, in1=right[n][:], op0=ALU.add, op1=ALU.mult
+            )
         nc.vector.quantize_mx(out=w1_w[:].bitcast(E4M3), scales=w1_sc[:], in_=w1_bf[:].rearrange("p k d -> p (k d)"))
-        for j in range(2, TILES):
-            for e in range(E):
-                product(e, j)
 
-        right.update({3: keep.tile([P, QUARTER * PACK], F32, name="slot_w31", align_bytes=64)})
-        left.update({3: keep.tile([P, QUARTER * PACK], F32, name="slot_sc11", align_bytes=64)})
-
-        starts = STARTS
-        last = len(BLOCKS) - 1
-        turn_banks = [[[0, 1]], [[2, 3], [4, 5]], [[6, 7], [4, 5]], [[2]], [[3]]]
-        SIDE = 4
         turned = {}
         sums = {}
-        rounded = {}
+        regrouped = {}
+        picked = {}
+        rounded = [keep.tile([P, QUARTER, PACK], BF16, name="da_bf%d" % n, align_bytes=64) for n in range(4)]
 
-        def regroup(dst, source, j0, j1, scale):
+        def entries(r, t0, width):
+            return pos_sb[r][:, t0 // PER_COLUMN : (t0 + width) // PER_COLUMN]
+
+        def regroup(b, r, scale):
+            regrouped.update({(b, r): keep.tile([P, PACK, P], F32, name="regrouped%d%d" % (b, r))})
             nc.scalar.activation(
-                out=dst[:, :, 32 * j0 : 32 * j1],
-                in_=source[:, j0 * P : j1 * P].rearrange("t (p d) -> t d p", d=PACK),
-                func=ACT.Copy,
-                scale=scale,
+                out=regrouped[b, r][:], in_=turned[b][:].rearrange("t (p d) -> t d p", d=PACK), func=ACT.Copy, scale=scale
             )
 
-        def fetch(n, b, r, j):
-            t0, width = starts[b], BLOCKS[b]
-            subs = range(width // P)
-            quarter = t0 // QUARTER
-            whole = quarter in WHOLE
-            picked = keep.tile([P, width], F32, name="picked%d" % (n % PICKED_BUFS), align_bytes=64)
-            nc.vector.tensor_tensor(
-                picked[:],
-                y[j][:].indirect(pos_sb[r][:, t0 // PER_COLUMN : (t0 + width) // PER_COLUMN]),
-                slope[quarter][:, j * width : (j + 1) * width] if whole else gate_wide[:, r, t0 - HALF : t0 - HALF + width],
-                ALU.mult,
-            )
-            alone = b == last and j == TILES - 1
-            if whole:
-                for c in subs:
-                    if j == 0:
-                        turned.update({(b, r, c): bank(turn_banks[b][r][c])})
-                    nc.tensor.transpose(turned[b, r, c][:, j * P : (j + 1) * P], picked[:, c * P : (c + 1) * P], ident[:])
-                if j == TILES - 1:
-                    if r == LISTS - 1:
-                        rounded.update({b: results.tile([P, width, PACK], BF16, name="da_bf", align_bytes=64)})
-                    for c in subs:
-                        col = GATE_ROWS * r + t0 // P + c
-                        gated = combine.tile([P, PACK, P], F32, name="gated")
-                        regroup(gated, turned[b, r, c], 0, TILES, gate_col[:, col : col + 1])
-                        if r == 0:
-                            sums.update({(b, c): bank(turn_banks[b][0][c])})
-                        for d in range(PACK):
-                            nc.tensor.matmul(
-                                sums[b, c][:, d * P : (d + 1) * P], gated[:, d, :], ident[:],
-                                start=(r == 0 and d == 0), stop=(r == LISTS - 1 and d == PACK - 1), is_transpose=True,
-                            )
-                    if r == LISTS - 1:
-                        for c in subs:
-                            nc.scalar.copy(
-                                out=rounded[b][:, c * P : (c + 1) * P, :], in_=sums[b, c][:].rearrange("p (d t) -> p t d", d=PACK)
-                            )
-                return
-            closing = TILES - 2 if b == last else TILES - 1
-            for c in subs:
-                if r == 0 and (j == 0 or alone):
-                    turned.update({(b, alone, c): bank(SIDE if alone else turn_banks[b][0][c])})
-                nc.tensor.matmul(
-                    turned[b, alone, c][:, j * P : (j + 1) * P], picked[:, c * P : (c + 1) * P], ident[:],
-                    start=(r == 0 and (j == 0 or alone)), stop=(r == LISTS - 1 and (j == closing or alone)), is_transpose=True,
-                )
+        def turn_back(b, lists):
+            sums.update({b: bank(BLOCK_BANK[b])})
+            for r in range(lists):
+                for d in range(PACK):
+                    nc.tensor.matmul(
+                        sums[b][:, d * P : (d + 1) * P], regrouped[b, r][:, d, :], ident[:],
+                        start=(r == 0 and d == 0), stop=(r == lists - 1 and d == PACK - 1), is_transpose=True,
+                    )
+
+        def fetch_gated(n, group, j):
+            t0, width = group[0] * P, len(group) * P
+            for r in range(LISTS):
+                values = keep.tile([P, width], F32, name="gated%d" % ((LISTS * n + r) % VECTOR_RING))
+                nc.vector.tensor_tensor(values[:], y[j][:].indirect(entries(r, t0, width)), gate_wide[group][:, r, :], ALU.mult)
+                for c, b in enumerate(group):
+                    if r == 0 and j == 0:
+                        turned.update({b: bank(BLOCK_BANK[b])})
+                    nc.tensor.matmul(
+                        turned[b][:, j * P : (j + 1) * P], values[:, c * P : (c + 1) * P], ident[:],
+                        start=(r == 0 and j == 0), stop=(r == LISTS - 1 and j == TILES - 1), is_transpose=True,
+                    )
+
+        def sum_back(group):
+            for b in group:
+                regroup(b, 0, 1.0)
+                turn_back(b, 1)
+
+        def gate_plain(n):
+            c, r = divmod(n, LISTS)
+            regroup(PLAIN[c], r, gate_col[:, n : n + 1])
             if r == LISTS - 1:
-                turn_back(b, j)
+                turn_back(PLAIN[c], LISTS)
 
-        def turn_back(b, j):
-            alone = b == last and j == TILES - 1
-            closing = TILES - 2 if b == last else TILES - 1
-            for c in range(BLOCKS[b] // P):
-                if j == closing:
-                    sums.update({("summed", b, c): combine.tile([P, PACK, P], F32, name="gated")})
-                    regroup(sums["summed", b, c], turned[b, False, c], 0, j + 1, 1.0)
-                if alone:
-                    regroup(sums["summed", b, c], turned[b, True, c], j, j + 1, 1.0)
-                if j == TILES - 1:
-                    sums.update({(b, c): bank(turn_banks[b][0][c])})
-                    for d in range(PACK):
-                        nc.tensor.transpose(sums[b, c][:, d * P : (d + 1) * P], sums["summed", b, c][:, d, :], ident[:])
+        def fetch_plain(n):
+            c, r = divmod(n, LISTS)
+            b = PLAIN[c]
 
-        def finish(b, c):
-            quarter, u = divmod(starts[b] + c * P, QUARTER)
-            if c == 0:
-                rounded.update({b: keep.tile([P, BLOCKS[b], PACK], BF16, name="picked%d" % ((len(order) - 2) % PICKED_BUFS), align_bytes=64)})
+            def turn(j):
+                nc.tensor.transpose(turned[b][:, j * P : (j + 1) * P], picked[j][:], ident[:])
+
+            for j in range(TILES):
+                picked.update({j: keep.tile([P, P], F32, name="plain%d" % ((TILES * n + j) % SCALAR_RING))})
+                nc.scalar.activation(out=picked[j][:], in_=y[j][:].indirect(entries(r, b * P, P)), func=ACT.Copy)
+                if j == 1:
+                    if n > 0:
+                        gate_plain(n - 1)
+                    turned.update({b: bank(BLOCK_BANK[b])})
+                    turn(0)
+                if j >= 1:
+                    turn(j)
+
+        def finish(b):
+            quarter, u = divmod(b * P, QUARTER)
             nc.vector.tensor_tensor(
-                rounded[b][:, c * P : (c + 1) * P, :],
+                rounded[quarter][:, u : u + P, :],
                 slope[quarter][:, u * PACK : (u + P) * PACK].rearrange("p (t d) -> p t d", d=PACK),
-                sums[b, c][:].rearrange("p (d t) -> p t d", d=PACK),
+                sums[b][:].rearrange("p (d t) -> p t d", d=PACK),
                 ALU.mult,
             )
-
-        def quantise(b):
-            t0, width = starts[b], BLOCKS[b]
-            nc.vector.quantize_mx(
-                out=da_w[:, t0 : t0 + width].bitcast(E5M2),
-                scales=da_sc[:, t0 : t0 + width],
-                in_=rounded[b][:].rearrange("p t d -> p (t d)"),
-            )
-
-        def last_quarter():
-            activate(3)
-            nc.scalar.activation(out=right[3][:], in_=right[3][:], func=ACT.Identity, scale=-0.5, bias=0.5)
 
         out_by_tile = out.rearrange("(m p) t -> p m t", p=P)
 
-        def project(end, new, banks, both_engines):
-            res = results.tile([P, K // P, new], F32, name="res")
+        def project(n, banks):
+            cols = slice(n * QUARTER, (n + 1) * QUARTER)
+            nc.vector.quantize_mx(
+                out=da_w[:, cols].bitcast(E5M2), scales=da_sc[:, cols], in_=rounded[n][:].rearrange("p t d -> p (t d)")
+            )
+            res = keep.tile([P, K // P, QUARTER], F32, name="res%d" % n)
+            accs = [bank(b) for b in banks]
             for m in range(K // P):
-                acc = bank(banks[m])
+                acc = accs[m % len(banks)]
                 nc.tensor.matmul_mx(
-                    out=acc[:],
+                    out=acc[:, m * QUARTER : (m + 1) * QUARTER],
                     lhsT=w1_w[:, m * P : (m + 1) * P].bitcast(E4M3),
                     lhsT_scale=w1_sc[:, m * P : (m + 1) * P],
-                    rhs=da_w[:, end - BANK : end].bitcast(E5M2),
-                    rhs_scale=da_sc[:, end - BANK : end],
+                    rhs=da_w[:, cols].bitcast(E5M2),
+                    rhs_scale=da_sc[:, cols],
                     start=True,
                     stop=True,
                 )
-                if m == 1 and both_engines:
-                    nc.vector.tensor_copy(out=res[:, m, :], in_=acc[:, BANK - new : BANK])
-                else:
-                    nc.scalar.copy(out=res[:, m, :], in_=acc[:, BANK - new : BANK])
-                nc.sync.dma_start(out=out_by_tile[:, m, end - new : end], in_=res[:, m, :])
+            if len(banks) == 1:
+                nc.scalar.copy(out=res[:].rearrange("p m t -> p (m t)"), in_=accs[0][:])
+                nc.sync.dma_start(out=out_by_tile[:, :, cols], in_=res[:])
+            else:
+                nc.scalar.copy(out=res[:, 0, :], in_=accs[0][:, 0:QUARTER])
+                nc.vector.tensor_copy(out=res[:, 1, :], in_=accs[1][:, QUARTER:])
+                for m in range(K // P):
+                    nc.sync.dma_start(out=out_by_tile[:, m, cols], in_=res[:, m, :])
 
-        order = [(b, r, j) for j in range(TILES) for b in (1, 0) for r in range(LISTS)]
-        order.extend([(2, r, j) for r in range(LISTS) for j in range(TILES)])
-        order.extend([(b, r, j) for b in (3, 4) for j in range(TILES) for r in range(LISTS)])
-        after = {
-            GATHERS: [last_quarter],
-            2 * GATHERS + 5: [lambda: quantise(1)],
-            4 * GATHERS + 3: [lambda: quantise(2), lambda: project(HALF, HALF, [6, 7], False)],
-        }
-        for n, (b, r, j) in enumerate(order):
-            fetch(n, b, r, j)
-            for step in after.get(n, []):
-                step()
-        finish(0, 0)
-        finish(0, 1)
-        quantise(0)
-        project(T - QUARTER, QUARTER, [0, 1], False)
-        slope.update({3: keep.tile([P, QUARTER * PACK], F32, name="picked%d" % ((len(order) - 3) % PICKED_BUFS), align_bytes=64)})
-        rounded.update({"tail": results.tile([P, QUARTER, PACK], BF16, name="da_bf", align_bytes=64)})
-        for c, b in enumerate((last - 1, last)):
-            cols = slice(c * BANK, (c + 1) * BANK)
-            nc.vector.scalar_tensor_tensor(
-                out=slope[3][:, cols], in0=left[3][:, cols], scalar=1.0, in1=right[3][:, cols], op0=ALU.add, op1=ALU.mult
-            )
-        for c, b in enumerate((last - 1, last)):
-            nc.vector.tensor_tensor(
-                rounded["tail"][:, c * P : (c + 1) * P, :],
-                slope[3][:, c * BANK : (c + 1) * BANK].rearrange("p (t d) -> p t d", d=PACK),
-                sums[b, 0][:].rearrange("p (d t) -> p t d", d=PACK),
-                ALU.mult,
-            )
-        nc.vector.quantize_mx(
-            out=da_w[:, T - QUARTER : T].bitcast(E5M2),
-            scales=da_sc[:, T - QUARTER : T],
-            in_=rounded["tail"][:].rearrange("p t d -> p (t d)"),
-        )
-        project(T, QUARTER, [5, 6], True)
+        for j in range(TILES):
+            fetch_gated(j, FIRST, j)
+            fetch_plain(j)
+        for j in range(TILES):
+            fetch_gated(TILES + j, SECOND, j)
+            if j == 0:
+                sum_back(FIRST)
+            if j in (1, 3):
+                fetch_plain(TILES + j // 2)
+        sum_back(SECOND)
+        gate_plain(LISTS * len(PLAIN) - 1)
+        for n in range(4):
+            finish(2 * n)
+            finish(2 * n + 1)
+            project(n, [2 * n] if n < 3 else [1, 3])

@@ -30,14 +30,15 @@ TILES = H // P
 SLOTS = E * C
 QUARTER = T // 4
 MOVED_PARTITIONS = 112
-FIRST = (0, 1, 2)
-SECOND = (5, 6)
-PLAIN = (3, 4, 7)
-BLOCK_BANK = {0: 0, 1: 1, 2: 2, 3: 3, 4: 4, 7: 5, 5: 6, 6: 7}
-VECTOR_RING = 4
-SCALAR_RING = 8
+HALF = T // 2
+QUARTERS = 4
+BLOCKS = T // P
+PAIR = 2
+PLAIN_BLOCKS = HALF // P
+HELD = TILES - 1
 WHOLE_ON_GPSIMD = 2
-W2_EXPERT = PASSES * H
+WIDE = H // 2
+W2_PIECE = PASSES * WIDE
 
 
 def tile_moe_sub_silu_kernel(
@@ -52,18 +53,20 @@ def tile_moe_sub_silu_kernel(
         def bank(b):
             return psum.tile([P, BANK], F32, name="bank%d" % b)
 
-        main_words = (E - 1) * W2_EXPERT
+        main_words = (2 * E - 1) * W2_PIECE
         offs_sb = keep.tile([P, SLOTS // PER_COLUMN], U16, name="offs_sb")
         pos_sb = [keep.tile([P, T // PER_COLUMN], U16, name="pos_sb%d" % r) for r in range(LISTS)]
         dy_sc = shared.tile([P, T], U8, name="dy_sc", align_bytes=64, offset=main_words * PACK - T // 2)
         slot_sc = [[keep.tile([P, 2 * C], U8, name="slot_sc%d%d" % (g, s), align_bytes=64) for s in range(PASSES)] for g in range(2)]
         dy_w = [keep.tile([P, T], I32, name="dy_w%d" % s, align_bytes=64) for s in range(PASSES)]
         w2_sc = keep.tile([P, E * PASSES, H], U8, name="w2_sc", align_bytes=64)
-        w2_first = keep.tile([P, W2_EXPERT], I32, name="w2_first", align_bytes=64)
+        w2_first = keep.tile([P, W2_PIECE], I32, name="w2_first", align_bytes=64)
         y = [keep.tile([P, SLOTS], F32, name="y%d" % j) for j in range(TILES)]
-        a_sb = [keep.tile([P, PACK, QUARTER], F32, name="a%d" % n) for n in range(4)]
+        a_widths = [P, P, QUARTER, QUARTER, QUARTER]
+        a_starts = [sum(a_widths[:n]) for n in range(len(a_widths))]
+        a_sb = [keep.tile([P, TILES, width], F32, name="a%d" % n) for n, width in enumerate(a_widths)]
         gate_rows = keep.tile([P, P], F32, name="gate_rows")
-        gate_col = keep.tile([P, LISTS * len(PLAIN)], F32, name="gate_col")
+        gate_col = keep.tile([P, LISTS * PLAIN_BLOCKS], F32, name="gate_col")
         ident = keep.tile([P, P], F32, name="ident")
         w1_w = keep.tile([P, K], U32, name="w1_w", align_bytes=64)
         w1_sc = keep.tile([P, K], U8, name="w1_sc", align_bytes=64)
@@ -81,31 +84,34 @@ def tile_moe_sub_silu_kernel(
                     in_=source(SCALE_ROWS * q, SCALE_ROWS * (q + 1)).bitcast(I32),
                 )
 
-        a_by_quad = a.rearrange("(p d) t -> p d t", d=PACK)
+        a_by_tile = a.rearrange("(j p) t -> p j t", p=P)
         w2_rows = w2t_scales.rearrange("e s b i -> b (e s) i")
         w2_by_pass = w2t_words.rearrange("e s p i d -> p (e s) (i d)").bitcast(I32)
 
         def load_a(n):
-            nc.sync.dma_start(out=a_sb[n][:], in_=a_by_quad[:, :, QUARTER * n : QUARTER * (n + 1)])
+            nc.sync.dma_start(out=a_sb[n][:], in_=a_by_tile[:, :, a_starts[n] : a_starts[n] + a_widths[n]])
 
         def load_dy(s):
             nc.sync.dma_start(out=dy_w[s][:], in_=dy_words[s].rearrange("p t d -> p (t d)").bitcast(I32))
 
-        def load_expert(e, words):
-            nc.sync.dma_start(out=words.rearrange("p (s i) -> p s i", s=PASSES), in_=w2_by_pass[:, e * PASSES : (e + 1) * PASSES, :])
+        def load_weights(words, e0, e1, h):
+            nc.sync.dma_start(
+                out=words.rearrange("p (g i) -> p g i", i=WIDE),
+                in_=w2_by_pass[:, e0 * PASSES : e1 * PASSES, h * WIDE : (h + 1) * WIDE],
+            )
 
         nc.sync.dma_start(offs_sb[:], offs)
         load_scale_rows(dy_sc, PASSES * SCALE_ROWS, lambda b0, b1: dy_scales[:, b0:b1, :])
         load_a(0)
         load_a(1)
-        load_dy(0)
-        load_scale_rows(w2_sc, SCALE_ROWS, lambda b0, b1: w2_rows[b0:b1, :, :])
         load_a(2)
-        load_dy(1)
+        load_dy(0)
+        nc.sync.dma_start(out=gate_rows[0 : LISTS * PLAIN_BLOCKS, :], in_=gate[:, 0, 0:HALF].rearrange("r (c t) -> r c t", t=P))
         load_a(3)
-        load_expert(0, w2_first[:])
-        nc.sync.dma_start(out=gate_rows[0:4, :], in_=gate[:, 0, PLAIN[0] * P : (PLAIN[1] + 1) * P].rearrange("r (c t) -> c r t", t=P))
-        nc.sync.dma_start(out=gate_rows[4:6, :], in_=gate[:, 0, PLAIN[2] * P : (PLAIN[2] + 1) * P])
+        load_dy(1)
+        load_a(4)
+        load_weights(w2_first[:], 0, 1, 0)
+        load_scale_rows(w2_sc, SCALE_ROWS, lambda b0, b1: w2_rows[b0:b1, :, :])
 
         def expert_offs(e):
             return offs_sb[:, e * C // PER_COLUMN : (e + 1) * C // PER_COLUMN]
@@ -113,50 +119,68 @@ def tile_moe_sub_silu_kernel(
         for g in range(2):
             for u in range(2):
                 nc.vector.tensor_copy(slot_sc[g][0][:, u * C : (u + 1) * C], dy_sc[:].indirect(expert_offs(2 * g + u)))
+
+        def move_second_pass(g):
             nc.sync.dma_start(
                 out=slot_sc[g][1][0:MOVED_PARTITIONS, :].bitcast(I32),
                 in_=slot_sc[g][0][SCALE_ROWS : SCALE_ROWS + MOVED_PARTITIONS, :].bitcast(I32),
             )
+
+        w2_main = shared.tile([P, main_words], I32, name="w2_main", align_bytes=64, offset=0)
+        late = shared.tile([P, PACK * K + LISTS * HALF], F32, name="late", align_bytes=64, offset=main_words * PACK)
+        w1_raw = late[:, 0 : PACK * K].rearrange("p (d k) -> p d k", d=PACK)
+        gate_wide = late[:, PACK * K :].rearrange("p (r t) -> p r t", r=LISTS)
+
+        def load_main(e0, e1, h):
+            load_weights(w2_main[:, (E * h + e0 - 1) * W2_PIECE : (E * h + e1 - 1) * W2_PIECE], e0, e1, h)
+
+        move_second_pass(0)
+        load_main(1, 2, 0)
+        move_second_pass(1)
+        load_main(2, E, 0)
+        load_main(0, 2, 1)
+        nc.sync.dma_start(out=w1_raw, in_=w1t.rearrange("(p d) k -> p d k", d=PACK))
+        nc.sync.dma_start(out=gate_wide, in_=gate.rearrange("r p t -> p r t")[:, :, HALF:T])
+        load_main(2, E, 1)
         nc.sync.dma_start(pos_sb[0][:], pos1)
         nc.sync.dma_start(pos_sb[1][:], pos2)
-        w2_main = shared.tile([P, main_words], I32, name="w2_main", align_bytes=64, offset=0)
-        wide = (len(FIRST) + len(SECOND)) * P
-        late = shared.tile([P, PACK * K + LISTS * wide], F32, name="late", align_bytes=64, offset=main_words * PACK)
-        w1_raw = late[:, 0 : PACK * K].rearrange("p (d k) -> p d k", d=PACK)
-        gate_by_row = gate.rearrange("r p t -> p r t")
-        gate_wide = {}
-        for e in range(1, E):
-            load_expert(e, w2_main[:, (e - 1) * W2_EXPERT : e * W2_EXPERT])
-        column = PACK * K
-        for group in (FIRST, SECOND):
-            width = len(group) * P
-            gate_wide.update({group: late[:, column : column + LISTS * width].rearrange("p (r t) -> p r t", r=LISTS)})
-            column = column + LISTS * width
-        nc.sync.dma_start(out=w1_raw, in_=w1t.rearrange("(p d) k -> p d k", d=PACK))
-        for group in (FIRST, SECOND):
-            nc.sync.dma_start(out=gate_wide[group], in_=gate_by_row[:, :, group[0] * P : (group[-1] + 1) * P])
 
         def weights(e, s, j):
-            if e == 0:
-                return w2_first[:, s * H + j * P : s * H + (j + 1) * P]
-            first = (e - 1) * W2_EXPERT + s * H + j * P
+            if e == 0 and j < 2:
+                return w2_first[:, s * WIDE + j * P : s * WIDE + (j + 1) * P]
+            first = ((E * (j // 2) + e - 1) * PASSES + s) * WIDE + j % 2 * P
             return w2_main[:, first : first + P]
 
-        slope = [keep.tile([P, QUARTER * PACK], F32, name="slope%d" % n) for n in range(4)]
-        right = [keep.tile([P, QUARTER * PACK], F32, name="right%d" % n) for n in range(4)]
-        left = [keep.tile([P, QUARTER * PACK], F32, name="left%d" % n) for n in range(4)]
+        def by_word(rows):
+            return rows.rearrange("t (u p e) -> t u p e", u=PAIR, e=PAIR)
 
-        for n in range(4):
-            src, pattern = a_sb[n][:].rearrange("p d (c i) -> p c d i", i=4), "p (c i d) -> p c d i"
-            nc.scalar.activation(out=right[n][:].rearrange(pattern, i=4, d=PACK), in_=src, func=ACT.Silu, scale=-1.0)
-            nc.scalar.activation(out=left[n][:].rearrange(pattern, i=4, d=PACK), in_=src, func=ACT.Tanh, scale=0.5)
-            nc.gpsimd.tensor_scalar(out=right[n][:], in0=right[n][:], scalar1=-0.5, scalar2=0.5, op0=ALU.mult, op1=ALU.add)
+        def as_words(rows):
+            return rows.rearrange("t (p u e) -> t u p e", u=PAIR, e=PAIR)
+
+        def a_block(b):
+            n = max(i for i, first in enumerate(a_starts) if first <= b * P)
+            first = b * P - a_starts[n]
+            return a_sb[n][:, :, first : first + P]
+
+        slope = [keep.tile([P, PAIR * H], F32, name="slope%d" % n) for n in range(QUARTERS)]
+        left = [keep.tile([P, PAIR * H], F32, name="left%d" % n) for n in range(QUARTERS)]
+
+        for n in range(QUARTERS):
+            if n == 2:
+                gate_t = bank(0)
+                nc.tensor.transpose(gate_t[:, 0:P], gate_rows[:], ident[:])
+                nc.scalar.copy(out=gate_col[:], in_=gate_t[:, 0 : LISTS * PLAIN_BLOCKS])
+            for c in range(PAIR):
+                a_t = bank(PAIR * n + c)
+                for j in range(TILES):
+                    nc.tensor.transpose(a_t[:, j * P : (j + 1) * P], a_block(PAIR * n + c)[:, j, :], ident[:])
+                cols = slice(c * H, (c + 1) * H)
+                nc.scalar.activation(out=by_word(slope[n][:, cols]), in_=as_words(a_t[:]), func=ACT.Silu, scale=-1.0)
+                nc.scalar.activation(out=by_word(left[n][:, cols]), in_=as_words(a_t[:]), func=ACT.Tanh, scale=0.5)
+            nc.gpsimd.tensor_scalar(out=slope[n][:], in0=slope[n][:], scalar1=-0.5, scalar2=0.5, op0=ALU.mult, op1=ALU.add)
             if n < WHOLE_ON_GPSIMD:
                 nc.gpsimd.tensor_scalar(out=left[n][:], in0=left[n][:], scalar1=1.0, scalar2=1.0, op0=ALU.mult, op1=ALU.add)
-                nc.gpsimd.tensor_tensor(slope[n][:], left[n][:], right[n][:], ALU.mult)
-        gate_t = bank(BANKS - 1)
-        nc.tensor.transpose(gate_t[:, 0:P], gate_rows[:], ident[:])
-        nc.scalar.copy(out=gate_col[:], in_=gate_t[:, 0 : LISTS * len(PLAIN)])
+                nc.gpsimd.tensor_tensor(slope[n][:], left[n][:], slope[n][:], ALU.mult)
 
         slot_w = {}
         for e in range(E):
@@ -164,8 +188,8 @@ def tile_moe_sub_silu_kernel(
                 slot_w[e, s] = keep.tile([P, C], U32, name="slot_w%d%d" % (e, s), align_bytes=64)
                 nc.vector.tensor_copy(slot_w[e, s][:], dy_w[s][:].bitcast(U32).indirect(expert_offs(e)))
 
-        products = [(e, j) for e in range(E) for j in range(TILES - e)]
-        products.extend([(e, j) for j in range(1, TILES) for e in range(E - j, E)])
+        products = [(e, j) for e in range(E - 1) for j in range(2)]
+        products.extend([(0, 2), (1, 2), (0, 3), (3, 0), (3, 1), (2, 2), (3, 2), (1, 3), (2, 3), (3, 3)])
         for n, (e, j) in enumerate(products):
             acc = bank(n % BANKS)
             for s in range(PASSES):
@@ -184,100 +208,103 @@ def tile_moe_sub_silu_kernel(
         nc.vector.tensor_copy(
             out=w1_bf[:].rearrange("p (c i) d -> p c d i", i=4), in_=w1_raw.rearrange("p d (c i) -> p c d i", i=4)
         )
-        for n in range(WHOLE_ON_GPSIMD, 4):
+        for n in range(WHOLE_ON_GPSIMD, QUARTERS):
             nc.vector.scalar_tensor_tensor(
-                out=slope[n][:], in0=left[n][:], scalar=1.0, in1=right[n][:], op0=ALU.add, op1=ALU.mult
+                out=slope[n][:], in0=left[n][:], scalar=1.0, in1=slope[n][:], op0=ALU.add, op1=ALU.mult
             )
         nc.vector.quantize_mx(out=w1_w[:].bitcast(E4M3), scales=w1_sc[:], in_=w1_bf[:].rearrange("p k d -> p (k d)"))
 
         turned = {}
-        sums = {}
-        regrouped = {}
-        picked = {}
-        rounded = [keep.tile([P, QUARTER, PACK], BF16, name="da_bf%d" % n, align_bytes=64) for n in range(4)]
+        first_term = {}
+        rounded = [keep.tile([P, QUARTER, PACK], BF16, name="da_bf%d" % n, align_bytes=64) for n in range(QUARTERS)]
 
         def entries(r, t0, width):
             return pos_sb[r][:, t0 // PER_COLUMN : (t0 + width) // PER_COLUMN]
 
-        def regroup(b, r, scale):
-            regrouped.update({(b, r): keep.tile([P, PACK, P], F32, name="regrouped%d%d" % (b, r))})
-            nc.scalar.activation(
-                out=regrouped[b, r][:], in_=turned[b][:].rearrange("t (p d) -> t d p", d=PACK), func=ACT.Copy, scale=scale
-            )
+        def block_bank(b):
+            return bank((b + PLAIN_BLOCKS) % BANKS)
 
-        def turn_back(b, lists):
-            sums.update({b: bank(BLOCK_BANK[b])})
-            for r in range(lists):
-                for d in range(PACK):
-                    nc.tensor.matmul(
-                        sums[b][:, d * P : (d + 1) * P], regrouped[b, r][:, d, :], ident[:],
-                        start=(r == 0 and d == 0), stop=(r == lists - 1 and d == PACK - 1), is_transpose=True,
-                    )
+        def fetch_gated(j, r):
+            if (j, r) == (3, 1):
+                values = shared.tile([P, HALF], F32, name="gated_last", offset=HELD * QUARTER * PACK)
+            else:
+                values = keep.tile([P, HALF], F32, name="plain00" if (j, r) == (2, 1) else "gated%d%d" % (j, r))
+            nc.vector.tensor_tensor(values[:], y[j][:].indirect(entries(r, HALF, HALF)), gate_wide[:, r, :], ALU.mult)
+            for c in range(HALF // P):
+                b = PLAIN_BLOCKS + c
+                if r == 0 and j == 0:
+                    turned.update({b: block_bank(b)})
+                nc.tensor.matmul(
+                    turned[b][:, j * P : (j + 1) * P], values[:, c * P : (c + 1) * P], ident[:],
+                    start=(r == 0 and j == 0), stop=(r == LISTS - 1 and j == TILES - 1), is_transpose=True,
+                )
 
-        def fetch_gated(n, group, j):
-            t0, width = group[0] * P, len(group) * P
-            for r in range(LISTS):
-                values = keep.tile([P, width], F32, name="gated%d" % ((LISTS * n + r) % VECTOR_RING))
-                nc.vector.tensor_tensor(values[:], y[j][:].indirect(entries(r, t0, width)), gate_wide[group][:, r, :], ALU.mult)
-                for c, b in enumerate(group):
-                    if r == 0 and j == 0:
-                        turned.update({b: bank(BLOCK_BANK[b])})
-                    nc.tensor.matmul(
-                        turned[b][:, j * P : (j + 1) * P], values[:, c * P : (c + 1) * P], ident[:],
-                        start=(r == 0 and j == 0), stop=(r == LISTS - 1 and j == TILES - 1), is_transpose=True,
-                    )
-
-        def sum_back(group):
-            for b in group:
-                regroup(b, 0, 1.0)
-                turn_back(b, 1)
-
-        def gate_plain(n):
-            c, r = divmod(n, LISTS)
-            regroup(PLAIN[c], r, gate_col[:, n : n + 1])
-            if r == LISTS - 1:
-                turn_back(PLAIN[c], LISTS)
-
-        def fetch_plain(n):
-            c, r = divmod(n, LISTS)
-            b = PLAIN[c]
+        def fetch_plain(n, r):
+            values = {}
 
             def turn(j):
-                nc.tensor.transpose(turned[b][:, j * P : (j + 1) * P], picked[j][:], ident[:])
+                for c in range(PAIR):
+                    nc.tensor.transpose(turned[PAIR * n + c][:, j * P : (j + 1) * P], values[j][:, c * P : (c + 1) * P], ident[:])
 
             for j in range(TILES):
-                picked.update({j: keep.tile([P, P], F32, name="plain%d" % ((TILES * n + j) % SCALAR_RING))})
-                nc.scalar.activation(out=picked[j][:], in_=y[j][:].indirect(entries(r, b * P, P)), func=ACT.Copy)
+                if (r, j) == (0, 0):
+                    values[j] = opening[:, n * QUARTER : (n + 1) * QUARTER]
+                else:
+                    if j < HELD:
+                        place = ((LISTS * n + r) * HELD + j) * QUARTER * PACK
+                        values[j] = shared.tile([P, QUARTER], F32, name="held%d%d%d" % (n, r, j), offset=place)
+                    else:
+                        values[j] = keep.tile([P, QUARTER], F32, name="plain%d%d" % (n, r))
+                    nc.scalar.activation(out=values[j][:], in_=y[j][:].indirect(entries(r, n * QUARTER, QUARTER)), func=ACT.Copy)
+                if j == 0:
+                    continue
                 if j == 1:
-                    if n > 0:
-                        gate_plain(n - 1)
-                    turned.update({b: bank(BLOCK_BANK[b])})
+                    for b in range(PAIR * n, PAIR * (n + 1)):
+                        if r == 1:
+                            first_term.update({b: keep.tile([P, H], F32, name="first_term%d" % b)})
+                            nc.scalar.activation(out=first_term[b][:], in_=turned[b][:], func=ACT.Copy, scale=gate_col[:, b : b + 1])
+                        turned.update({b: block_bank(b)})
                     turn(0)
-                if j >= 1:
-                    turn(j)
+                turn(j)
+
+        def add_second(b):
+            col = PLAIN_BLOCKS + b
+            nc.vector.scalar_tensor_tensor(
+                out=first_term[b][:], in0=turned[b][:], scalar=gate_col[:, col : col + 1], in1=first_term[b][:],
+                op0=ALU.mult, op1=ALU.add,
+            )
 
         def finish(b):
-            quarter, u = divmod(b * P, QUARTER)
+            quarter, c = divmod(b, PAIR)
+            total = first_term[b] if b < PLAIN_BLOCKS else turned[b]
+            rows = keep.tile([P, H], BF16, name="da_rows%d" % b)
             nc.vector.tensor_tensor(
-                rounded[quarter][:, u : u + P, :],
-                slope[quarter][:, u * PACK : (u + P) * PACK].rearrange("p (t d) -> p t d", d=PACK),
-                sums[b][:].rearrange("p (d t) -> p t d", d=PACK),
-                ALU.mult,
+                by_word(rows[:]), by_word(slope[quarter][:, c * H : (c + 1) * H]), as_words(total[:]), ALU.mult
+            )
+            back = block_bank(b)
+            for u in range(PAIR):
+                nc.tensor.transpose(back[:, u * P : (u + 1) * P], rows[:].bitcast(F32)[:, u * P : (u + 1) * P], ident[:])
+            nc.scalar.copy(
+                out=rounded[quarter][:, c * P : (c + 1) * P, :].bitcast(F32),
+                in_=back[:, 0 : PAIR * P].rearrange("p (u t) -> p t u", u=PAIR),
             )
 
         out_by_tile = out.rearrange("(m p) t -> p m t", p=P)
 
-        def project(n, banks):
-            cols = slice(n * QUARTER, (n + 1) * QUARTER)
+        def project(b0, blocks, b):
+            width = blocks * P
+            cols = slice(b0 * P, b0 * P + width)
+            quarter, c = divmod(b0, PAIR)
             nc.vector.quantize_mx(
-                out=da_w[:, cols].bitcast(E5M2), scales=da_sc[:, cols], in_=rounded[n][:].rearrange("p t d -> p (t d)")
+                out=da_w[:, cols].bitcast(E5M2),
+                scales=da_sc[:, cols],
+                in_=rounded[quarter][:, c * P : c * P + width, :].rearrange("p t d -> p (t d)"),
             )
-            res = keep.tile([P, K // P, QUARTER], F32, name="res%d" % n)
-            accs = [bank(b) for b in banks]
+            res = keep.tile([P, K // P, width], F32, name="res%d" % b0)
+            acc = bank(b)
             for m in range(K // P):
-                acc = accs[m % len(banks)]
                 nc.tensor.matmul_mx(
-                    out=acc[:, m * QUARTER : (m + 1) * QUARTER],
+                    out=acc[:, m * width : (m + 1) * width],
                     lhsT=w1_w[:, m * P : (m + 1) * P].bitcast(E4M3),
                     lhsT_scale=w1_sc[:, m * P : (m + 1) * P],
                     rhs=da_w[:, cols].bitcast(E5M2),
@@ -285,27 +312,30 @@ def tile_moe_sub_silu_kernel(
                     start=True,
                     stop=True,
                 )
-            if len(banks) == 1:
-                nc.scalar.copy(out=res[:].rearrange("p m t -> p (m t)"), in_=accs[0][:])
-                nc.sync.dma_start(out=out_by_tile[:, :, cols], in_=res[:])
-            else:
-                nc.scalar.copy(out=res[:, 0, :], in_=accs[0][:, 0:QUARTER])
-                nc.vector.tensor_copy(out=res[:, 1, :], in_=accs[1][:, QUARTER:])
-                for m in range(K // P):
-                    nc.sync.dma_start(out=out_by_tile[:, m, cols], in_=res[:, m, :])
+            nc.scalar.copy(out=res[:].rearrange("p m t -> p (m t)"), in_=acc[:, 0 : K // P * width])
+            nc.sync.dma_start(out=out_by_tile[:, :, cols], in_=res[:])
 
+        def finish_plain(n):
+            for b in range(PAIR * n, PAIR * (n + 1)):
+                add_second(b)
+            for b in range(PAIR * n, PAIR * (n + 1)):
+                finish(b)
+
+        opening = keep.tile([P, HALF], F32, name="opening")
+        nc.vector.tensor_copy(opening[:], y[0][:].indirect(entries(0, 0, HALF)))
         for j in range(TILES):
-            fetch_gated(j, FIRST, j)
-            fetch_plain(j)
-        for j in range(TILES):
-            fetch_gated(TILES + j, SECOND, j)
-            if j == 0:
-                sum_back(FIRST)
-            if j in (1, 3):
-                fetch_plain(TILES + j // 2)
-        sum_back(SECOND)
-        gate_plain(LISTS * len(PLAIN) - 1)
-        for n in range(4):
-            finish(2 * n)
-            finish(2 * n + 1)
-            project(n, [2 * n] if n < 3 else [1, 3])
+            fetch_gated(j, 0)
+            fetch_plain(*divmod(j, LISTS))
+            fetch_gated(j, 1)
+        finish_plain(0)
+        for b in range(PLAIN_BLOCKS, BLOCKS):
+            finish(b)
+        for b in (2, 3):
+            add_second(b)
+        project(0, PAIR, 4)
+        finish(2)
+        project(4, PAIR, 0)
+        finish(3)
+        project(6, PAIR, 2)
+        project(2, 1, 1)
+        project(3, 1, 3)

@@ -22,23 +22,24 @@ PACK = 4
 QUADRANTS = 4
 SCALE_ROWS = 4
 BANK = 512
-BANKS = 8
 LISTS = 2
 PER_COLUMN = 16
 PASSES = N // (P * PACK)
 TILES = H // P
 SLOTS = E * C
 QUARTER = T // 4
+PAIR = QUARTER // P
 MOVED_PARTITIONS = 112
-HALF = T // 2
-QUARTERS = 4
-BLOCKS = T // P
-PAIR = 2
-PLAIN_BLOCKS = HALF // P
-HELD = TILES - 1
-WHOLE_ON_GPSIMD = 2
+SLOPE_GROUPS = 3
+SLOPE_FIRST = SLOPE_GROUPS * QUARTER
+GATE_ROWS = SLOPE_FIRST // P
+RING = 8
 WIDE = H // 2
 W2_PIECE = PASSES * WIDE
+FIRST_BANKS = ((2, 3), (6, 7), (2, 3))
+SECOND_BANKS = (4, 5)
+GATED_BANKS = (0, 1)
+SIDE_BANK = 6
 
 
 def tile_moe_sub_silu_kernel(
@@ -58,15 +59,13 @@ def tile_moe_sub_silu_kernel(
         pos_sb = [keep.tile([P, T // PER_COLUMN], U16, name="pos_sb%d" % r) for r in range(LISTS)]
         dy_sc = shared.tile([P, T], U8, name="dy_sc", align_bytes=64, offset=main_words * PACK - T // 2)
         slot_sc = [[keep.tile([P, 2 * C], U8, name="slot_sc%d%d" % (g, s), align_bytes=64) for s in range(PASSES)] for g in range(2)]
-        dy_w = [keep.tile([P, T], I32, name="dy_w%d" % s, align_bytes=64) for s in range(PASSES)]
+        dy_w = keep.tile([P, PASSES * T], I32, name="dy_w", align_bytes=64)
         w2_sc = keep.tile([P, E * PASSES, H], U8, name="w2_sc", align_bytes=64)
         w2_first = keep.tile([P, W2_PIECE], I32, name="w2_first", align_bytes=64)
         y = [keep.tile([P, SLOTS], F32, name="y%d" % j) for j in range(TILES)]
-        a_widths = [P, P, QUARTER, QUARTER, QUARTER]
-        a_starts = [sum(a_widths[:n]) for n in range(len(a_widths))]
-        a_sb = [keep.tile([P, TILES, width], F32, name="a%d" % n) for n, width in enumerate(a_widths)]
+        a_sb = [keep.tile([P, SLOPE_FIRST], F32, name="a%d" % j) for j in range(TILES)]
         gate_rows = keep.tile([P, P], F32, name="gate_rows")
-        gate_col = keep.tile([P, LISTS * PLAIN_BLOCKS], F32, name="gate_col")
+        gate_col = keep.tile([P, LISTS * GATE_ROWS], F32, name="gate_col")
         ident = keep.tile([P, P], F32, name="ident")
         w1_w = keep.tile([P, K], U32, name="w1_w", align_bytes=64)
         w1_sc = keep.tile([P, K], U8, name="w1_sc", align_bytes=64)
@@ -84,15 +83,11 @@ def tile_moe_sub_silu_kernel(
                     in_=source(SCALE_ROWS * q, SCALE_ROWS * (q + 1)).bitcast(I32),
                 )
 
-        a_by_tile = a.rearrange("(j p) t -> p j t", p=P)
         w2_rows = w2t_scales.rearrange("e s b i -> b (e s) i")
         w2_by_pass = w2t_words.rearrange("e s p i d -> p (e s) (i d)").bitcast(I32)
 
-        def load_a(n):
-            nc.sync.dma_start(out=a_sb[n][:], in_=a_by_tile[:, :, a_starts[n] : a_starts[n] + a_widths[n]])
-
-        def load_dy(s):
-            nc.sync.dma_start(out=dy_w[s][:], in_=dy_words[s].rearrange("p t d -> p (t d)").bitcast(I32))
+        def load_a(j):
+            nc.sync.dma_start(out=a_sb[j][:], in_=a[j * P : (j + 1) * P, 0:SLOPE_FIRST])
 
         def load_weights(words, e0, e1, h):
             nc.sync.dma_start(
@@ -104,13 +99,15 @@ def tile_moe_sub_silu_kernel(
         load_scale_rows(dy_sc, PASSES * SCALE_ROWS, lambda b0, b1: dy_scales[:, b0:b1, :])
         load_a(0)
         load_a(1)
+        nc.sync.dma_start(
+            out=dy_w[:].rearrange("p (s t) -> p s t", s=PASSES), in_=dy_words.rearrange("s p t d -> p s (t d)").bitcast(I32)
+        )
         load_a(2)
-        load_dy(0)
-        nc.sync.dma_start(out=gate_rows[0 : LISTS * PLAIN_BLOCKS, :], in_=gate[:, 0, 0:HALF].rearrange("r (c t) -> r c t", t=P))
         load_a(3)
-        load_dy(1)
-        load_a(4)
         load_weights(w2_first[:], 0, 1, 0)
+        nc.sync.dma_start(
+            out=gate_rows[0 : LISTS * GATE_ROWS, :], in_=gate[:, 0, 0:SLOPE_FIRST].rearrange("r (c t) -> r c t", t=P)
+        )
         load_scale_rows(w2_sc, SCALE_ROWS, lambda b0, b1: w2_rows[b0:b1, :, :])
 
         def expert_offs(e):
@@ -127,9 +124,10 @@ def tile_moe_sub_silu_kernel(
             )
 
         w2_main = shared.tile([P, main_words], I32, name="w2_main", align_bytes=64, offset=0)
-        late = shared.tile([P, PACK * K + LISTS * HALF], F32, name="late", align_bytes=64, offset=main_words * PACK)
+        late = shared.tile([P, PACK * K + LISTS * QUARTER + T], F32, name="late", align_bytes=64, offset=main_words * PACK)
         w1_raw = late[:, 0 : PACK * K].rearrange("p (d k) -> p d k", d=PACK)
-        gate_wide = late[:, PACK * K :].rearrange("p (r t) -> p r t", r=LISTS)
+        gate_wide = late[:, PACK * K : PACK * K + LISTS * QUARTER].rearrange("p (r t) -> p r t", r=LISTS)
+        a_last = late[:, PACK * K + LISTS * QUARTER :].rearrange("p (d t) -> p d t", d=PACK)
 
         def load_main(e0, e1, h):
             load_weights(w2_main[:, (E * h + e0 - 1) * W2_PIECE : (E * h + e1 - 1) * W2_PIECE], e0, e1, h)
@@ -138,12 +136,13 @@ def tile_moe_sub_silu_kernel(
         load_main(1, 2, 0)
         move_second_pass(1)
         load_main(2, E, 0)
-        load_main(0, 2, 1)
         nc.sync.dma_start(out=w1_raw, in_=w1t.rearrange("(p d) k -> p d k", d=PACK))
-        nc.sync.dma_start(out=gate_wide, in_=gate.rearrange("r p t -> p r t")[:, :, HALF:T])
-        load_main(2, E, 1)
         nc.sync.dma_start(pos_sb[0][:], pos1)
         nc.sync.dma_start(pos_sb[1][:], pos2)
+        nc.sync.dma_start(out=gate_wide, in_=gate.rearrange("r p t -> p r t")[:, :, SLOPE_FIRST:T])
+        load_main(0, 2, 1)
+        load_main(2, E, 1)
+        nc.sync.dma_start(out=a_last, in_=a.rearrange("(p d) t -> p d t", d=PACK)[:, :, SLOPE_FIRST:T])
 
         def weights(e, s, j):
             if e == 0 and j < 2:
@@ -151,156 +150,173 @@ def tile_moe_sub_silu_kernel(
             first = ((E * (j // 2) + e - 1) * PASSES + s) * WIDE + j % 2 * P
             return w2_main[:, first : first + P]
 
-        def by_word(rows):
-            return rows.rearrange("t (u p e) -> t u p e", u=PAIR, e=PAIR)
-
-        def as_words(rows):
-            return rows.rearrange("t (p u e) -> t u p e", u=PAIR, e=PAIR)
-
-        def a_block(b):
-            n = max(i for i, first in enumerate(a_starts) if first <= b * P)
-            first = b * P - a_starts[n]
-            return a_sb[n][:, :, first : first + P]
-
-        slope = [keep.tile([P, PAIR * H], F32, name="slope%d" % n) for n in range(QUARTERS)]
-        left = [keep.tile([P, PAIR * H], F32, name="left%d" % n) for n in range(QUARTERS)]
-
-        for n in range(QUARTERS):
-            if n == 2:
-                gate_t = bank(0)
-                nc.tensor.transpose(gate_t[:, 0:P], gate_rows[:], ident[:])
-                nc.scalar.copy(out=gate_col[:], in_=gate_t[:, 0 : LISTS * PLAIN_BLOCKS])
-            for c in range(PAIR):
-                a_t = bank(PAIR * n + c)
-                for j in range(TILES):
-                    nc.tensor.transpose(a_t[:, j * P : (j + 1) * P], a_block(PAIR * n + c)[:, j, :], ident[:])
-                cols = slice(c * H, (c + 1) * H)
-                nc.scalar.activation(out=by_word(slope[n][:, cols]), in_=as_words(a_t[:]), func=ACT.Silu, scale=-1.0)
-                nc.scalar.activation(out=by_word(left[n][:, cols]), in_=as_words(a_t[:]), func=ACT.Tanh, scale=0.5)
-            nc.gpsimd.tensor_scalar(out=slope[n][:], in0=slope[n][:], scalar1=-0.5, scalar2=0.5, op0=ALU.mult, op1=ALU.add)
-            if n < WHOLE_ON_GPSIMD:
-                nc.gpsimd.tensor_scalar(out=left[n][:], in0=left[n][:], scalar1=1.0, scalar2=1.0, op0=ALU.mult, op1=ALU.add)
-                nc.gpsimd.tensor_tensor(slope[n][:], left[n][:], slope[n][:], ALU.mult)
+        slope = [keep.tile([P, SLOPE_FIRST], F32, name="slope%d" % j) for j in range(TILES)]
+        left = [keep.tile([P, SLOPE_FIRST], F32, name="left%d" % j) for j in range(TILES)]
+        for j in range(TILES):
+            nc.scalar.activation(out=slope[j][:], in_=a_sb[j][:], func=ACT.Silu, scale=-1.0)
+            nc.scalar.activation(out=left[j][:], in_=a_sb[j][:], func=ACT.Tanh, scale=0.5)
+            nc.scalar.activation(out=left[j][:], in_=left[j][:], func=ACT.Identity, bias=1.0)
+            nc.gpsimd.tensor_scalar(out=slope[j][:], in0=slope[j][:], scalar1=-0.5, scalar2=0.5, op0=ALU.mult, op1=ALU.add)
+            nc.gpsimd.tensor_tensor(slope[j][:], left[j][:], slope[j][:], ALU.mult)
 
         slot_w = {}
         for e in range(E):
             for s in range(PASSES):
                 slot_w[e, s] = keep.tile([P, C], U32, name="slot_w%d%d" % (e, s), align_bytes=64)
-                nc.vector.tensor_copy(slot_w[e, s][:], dy_w[s][:].bitcast(U32).indirect(expert_offs(e)))
+                pieces = 2 if (e, s) == (E - 1, PASSES - 1) else 1
+                for u in range(pieces):
+                    first, width = e * C + u * C // pieces, C // pieces
+                    nc.vector.tensor_copy(
+                        slot_w[e, s][:, first - e * C : first - e * C + width],
+                        dy_w[:, s * T : (s + 1) * T].bitcast(U32).indirect(offs_sb[:, first // PER_COLUMN : (first + width) // PER_COLUMN]),
+                    )
 
-        products = [(e, j) for e in range(E - 1) for j in range(2)]
-        products.extend([(0, 2), (1, 2), (0, 3), (3, 0), (3, 1), (2, 2), (3, 2), (1, 3), (2, 3), (3, 3)])
-        for n, (e, j) in enumerate(products):
-            acc = bank(n % BANKS)
+        def product(e, j, u0, width, b):
+            acc = bank(b)
             for s in range(PASSES):
                 nc.tensor.matmul_mx(
-                    out=acc[:],
+                    out=acc[:, 0:width],
                     lhsT=weights(e, s, j).bitcast(E4M3),
                     lhsT_scale=w2_sc[:, e * PASSES + s, j * P : (j + 1) * P],
-                    rhs=slot_w[e, s][:].bitcast(E5M2),
-                    rhs_scale=slot_sc[e // 2][s][:, e % 2 * C : (e % 2 + 1) * C],
+                    rhs=slot_w[e, s][:, u0 : u0 + width].bitcast(E5M2),
+                    rhs_scale=slot_sc[e // 2][s][:, e % 2 * C + u0 : e % 2 * C + u0 + width],
                     start=(s == 0),
                     stop=(s == PASSES - 1),
                 )
-            nc.scalar.copy(out=y[j][:, e * C : (e + 1) * C], in_=acc[:])
+            nc.scalar.copy(out=y[j][:, e * C + u0 : e * C + u0 + width], in_=acc[:, 0:width])
 
-        w1_bf = keep.tile([P, K, PACK], BF16, name="w1_bf", align_bytes=64)
-        nc.vector.tensor_copy(
-            out=w1_bf[:].rearrange("p (c i) d -> p c d i", i=4), in_=w1_raw.rearrange("p d (c i) -> p c d i", i=4)
-        )
-        for n in range(WHOLE_ON_GPSIMD, QUARTERS):
-            nc.vector.scalar_tensor_tensor(
-                out=slope[n][:], in0=left[n][:], scalar=1.0, in1=slope[n][:], op0=ALU.add, op1=ALU.mult
-            )
+        gate_t = bank(E - 1)
+        nc.tensor.transpose(gate_t[:, 0:P], gate_rows[:], ident[:])
+        nc.scalar.copy(out=gate_col[:], in_=gate_t[:, 0 : LISTS * GATE_ROWS])
+        for e in range(E):
+            if e == E - 1:
+                w1_bf = keep.tile([P, K, PACK], BF16, name="w1_bf", align_bytes=64)
+                nc.vector.tensor_copy(
+                    out=w1_bf[:].rearrange("p (c i) d -> p c d i", i=4), in_=w1_raw.rearrange("p d (c i) -> p c d i", i=4)
+                )
+                product(e, 0, 0, C // 2, e)
+                product(e, 0, C // 2, C // 2, 0)
+            else:
+                product(e, 0, 0, C, e)
+            product(e, 1, 0, C, E + e)
         nc.vector.quantize_mx(out=w1_w[:].bitcast(E4M3), scales=w1_sc[:], in_=w1_bf[:].rearrange("p k d -> p (k d)"))
+        for j in range(2, TILES):
+            for e in range(E):
+                product(e, j, 0, C, E * (j % 2) + e)
 
         turned = {}
-        first_term = {}
-        rounded = [keep.tile([P, QUARTER, PACK], BF16, name="da_bf%d" % n, align_bytes=64) for n in range(QUARTERS)]
+        sums = {}
+        regrouped = {}
+        rounded = [keep.tile([P, QUARTER, PACK], BF16, name="da_bf%d" % g, align_bytes=64) for g in range(SLOPE_GROUPS + 1)]
+        fetched = []
 
-        def entries(r, t0, width):
-            return pos_sb[r][:, t0 // PER_COLUMN : (t0 + width) // PER_COLUMN]
+        def gather(t0, width, r, j, factor):
+            values = keep.tile([P, width], F32, name="picked%d" % (len(fetched) % RING))
+            fetched.append(values)
+            entries = pos_sb[r][:, t0 // PER_COLUMN : (t0 + width) // PER_COLUMN]
+            nc.vector.tensor_tensor(values[:], y[j][:].indirect(entries), factor, ALU.mult)
+            return values
 
-        def block_bank(b):
-            return bank((b + PLAIN_BLOCKS) % BANKS)
+        def regroup(key, source, j0, j1, scale):
+            if j0 == 0:
+                regrouped.update({key: keep.tile([P, PACK, P], F32, name="regrouped%d%d%d" % (key[0] % 2, key[1], key[2]))})
+            nc.scalar.activation(
+                out=regrouped[key][:, :, 32 * j0 : 32 * j1],
+                in_=source.rearrange("t (p d) -> t d p", d=PACK),
+                func=ACT.Copy,
+                scale=scale,
+            )
 
-        def fetch_gated(j, r):
-            if (j, r) == (3, 1):
-                values = shared.tile([P, HALF], F32, name="gated_last", offset=HELD * QUARTER * PACK)
-            else:
-                values = keep.tile([P, HALF], F32, name="plain00" if (j, r) == (2, 1) else "gated%d%d" % (j, r))
-            nc.vector.tensor_tensor(values[:], y[j][:].indirect(entries(r, HALF, HALF)), gate_wide[:, r, :], ALU.mult)
-            for c in range(HALF // P):
-                b = PLAIN_BLOCKS + c
-                if r == 0 and j == 0:
-                    turned.update({b: block_bank(b)})
+        def turn_back(g, r, c, b, lists):
+            if r == 0:
+                sums.update({(g, c): bank(b)})
+            for d in range(PACK):
                 nc.tensor.matmul(
-                    turned[b][:, j * P : (j + 1) * P], values[:, c * P : (c + 1) * P], ident[:],
-                    start=(r == 0 and j == 0), stop=(r == LISTS - 1 and j == TILES - 1), is_transpose=True,
+                    sums[g, c][:, d * P : (d + 1) * P], regrouped[g, r, c][:, d, :], ident[:],
+                    start=(r == 0 and d == 0), stop=(r == lists - 1 and d == PACK - 1), is_transpose=True,
                 )
 
-        def fetch_plain(n, r):
-            values = {}
-
-            def turn(j):
-                for c in range(PAIR):
-                    nc.tensor.transpose(turned[PAIR * n + c][:, j * P : (j + 1) * P], values[j][:, c * P : (c + 1) * P], ident[:])
-
-            for j in range(TILES):
-                if (r, j) == (0, 0):
-                    values[j] = opening[:, n * QUARTER : (n + 1) * QUARTER]
-                else:
-                    if j < HELD:
-                        place = ((LISTS * n + r) * HELD + j) * QUARTER * PACK
-                        values[j] = shared.tile([P, QUARTER], F32, name="held%d%d%d" % (n, r, j), offset=place)
-                    else:
-                        values[j] = keep.tile([P, QUARTER], F32, name="plain%d%d" % (n, r))
-                    nc.scalar.activation(out=values[j][:], in_=y[j][:].indirect(entries(r, n * QUARTER, QUARTER)), func=ACT.Copy)
+        def fetch_sloped(g, r, j, blocks):
+            t0, width = g * QUARTER + blocks[0] * P, len(blocks) * P
+            values = gather(t0, width, r, j, slope[j][:, t0 : t0 + width])
+            split = (g, r, blocks[0]) == (SLOPE_GROUPS - 1, LISTS - 1, PAIR - 1)
+            alone = split and j == TILES - 1
+            if alone:
+                turned.update({"side": bank(SIDE_BANK)})
+            for u, c in enumerate(blocks):
                 if j == 0:
-                    continue
-                if j == 1:
-                    for b in range(PAIR * n, PAIR * (n + 1)):
-                        if r == 1:
-                            first_term.update({b: keep.tile([P, H], F32, name="first_term%d" % b)})
-                            nc.scalar.activation(out=first_term[b][:], in_=turned[b][:], func=ACT.Copy, scale=gate_col[:, b : b + 1])
-                        turned.update({b: block_bank(b)})
-                    turn(0)
-                turn(j)
+                    turned.update({(r, c): bank((FIRST_BANKS[g], SECOND_BANKS)[r][c])})
+                target = turned["side"][:, 0:P] if alone else turned[r, c][:, j * P : (j + 1) * P]
+                nc.tensor.transpose(target, values[:, u * P : (u + 1) * P], ident[:])
+            for c in blocks:
+                col = GATE_ROWS * r + PAIR * g + c
+                weight = gate_col[:, col : col + 1]
+                if alone:
+                    regroup((g, r, c), turned["side"][:, 0:P], j, TILES, weight)
+                elif j == (TILES - 2 if split else TILES - 1):
+                    regroup((g, r, c), turned[r, c][:, 0 : (j + 1) * P], 0, j + 1, weight)
+                if j == TILES - 1:
+                    turn_back(g, r, c, FIRST_BANKS[g][c], LISTS)
+            if j == TILES - 1 and r == LISTS - 1:
+                for c in blocks:
+                    nc.scalar.copy(
+                        out=rounded[g][:, c * P : (c + 1) * P, :], in_=sums[g, c][:].rearrange("p (d t) -> p t d", d=PACK)
+                    )
 
-        def add_second(b):
-            col = PLAIN_BLOCKS + b
-            nc.vector.scalar_tensor_tensor(
-                out=first_term[b][:], in0=turned[b][:], scalar=gate_col[:, col : col + 1], in1=first_term[b][:],
-                op0=ALU.mult, op1=ALU.add,
-            )
+        def fetch_gated(r, j):
+            g = SLOPE_GROUPS
+            values = gather(SLOPE_FIRST, QUARTER, r, j, gate_wide[:, r, :])
+            for c in range(PAIR):
+                if r == 0 and j == 0:
+                    turned.update({("gated", c): bank(GATED_BANKS[c])})
+                nc.tensor.matmul(
+                    turned["gated", c][:, j * P : (j + 1) * P], values[:, c * P : (c + 1) * P], ident[:],
+                    start=(r == 0 and j == 0), stop=(r == LISTS - 1 and j == TILES - 1), is_transpose=True,
+                )
+            if r == LISTS - 1 and j == TILES - 1:
+                for c in range(PAIR):
+                    regroup((g, 0, c), turned["gated", c][:], 0, TILES, -0.5)
+                    turn_back(g, 0, c, GATED_BANKS[c], 1)
 
-        def finish(b):
-            quarter, c = divmod(b, PAIR)
-            total = first_term[b] if b < PLAIN_BLOCKS else turned[b]
-            rows = keep.tile([P, H], BF16, name="da_rows%d" % b)
-            nc.vector.tensor_tensor(
-                by_word(rows[:]), by_word(slope[quarter][:, c * H : (c + 1) * H]), as_words(total[:]), ALU.mult
-            )
-            back = block_bank(b)
-            for u in range(PAIR):
-                nc.tensor.transpose(back[:, u * P : (u + 1) * P], rows[:].bitcast(F32)[:, u * P : (u + 1) * P], ident[:])
-            nc.scalar.copy(
-                out=rounded[quarter][:, c * P : (c + 1) * P, :].bitcast(F32),
-                in_=back[:, 0 : PAIR * P].rearrange("p (u t) -> p t u", u=PAIR),
-            )
+        silu_last = keep.tile([P, QUARTER * PACK], F32, name="slot_w31", align_bytes=64)
+        tanh_last = keep.tile([P, QUARTER * PACK], F32, name="slot_sc11", align_bytes=64)
+
+        def activate_last():
+            src, pattern = a_last.rearrange("p d (c i) -> p c d i", i=4), "p (c i d) -> p c d i"
+            nc.scalar.activation(out=silu_last[:].rearrange(pattern, i=4, d=PACK), in_=src, func=ACT.Silu, scale=-1.0)
+            nc.scalar.activation(out=tanh_last[:].rearrange(pattern, i=4, d=PACK), in_=src, func=ACT.Tanh, scale=0.5)
+
+        def finish_gated():
+            g = SLOPE_GROUPS
+            part = keep.tile([P, QUARTER * PACK], F32, name="picked%d" % ((len(fetched) - 2) % RING))
+            for c in range(PAIR):
+                cols = slice(c * BANK, (c + 1) * BANK)
+                nc.vector.scalar_tensor_tensor(
+                    out=part[:, cols].rearrange("p (t d) -> p t d", d=PACK),
+                    in0=silu_last[:, cols].rearrange("p (t d) -> p t d", d=PACK),
+                    scalar=-1.0,
+                    in1=sums[g, c][:].rearrange("p (d t) -> p t d", d=PACK),
+                    op0=ALU.add,
+                    op1=ALU.mult,
+                )
+            for c in range(PAIR):
+                cols = slice(c * BANK, (c + 1) * BANK)
+                nc.vector.scalar_tensor_tensor(
+                    out=rounded[g][:].rearrange("p t d -> p (t d)")[:, cols], in0=tanh_last[:, cols], scalar=1.0, in1=part[:, cols],
+                    op0=ALU.add, op1=ALU.mult,
+                )
 
         out_by_tile = out.rearrange("(m p) t -> p m t", p=P)
 
-        def project(b0, blocks, b):
-            width = blocks * P
-            cols = slice(b0 * P, b0 * P + width)
-            quarter, c = divmod(b0, PAIR)
+        def project(g, blocks, b):
+            width = len(blocks) * P
+            cols = slice(g * QUARTER + blocks[0] * P, g * QUARTER + blocks[0] * P + width)
             nc.vector.quantize_mx(
                 out=da_w[:, cols].bitcast(E5M2),
                 scales=da_sc[:, cols],
-                in_=rounded[quarter][:, c * P : c * P + width, :].rearrange("p t d -> p (t d)"),
+                in_=rounded[g][:, blocks[0] * P : blocks[0] * P + width, :].rearrange("p t d -> p (t d)"),
             )
-            res = keep.tile([P, K // P, width], F32, name="res%d" % b0)
+            res = keep.tile([P, K // P, width], F32, name="res%d%d" % (g, blocks[0]))
             acc = bank(b)
             for m in range(K // P):
                 nc.tensor.matmul_mx(
@@ -315,27 +331,23 @@ def tile_moe_sub_silu_kernel(
             nc.scalar.copy(out=res[:].rearrange("p m t -> p (m t)"), in_=acc[:, 0 : K // P * width])
             nc.sync.dma_start(out=out_by_tile[:, :, cols], in_=res[:])
 
-        def finish_plain(n):
-            for b in range(PAIR * n, PAIR * (n + 1)):
-                add_second(b)
-            for b in range(PAIR * n, PAIR * (n + 1)):
-                finish(b)
-
-        opening = keep.tile([P, HALF], F32, name="opening")
-        nc.vector.tensor_copy(opening[:], y[0][:].indirect(entries(0, 0, HALF)))
+        both = list(range(PAIR))
+        last = SLOPE_GROUPS - 1
         for j in range(TILES):
-            fetch_gated(j, 0)
-            fetch_plain(*divmod(j, LISTS))
-            fetch_gated(j, 1)
-        finish_plain(0)
-        for b in range(PLAIN_BLOCKS, BLOCKS):
-            finish(b)
-        for b in (2, 3):
-            add_second(b)
-        project(0, PAIR, 4)
-        finish(2)
-        project(4, PAIR, 0)
-        finish(3)
-        project(6, PAIR, 2)
-        project(2, 1, 1)
-        project(3, 1, 3)
+            for r in range(LISTS):
+                fetch_sloped(0, r, j, both)
+            for r in range(LISTS):
+                fetch_gated(r, j)
+            if j == TILES - 2:
+                activate_last()
+        for g in range(1, SLOPE_GROUPS):
+            for r in range(LISTS):
+                for blocks in [[c] for c in both] if (g, r) == (last, LISTS - 1) else [both]:
+                    for j in range(TILES):
+                        fetch_sloped(g, r, j, blocks)
+                        if (r, j, blocks[0]) == (LISTS - 1, 1, 0):
+                            project(g - 1, both, FIRST_BANKS[g - 1][1])
+        finish_gated()
+        project(last, [0], SECOND_BANKS[0])
+        project(SLOPE_GROUPS, both, GATED_BANKS[0])
+        project(last, [1], GATED_BANKS[1])

@@ -308,7 +308,7 @@ def tile_moe_sub_silu_kernel(
 
         out_by_tile = out.rearrange("(m p) t -> p m t", p=P)
 
-        def project(g, blocks, b):
+        def project(g, blocks, banks):
             width = len(blocks) * P
             cols = slice(g * QUARTER + blocks[0] * P, g * QUARTER + blocks[0] * P + width)
             nc.vector.quantize_mx(
@@ -316,11 +316,10 @@ def tile_moe_sub_silu_kernel(
                 scales=da_sc[:, cols],
                 in_=rounded[g][:, blocks[0] * P : blocks[0] * P + width, :].rearrange("p t d -> p (t d)"),
             )
-            res = keep.tile([P, K // P, width], F32, name="res%d%d" % (g, blocks[0]))
-            acc = bank(b)
+            accs = [bank(b) for b in banks]
             for m in range(K // P):
                 nc.tensor.matmul_mx(
-                    out=acc[:, m * width : (m + 1) * width],
+                    out=accs[m % len(banks)][:, m * width : (m + 1) * width],
                     lhsT=w1_w[:, m * P : (m + 1) * P].bitcast(E4M3),
                     lhsT_scale=w1_sc[:, m * P : (m + 1) * P],
                     rhs=da_w[:, cols].bitcast(E5M2),
@@ -328,7 +327,12 @@ def tile_moe_sub_silu_kernel(
                     start=True,
                     stop=True,
                 )
-            nc.scalar.copy(out=res[:].rearrange("p m t -> p (m t)"), in_=acc[:, 0 : K // P * width])
+            return accs, cols, width
+
+        def store(projected, move, name):
+            accs, cols, width = projected
+            res = keep.tile([P, K // P, width], F32, name=name, align_bytes=64)
+            move(out=res[:].rearrange("p m t -> p (m t)"), in_=accs[0][:, 0 : K // P * width])
             nc.sync.dma_start(out=out_by_tile[:, :, cols], in_=res[:])
 
         both = list(range(PAIR))
@@ -345,9 +349,12 @@ def tile_moe_sub_silu_kernel(
                 for blocks in [[c] for c in both] if (g, r) == (last, LISTS - 1) else [both]:
                     for j in range(TILES):
                         fetch_sloped(g, r, j, blocks)
-                        if (r, j, blocks[0]) == (LISTS - 1, 1, 0):
-                            project(g - 1, both, FIRST_BANKS[g - 1][1])
+                        if (g, r, j) == (1, LISTS - 1, 1):
+                            store(project(0, both, [FIRST_BANKS[0][1]]), nc.scalar.copy, "res0")
         finish_gated()
-        project(last, [0], SECOND_BANKS[0])
-        project(SLOPE_GROUPS, both, GATED_BANKS[0])
-        project(last, [1], GATED_BANKS[1])
+        store(project(1, both, [FIRST_BANKS[1][1]]), nc.scalar.copy, "res1")
+        store(project(last, [0], [SECOND_BANKS[0]]), nc.scalar.copy, "res2")
+        gated = project(SLOPE_GROUPS, both, GATED_BANKS[0:1])
+        closing = project(last, [1], [SECOND_BANKS[1]])
+        store(closing, nc.scalar.copy, "res_closing")
+        store(gated, nc.vector.tensor_copy, "da_bf%d" % last)

@@ -29,7 +29,7 @@ TILES = H // P
 SLOTS = E * C
 QUARTER = T // 4
 PAIR = QUARTER // P
-MOVED_PARTITIONS = 112
+MOVED_PARTITIONS = 32 * (QUADRANTS - 1) + SCALE_ROWS
 SLOPE_GROUPS = 3
 SLOPE_FIRST = SLOPE_GROUPS * QUARTER
 GATE_ROWS = SLOPE_FIRST // P

from contextlib import ExitStack

import concourse.mybir as mybir
from concourse.masks import make_identity

K, T, E, C, H, N = 256, 1024, 4, 512, 512, 1024
FLOPS = 2 * E * C * N * H + 2 * T * H * K

F32 = mybir.dt.float32
BF16 = mybir.dt.bfloat16
I32 = mybir.dt.int32
U32 = mybir.dt.uint32
U16 = mybir.dt.uint16
U8 = mybir.dt.uint8
E4M3 = mybir.dt.float8_e4m3fn_x4
E5M2 = mybir.dt.float8_e5m2_x4
ACT = mybir.ActivationFunctionType
ALU = mybir.AluOpType

P = 128
PACK = 4
QUADRANTS = 4
SCALE_ROWS = 4
BANK = 512
LISTS = 2
PER_COLUMN = 16
PASSES = N // (P * PACK)
TILES = H // P
SLOTS = E * C
QUARTER = T // 4
PAIR = QUARTER // P
MOVED_PARTITIONS = 32 * (QUADRANTS - 1) + SCALE_ROWS
SLOPE_GROUPS = 3
SLOPE_FIRST = SLOPE_GROUPS * QUARTER
GATE_ROWS = SLOPE_FIRST // P
RING = 8
WIDE = H // 2
W2_PIECE = PASSES * WIDE
FIRST_BANKS = ((2, 3), (6, 7), (2, 3))
SECOND_BANKS = (4, 5)
GATED_BANKS = (0, 1)
SIDE_BANK = 6


def tile_moe_sub_silu_kernel(
    tc, dy_words, dy_scales, w2t_words, w2t_scales, w1t, a, gate, offs, pos1, pos2, out
):
    nc = tc.nc
    with ExitStack() as ctx:
        keep = ctx.enter_context(tc.tile_pool(name="keep", bufs=1))
        shared = ctx.enter_context(tc.tile_pool(name="shared", bufs=1))
        psum = ctx.enter_context(tc.psum_pool(name="psum", bufs=1))

        def bank(b):
            return psum.tile([P, BANK], F32, name="bank%d" % b)

        main_words = (2 * E - 1) * W2_PIECE
        offs_sb = keep.tile([P, SLOTS // PER_COLUMN], U16, name="offs_sb")
        pos_sb = [keep.tile([P, T // PER_COLUMN], U16, name="pos_sb%d" % r) for r in range(LISTS)]
        dy_sc = shared.tile([P, T], U8, name="dy_sc", align_bytes=64, offset=main_words * PACK - T // 2)
        slot_sc = [[keep.tile([P, 2 * C], U8, name="slot_sc%d%d" % (g, s), align_bytes=64) for s in range(PASSES)] for g in range(2)]
        dy_w = keep.tile([P, PASSES * T], I32, name="dy_w", align_bytes=64)
        w2_sc = keep.tile([P, E * PASSES, H], U8, name="w2_sc", align_bytes=64)
        w2_first = keep.tile([P, W2_PIECE], I32, name="w2_first", align_bytes=64)
        y = [keep.tile([P, SLOTS], F32, name="y%d" % j) for j in range(TILES)]
        a_sb = [keep.tile([P, SLOPE_FIRST], F32, name="a%d" % j) for j in range(TILES)]
        gate_rows = keep.tile([P, P], F32, name="gate_rows")
        gate_col = keep.tile([P, LISTS * GATE_ROWS], F32, name="gate_col")
        ident = keep.tile([P, P], F32, name="ident")
        w1_w = keep.tile([P, K], U32, name="w1_w", align_bytes=64)
        w1_sc = keep.tile([P, K], U8, name="w1_sc", align_bytes=64)
        da_w = keep.tile([P, T], U32, name="da_w", align_bytes=64)
        da_sc = keep.tile([P, T], U8, name="da_sc", align_bytes=64)

        nc.gpsimd.memset(dy_sc[:].bitcast(I32), 0)
        nc.gpsimd.memset(gate_rows[:], 0.0)
        make_identity(nc, ident[:])

        def load_scale_rows(tile, rows_a_quadrant, source):
            for q in range(QUADRANTS):
                nc.sync.dma_start(
                    out=tile[32 * q : 32 * q + rows_a_quadrant].bitcast(I32),
                    in_=source(SCALE_ROWS * q, SCALE_ROWS * (q + 1)).bitcast(I32),
                )

        w2_rows = w2t_scales.rearrange("e s b i -> b (e s) i")
        w2_by_pass = w2t_words.rearrange("e s p i d -> p (e s) (i d)").bitcast(I32)

        def load_a(j):
            nc.sync.dma_start(out=a_sb[j][:], in_=a[j * P : (j + 1) * P, 0:SLOPE_FIRST])

        def load_weights(words, e0, e1, h):
            nc.sync.dma_start(
                out=words.rearrange("p (g i) -> p g i", i=WIDE),
                in_=w2_by_pass[:, e0 * PASSES : e1 * PASSES, h * WIDE : (h + 1) * WIDE],
            )

        nc.sync.dma_start(offs_sb[:], offs)
        load_scale_rows(dy_sc, PASSES * SCALE_ROWS, lambda b0, b1: dy_scales[:, b0:b1, :])
        load_a(0)
        load_a(1)
        nc.sync.dma_start(
            out=dy_w[:].rearrange("p (s t) -> p s t", s=PASSES), in_=dy_words.rearrange("s p t d -> p s (t d)").bitcast(I32)
        )
        load_a(2)
        load_a(3)
        load_weights(w2_first[:], 0, 1, 0)
        nc.sync.dma_start(
            out=gate_rows[0 : LISTS * GATE_ROWS, :], in_=gate[:, 0, 0:SLOPE_FIRST].rearrange("r (c t) -> r c t", t=P)
        )
        load_scale_rows(w2_sc, SCALE_ROWS, lambda b0, b1: w2_rows[b0:b1, :, :])

        def expert_offs(e):
            return offs_sb[:, e * C // PER_COLUMN : (e + 1) * C // PER_COLUMN]

        for g in range(2):
            for u in range(2):
                nc.vector.tensor_copy(slot_sc[g][0][:, u * C : (u + 1) * C], dy_sc[:].indirect(expert_offs(2 * g + u)))

        def move_second_pass(g):
            nc.sync.dma_start(
                out=slot_sc[g][1][0:MOVED_PARTITIONS, :].bitcast(I32),
                in_=slot_sc[g][0][SCALE_ROWS : SCALE_ROWS + MOVED_PARTITIONS, :].bitcast(I32),
            )

        w2_main = shared.tile([P, main_words], I32, name="w2_main", align_bytes=64, offset=0)
        late = shared.tile([P, PACK * K + LISTS * QUARTER + T], F32, name="late", align_bytes=64, offset=main_words * PACK)
        w1_raw = late[:, 0 : PACK * K].rearrange("p (d k) -> p d k", d=PACK)
        gate_wide = late[:, PACK * K : PACK * K + LISTS * QUARTER].rearrange("p (r t) -> p r t", r=LISTS)
        a_last = late[:, PACK * K + LISTS * QUARTER :].rearrange("p (d t) -> p d t", d=PACK)

        def load_main(e0, e1, h):
            load_weights(w2_main[:, (E * h + e0 - 1) * W2_PIECE : (E * h + e1 - 1) * W2_PIECE], e0, e1, h)

        move_second_pass(0)
        load_main(1, 2, 0)
        move_second_pass(1)
        load_main(2, E, 0)
        nc.sync.dma_start(out=w1_raw, in_=w1t.rearrange("(p d) k -> p d k", d=PACK))
        nc.sync.dma_start(pos_sb[0][:], pos1)
        nc.sync.dma_start(pos_sb[1][:], pos2)
        nc.sync.dma_start(out=gate_wide, in_=gate.rearrange("r p t -> p r t")[:, :, SLOPE_FIRST:T])
        load_main(0, 2, 1)
        load_main(2, E, 1)
        nc.sync.dma_start(out=a_last, in_=a.rearrange("(p d) t -> p d t", d=PACK)[:, :, SLOPE_FIRST:T])

        def weights(e, s, j):
            if e == 0 and j < 2:
                return w2_first[:, s * WIDE + j * P : s * WIDE + (j + 1) * P]
            first = ((E * (j // 2) + e - 1) * PASSES + s) * WIDE + j % 2 * P
            return w2_main[:, first : first + P]

        slope = [keep.tile([P, SLOPE_FIRST], F32, name="slope%d" % j) for j in range(TILES)]
        left = [keep.tile([P, SLOPE_FIRST], F32, name="left%d" % j) for j in range(TILES)]
        for j in range(TILES):
            nc.scalar.activation(out=slope[j][:], in_=a_sb[j][:], func=ACT.Silu, scale=-1.0)
            nc.scalar.activation(out=left[j][:], in_=a_sb[j][:], func=ACT.Tanh, scale=0.5)
            nc.scalar.activation(out=left[j][:], in_=left[j][:], func=ACT.Identity, bias=1.0)
            nc.gpsimd.tensor_scalar(out=slope[j][:], in0=slope[j][:], scalar1=-0.5, scalar2=0.5, op0=ALU.mult, op1=ALU.add)
            nc.gpsimd.tensor_tensor(slope[j][:], left[j][:], slope[j][:], ALU.mult)

        slot_w = {}
        for e in range(E):
            for s in range(PASSES):
                slot_w[e, s] = keep.tile([P, C], U32, name="slot_w%d%d" % (e, s), align_bytes=64)
                pieces = 2 if (e, s) == (E - 1, PASSES - 1) else 1
                for u in range(pieces):
                    first, width = e * C + u * C // pieces, C // pieces
                    nc.vector.tensor_copy(
                        slot_w[e, s][:, first - e * C : first - e * C + width],
                        dy_w[:, s * T : (s + 1) * T].bitcast(U32).indirect(offs_sb[:, first // PER_COLUMN : (first + width) // PER_COLUMN]),
                    )

        def product(e, j, u0, width, b):
            acc = bank(b)
            for s in range(PASSES):
                nc.tensor.matmul_mx(
                    out=acc[:, 0:width],
                    lhsT=weights(e, s, j).bitcast(E4M3),
                    lhsT_scale=w2_sc[:, e * PASSES + s, j * P : (j + 1) * P],
                    rhs=slot_w[e, s][:, u0 : u0 + width].bitcast(E5M2),
                    rhs_scale=slot_sc[e // 2][s][:, e % 2 * C + u0 : e % 2 * C + u0 + width],
                    start=(s == 0),
                    stop=(s == PASSES - 1),
                )
            nc.scalar.copy(out=y[j][:, e * C + u0 : e * C + u0 + width], in_=acc[:, 0:width])

        gate_t = bank(E - 1)
        nc.tensor.transpose(gate_t[:, 0:P], gate_rows[:], ident[:])
        nc.scalar.copy(out=gate_col[:], in_=gate_t[:, 0 : LISTS * GATE_ROWS])
        for e in range(E):
            if e == E - 1:
                w1_bf = keep.tile([P, K, PACK], BF16, name="w1_bf", align_bytes=64)
                nc.vector.tensor_copy(
                    out=w1_bf[:].rearrange("p (c i) d -> p c d i", i=4), in_=w1_raw.rearrange("p d (c i) -> p c d i", i=4)
                )
                product(e, 0, 0, C // 2, e)
                product(e, 0, C // 2, C // 2, 0)
            else:
                product(e, 0, 0, C, e)
            product(e, 1, 0, C, E + e)
        nc.vector.quantize_mx(out=w1_w[:].bitcast(E4M3), scales=w1_sc[:], in_=w1_bf[:].rearrange("p k d -> p (k d)"))
        for j in range(2, TILES):
            for e in range(E):
                product(e, j, 0, C, E * (j % 2) + e)

        turned = {}
        sums = {}
        regrouped = {}
        rounded = [keep.tile([P, QUARTER, PACK], BF16, name="da_bf%d" % g, align_bytes=64) for g in range(SLOPE_GROUPS + 1)]
        fetched = []

        def gather(t0, width, r, j, factor):
            values = keep.tile([P, width], F32, name="picked%d" % (len(fetched) % RING))
            fetched.append(values)
            entries = pos_sb[r][:, t0 // PER_COLUMN : (t0 + width) // PER_COLUMN]
            nc.vector.tensor_tensor(values[:], y[j][:].indirect(entries), factor, ALU.mult)
            return values

        def regroup(key, source, j0, j1, scale):
            if j0 == 0:
                regrouped.update({key: keep.tile([P, PACK, P], F32, name="regrouped%d%d%d" % (key[0] % 2, key[1], key[2]))})
            nc.scalar.activation(
                out=regrouped[key][:, :, 32 * j0 : 32 * j1],
                in_=source.rearrange("t (p d) -> t d p", d=PACK),
                func=ACT.Copy,
                scale=scale,
            )

        def turn_back(g, r, c, b, lists):
            if r == 0:
                sums.update({(g, c): bank(b)})
            for d in range(PACK):
                nc.tensor.matmul(
                    sums[g, c][:, d * P : (d + 1) * P], regrouped[g, r, c][:, d, :], ident[:],
                    start=(r == 0 and d == 0), stop=(r == lists - 1 and d == PACK - 1), is_transpose=True,
                )

        def fetch_sloped(g, r, j, blocks):
            t0, width = g * QUARTER + blocks[0] * P, len(blocks) * P
            values = gather(t0, width, r, j, slope[j][:, t0 : t0 + width])
            split = (g, r, blocks[0]) == (SLOPE_GROUPS - 1, LISTS - 1, PAIR - 1)
            alone = split and j == TILES - 1
            if alone:
                turned.update({"side": bank(SIDE_BANK)})
            for u, c in enumerate(blocks):
                if j == 0:
                    turned.update({(r, c): bank((FIRST_BANKS[g], SECOND_BANKS)[r][c])})
                target = turned["side"][:, 0:P] if alone else turned[r, c][:, j * P : (j + 1) * P]
                nc.tensor.transpose(target, values[:, u * P : (u + 1) * P], ident[:])
            for c in blocks:
                col = GATE_ROWS * r + PAIR * g + c
                weight = gate_col[:, col : col + 1]
                if alone:
                    regroup((g, r, c), turned["side"][:, 0:P], j, TILES, weight)
                elif j == (TILES - 2 if split else TILES - 1):
                    regroup((g, r, c), turned[r, c][:, 0 : (j + 1) * P], 0, j + 1, weight)
                if j == TILES - 1:
                    turn_back(g, r, c, FIRST_BANKS[g][c], LISTS)
            if j == TILES - 1 and r == LISTS - 1:
                for c in blocks:
                    nc.scalar.copy(
                        out=rounded[g][:, c * P : (c + 1) * P, :], in_=sums[g, c][:].rearrange("p (d t) -> p t d", d=PACK)
                    )

        def fetch_gated(r, j):
            g = SLOPE_GROUPS
            values = gather(SLOPE_FIRST, QUARTER, r, j, gate_wide[:, r, :])
            for c in range(PAIR):
                if r == 0 and j == 0:
                    turned.update({("gated", c): bank(GATED_BANKS[c])})
                nc.tensor.matmul(
                    turned["gated", c][:, j * P : (j + 1) * P], values[:, c * P : (c + 1) * P], ident[:],
                    start=(r == 0 and j == 0), stop=(r == LISTS - 1 and j == TILES - 1), is_transpose=True,
                )
            if r == LISTS - 1 and j == TILES - 1:
                for c in range(PAIR):
                    regroup((g, 0, c), turned["gated", c][:], 0, TILES, -0.5)
                    turn_back(g, 0, c, GATED_BANKS[c], 1)

        silu_last = keep.tile([P, QUARTER * PACK], F32, name="slot_w31", align_bytes=64)
        tanh_last = keep.tile([P, QUARTER * PACK], F32, name="slot_sc11", align_bytes=64)

        def activate_last():
            src, pattern = a_last.rearrange("p d (c i) -> p c d i", i=4), "p (c i d) -> p c d i"
            nc.scalar.activation(out=silu_last[:].rearrange(pattern, i=4, d=PACK), in_=src, func=ACT.Silu, scale=-1.0)
            nc.scalar.activation(out=tanh_last[:].rearrange(pattern, i=4, d=PACK), in_=src, func=ACT.Tanh, scale=0.5)

        def finish_gated():
            g = SLOPE_GROUPS
            part = keep.tile([P, QUARTER * PACK], F32, name="picked%d" % ((len(fetched) - 2) % RING))
            for c in range(PAIR):
                cols = slice(c * BANK, (c + 1) * BANK)
                nc.vector.scalar_tensor_tensor(
                    out=part[:, cols].rearrange("p (t d) -> p t d", d=PACK),
                    in0=silu_last[:, cols].rearrange("p (t d) -> p t d", d=PACK),
                    scalar=-1.0,
                    in1=sums[g, c][:].rearrange("p (d t) -> p t d", d=PACK),
                    op0=ALU.add,
                    op1=ALU.mult,
                )
            for c in range(PAIR):
                cols = slice(c * BANK, (c + 1) * BANK)
                nc.vector.scalar_tensor_tensor(
                    out=rounded[g][:].rearrange("p t d -> p (t d)")[:, cols], in0=tanh_last[:, cols], scalar=1.0, in1=part[:, cols],
                    op0=ALU.add, op1=ALU.mult,
                )

        out_by_tile = out.rearrange("(m p) t -> p m t", p=P)

        def project(g, blocks, banks):
            width = len(blocks) * P
            cols = slice(g * QUARTER + blocks[0] * P, g * QUARTER + blocks[0] * P + width)
            nc.vector.quantize_mx(
                out=da_w[:, cols].bitcast(E5M2),
                scales=da_sc[:, cols],
                in_=rounded[g][:, blocks[0] * P : blocks[0] * P + width, :].rearrange("p t d -> p (t d)"),
            )
            accs = [bank(b) for b in banks]
            for m in range(K // P):
                nc.tensor.matmul_mx(
                    out=accs[m % len(banks)][:, m * width : (m + 1) * width],
                    lhsT=w1_w[:, m * P : (m + 1) * P].bitcast(E4M3),
                    lhsT_scale=w1_sc[:, m * P : (m + 1) * P],
                    rhs=da_w[:, cols].bitcast(E5M2),
                    rhs_scale=da_sc[:, cols],
                    start=True,
                    stop=True,
                )
            return accs, cols, width

        def store(projected, move, name):
            accs, cols, width = projected
            res = keep.tile([P, K // P, width], F32, name=name, align_bytes=64)
            move(out=res[:].rearrange("p m t -> p (m t)"), in_=accs[0][:, 0 : K // P * width])
            nc.sync.dma_start(out=out_by_tile[:, :, cols], in_=res[:])

        both = list(range(PAIR))
        last = SLOPE_GROUPS - 1
        for j in range(TILES):
            for r in range(LISTS):
                fetch_sloped(0, r, j, both)
            for r in range(LISTS):
                fetch_gated(r, j)
            if j == TILES - 2:
                activate_last()
        for g in range(1, SLOPE_GROUPS):
            for r in range(LISTS):
                for blocks in [[c] for c in both] if (g, r) == (last, LISTS - 1) else [both]:
                    for j in range(TILES):
                        fetch_sloped(g, r, j, blocks)
                        if (g, r, j) == (1, LISTS - 1, 1):
                            store(project(0, both, [FIRST_BANKS[0][1]]), nc.scalar.copy, "res0")
        finish_gated()
        store(project(1, both, [FIRST_BANKS[1][1]]), nc.scalar.copy, "res1")
        store(project(last, [0], [SECOND_BANKS[0]]), nc.scalar.copy, "res2")
        gated = project(SLOPE_GROUPS, both, GATED_BANKS[0:1])
        closing = project(last, [1], [SECOND_BANKS[1]])
        store(closing, nc.scalar.copy, "res_closing")
        store(gated, nc.vector.tensor_copy, "da_bf%d" % last)
